import numpy as np
import ml_dtypes


def mxq(x, axis, fmt="e4m3"):
    dtype, down = {"e4m3": (ml_dtypes.float8_e4m3fn, 7), "e5m2": (ml_dtypes.float8_e5m2, 14)}[fmt]
    v = np.moveaxis(np.asarray(x, np.float32).astype(ml_dtypes.bfloat16).astype(np.float64), axis, -1)
    blocks = v.reshape(v.shape[:-1] + (-1, 32))
    amax = np.abs(blocks).max(-1, keepdims=True)
    byte = np.maximum(np.where(amax > 0, np.frexp(amax)[1] - 1 + 127, 0) - down, 1)
    scale = np.exp2(byte - 127.0)
    codes = (blocks / scale).astype(np.float32).astype(dtype).astype(np.float64)
    return np.moveaxis((codes * scale).reshape(v.shape), -1, axis)


WIDE = False


def mx_kscale(k):
    if not WIDE:
        return np.ones(k)
    levels = np.array([10, -10, 5, -5, 0])
    if k % 512:
        return np.exp2(np.random.permutation(np.resize(levels, k // 32))).repeat(32)
    a = np.empty((k // 512, 16))
    for p in range(k // 512):
        a[p, :8] = np.random.permutation(np.resize(levels, 8))
        for g in range(8):
            far = levels[np.abs(levels - a[p, g]) >= 10]
            a[p, g + 8] = far[np.random.randint(len(far))]
    return np.exp2(a.ravel()).repeat(32)


BF16 = ml_dtypes.bfloat16


def bf(x):
    return np.asarray(x, np.float32).astype(BF16)


def f64(x):
    return np.asarray(x).astype(np.float64)


E2M1 = np.array([0.0, 0.5, 1.0, 1.5, 2.0, 3.0, 4.0, 6.0, -0.0, -0.5, -1.0, -1.5, -2.0, -3.0, -4.0, -6.0])


def pack_weight(w, fmt):
    k, n = w.shape
    w = f64(bf(w)).reshape(k // 32, 32, n)
    amax = np.abs(w).max(1)
    if fmt == "e4m3":
        byte = np.frexp(amax)[1] - 1 + 127 - 7
    else:
        mant, ex = np.frexp(amax / 6.0)
        byte = np.where(mant > 0.5, ex, ex - 1) + 127
    byte = np.clip(np.where(amax > 0, byte, 1), 1, 254)
    scaled = (w * np.exp2(127.0 - byte)[:, None, :]).reshape(k, n).astype(np.float32)
    by_word = np.ascontiguousarray(scaled.reshape(k // 512, 128, 4, n).transpose(0, 1, 3, 2))
    if fmt == "e4m3":
        words = by_word.astype(ml_dtypes.float8_e4m3fn).view(np.uint8)
    else:
        c = by_word.astype(ml_dtypes.float4_e2m1fn).view(np.uint8) & 0xF
        words = c[..., 0::2] | (c[..., 1::2] << 4)
    return np.ascontiguousarray(words), np.ascontiguousarray(byte.astype(np.uint8).reshape(k // 512, 16, n))


def unpack_weight(words, scales, fmt):
    g, p, n, _ = words.shape
    if fmt == "e4m3":
        vals = np.ascontiguousarray(words).view(ml_dtypes.float8_e4m3fn).astype(np.float64)
    else:
        nib = np.empty((g, p, n, 4), np.uint8)
        nib[..., 0::2] = words & 0xF
        nib[..., 1::2] = words >> 4
        vals = E2M1[nib]
    vals = vals * np.repeat(np.exp2(scales.astype(np.float64) - 127.0), 8, axis=1)[..., None]
    return vals.transpose(0, 1, 3, 2).reshape(g * 512, n)
def pack4(w):
    words, scales = pack_weight(w, "e2m1")
    return words.reshape(words.shape[0], 128, -1), scales


def unpack4(words, scales):
    return unpack_weight(words.reshape(words.shape[0], 128, -1, 2), scales, "e2m1")


def planes(Y):
    n, m = Y.shape
    b = f64(bf(Y)).reshape(n // 32, 32, m)
    amax = np.abs(b).max(1)
    byte = np.clip(np.where(amax > 0, np.frexp(amax)[1] - 1 + 127 - 7, 1), 1, 254)
    codes = (b * np.exp2(127.0 - byte)[:, None, :]).reshape(n, m).astype(np.float32).astype(ml_dtypes.float8_e4m3fn).view(np.uint8)
    words = codes.reshape(n // 512, 128, 4, m).transpose(0, 1, 3, 2)
    return np.ascontiguousarray(words), np.ascontiguousarray(byte.astype(np.uint8).reshape(n // 512, 16, m))


B, I, J, P, Q = 4, 512, 512, 512, 512


def silu(v):
    return v / (1.0 + np.exp(-v))


def two_sided(xq, a, b):
    t = xq @ b
    return a @ mxq(t, 1, "e4m3")


def setup_inputs():
    s, u = mx_kscale(J), mx_kscale(I)
    x = np.random.standard_normal((B, I, J)) * s[None, None, :] * u[None, :, None]
    b1 = np.random.standard_normal((J, Q)) / np.sqrt(J) / s[:, None]
    b2 = np.random.standard_normal((J, Q)) / np.sqrt(J) / s[:, None]
    a1 = np.random.standard_normal((P, I)) / np.sqrt(I) / u[None, :]
    a2 = np.random.standard_normal((P, I)) / np.sqrt(I) / u[None, :]
    c = 0.5 * np.random.standard_normal((P, Q))
    b1_words, b1_scales = pack4(b1)
    b2_words, b2_scales = pack4(b2)
    a1_words, a1_scales = pack4(a1.T)
    a2_words, a2_scales = pack4(a2.T)
    return {"x": bf(x), "b1_words": b1_words, "b1_scales": b1_scales, "b2_words": b2_words, "b2_scales": b2_scales,
            "a1_words": a1_words, "a1_scales": a1_scales, "a2_words": a2_words, "a2_scales": a2_scales, "c": bf(c)}


def core(x, b1_words, b1_scales, b2_words, b2_scales, a1_words, a1_scales, a2_words, a2_scales, c):
    xq = mxq(f64(x), 2, "e4m3")
    u1 = two_sided(xq, unpack4(a1_words, a1_scales).T, unpack4(b1_words, b1_scales))
    u2 = two_sided(xq, unpack4(a2_words, a2_scales).T, unpack4(b2_words, b2_scales))
    z = u1 + u2 + f64(c)[None, :, :]
    return silu(z)


def reference(x, b1_words, b1_scales, b2_words, b2_scales, a1_words, a1_scales, a2_words, a2_scales, c):
    R_out = core(x, b1_words, b1_scales, b2_words, b2_scales, a1_words, a1_scales, a2_words, a2_scales, c)
    words, scales = planes(np.moveaxis(R_out, 2, 0).reshape(512, -1))
    return R_out, words, scales

@@ -1,0 +1,257 @@
+from contextlib import ExitStack
+
+import concourse.mybir as mybir
+from concourse.masks import make_identity
+
+F32 = mybir.dt.float32
+BF16 = mybir.dt.bfloat16
+I32 = mybir.dt.int32
+U32 = mybir.dt.uint32
+U8 = mybir.dt.uint8
+FP8X4 = mybir.dt.float8_e4m3fn_x4
+FP4X4 = mybir.dt.float4_e2m1fn_x4
+SILU = mybir.ActivationFunctionType.Silu
+ADD = mybir.AluOpType.add
+
+B, D = 4, 512
+P = 128
+FLOPS = 2 * 2 * 2 * B * D * D * D
+
+STEPS = ["XX...XXTTTTTTTT", "TTXXTZTZTTTToZZa", "TTXXTZTZTTTToZZa", "TTXXTZTZTTTToZZa", "..ZZZ.Z.o.....a.b"]
+D_XC, D_XQ, D_TC, D_TQ, D_ZA, D_ZS, D_ZC, D_OC, D_OQ = 3, 2, 2, 3, 2, 3, 2, 3, 4
+T_ON_VECTOR = ((0, 4), (0, 4), (0, 4), (0, 5))
+
+
+def tile_ranktwokroneckersumlayer_x2_kernel(
+    tc, x, b1_words, b1_scales, b2_words, b2_scales, a1_words, a1_scales, a2_words, a2_scales, c, out_0, out_1, out_2
+):
+    nc = tc.nc
+    with ExitStack() as ctx:
+        keep = ctx.enter_context(tc.tile_pool(name="keep", bufs=1))
+        work = ctx.enter_context(tc.tile_pool(name="work", bufs=4))
+        psum = ctx.enter_context(tc.psum_pool(name="psum", bufs=2))
+        ctx.enter_context(tc.manual_schedule())
+
+        w_scales = keep.tile([P, 4, D], U8, name="w_scales", align_bytes=256)
+        nc.vector.memset(w_scales[:].rearrange("p w n -> p (w n)").bitcast(I32), 0)
+        warm = keep.tile([P, 1], F32, name="warm")
+        nc.vector.memset(warm[:], 0.0)
+        ident = keep.tile([P, P], F32, name="ident")
+        make_identity(nc, ident[:])
+        warm_out = keep.tile([P, 1], F32, name="warm_out")
+        nc.scalar.activation(warm_out[:], warm[:], SILU)
+
+        x_in = [keep.tile([P, 4, D], BF16, name=f"x_in{n}") for n in range(B)]
+
+        def load_x(n, b):
+            rows = x[n].rearrange("(m t) j -> m t j", t=4)
+            nc.sync.dma_start(out=x_in[n][:, 2 * b : 2 * b + 2, :], in_=rows[:, 2 * b : 2 * b + 2, :])
+
+        w_words = [keep.tile([P, 2 * D], U8, name=f"w_words{w}", align_bytes=256) for w in range(4)]
+        words_in = [b1_words, b2_words, a1_words, a2_words]
+        scales_in = [b1_scales, b2_scales, a1_scales, a2_scales]
+
+        def load_words(w):
+            nc.sync.dma_start(out=w_words[w][:].bitcast(I32), in_=words_in[w][0].bitcast(I32))
+
+        def load_scales(w):
+            queue = nc.scalar if w < 2 else nc.gpsimd
+            for q in range(4):
+                queue.dma_start(
+                    out=w_scales[32 * q : 32 * q + 4, w, :].bitcast(I32),
+                    in_=scales_in[w][0, 4 * q : 4 * q + 4, :].bitcast(I32),
+                )
+
+        c_sb = keep.tile([P, 4, D], BF16, name="c_sb")
+        load_x(0, 0)
+        load_x(0, 1)
+        load_scales(0)
+        load_words(0)
+        load_words(1)
+        load_scales(1)
+        load_scales(2)
+        load_scales(3)
+        load_x(1, 0)
+        load_x(1, 1)
+        load_words(2)
+        load_words(3)
+        nc.sync.dma_start(out=c_sb[:], in_=c.rearrange("(j p) q -> p j q", p=P))
+        for n in range(2, B):
+            load_x(n, 0)
+            load_x(n, 1)
+
+        x_codes = [keep.tile([P, D], U32, name=f"x_codes{n}", align_bytes=256) for n in range(B)]
+        x_scales = [keep.tile([P, D], U8, name=f"x_scales{n}", align_bytes=256) for n in range(B)]
+        t_codes = [[keep.tile([P, D], U32, name=f"t_codes{n}{s}", align_bytes=256) for s in range(2)] for n in range(B)]
+        t_scales = [[keep.tile([P, D], U8, name=f"t_scales{n}{s}", align_bytes=256) for s in range(2)] for n in range(B)]
+        o_codes = keep.tile([P, B * D], I32, name="o_codes", align_bytes=256)
+        o_scales = keep.tile([P, B * D], U8, name="o_scales", align_bytes=256)
+
+        o_bf = {}
+
+        def copy(on_vector, out, in_):
+            if on_vector:
+                nc.vector.tensor_copy(out=out, in_=in_)
+            else:
+                nc.scalar.copy(out=out, in_=in_)
+
+        steps = []
+        for n in range(B + 1):
+            count = {"X": 0, "T": 0, "Z": 0}
+            for ch in STEPS[n]:
+                k = count.get(ch, 0)
+                if ch == "X":
+                    m = 0 if (n == 0 and k < 2) else n + 1
+                    if m < B:
+                        steps.append(("X", m, k % 2))
+                elif ch == "T":
+                    steps.append(("T", n, k))
+                elif ch == "Z":
+                    steps.append(("Z", n - 1, k))
+                elif ch == "o":
+                    if n >= 2:
+                        steps.append(("O", n - 2, 1))
+                elif ch == "a":
+                    steps.append(("O", n - 1, 0))
+                elif ch == "b":
+                    steps.append(("O", n - 1, 1))
+                else:
+                    steps.append((".", 0, 0))
+                count[ch] = k + 1
+        waiting = [[] for i in range(len(steps) + 24)]
+
+        def later(i, delay, fn):
+            waiting[i + delay].append(fn)
+
+        def step_x(i, n, b):
+            bank = psum.tile([P, 2, 2, P], F32, name="bank_x", tag="tr", bufs=2)
+            for s in range(2):
+                row_words = x_in[n][:, 2 * b + s, :].bitcast(F32)
+                for u in range(2):
+                    nc.tensor.transpose(bank[:, s, u, :], row_words[:, u::2], ident[:])
+
+            def do_copy(i):
+                grouped = work.tile([P, 1024], BF16, name="x_grouped", tag="x_grouped", bufs=4, align_bytes=256)
+                copy(
+                    b == 1,
+                    grouped[:].bitcast(F32).rearrange("p (s m u) -> p s m u", s=2, u=2),
+                    bank[:].rearrange("p s u m -> p s m u"),
+                )
+
+                def quant(i):
+                    cols = slice(256 * b, 256 * b + 256)
+                    nc.vector.quantize_mx(out=x_codes[n][:, cols].bitcast(FP8X4), scales=x_scales[n][:, cols], in_=grouped[:])
+
+                later(i, D_XQ, quant)
+
+            later(i, D_XC, do_copy)
+
+        grouped_t = {}
+
+        def step_t(i, n, k):
+            s, h = k // 4, k % 4
+            bank = psum.tile([P, 4, P], F32, name="bank_t", tag="t", bufs=4)
+            for t in range(4):
+                cols = slice(P * t, P * t + P)
+                nc.tensor.matmul_mx(
+                    out=bank[:, t, :],
+                    lhsT=x_codes[n][:, cols].bitcast(FP8X4),
+                    lhsT_scale=x_scales[n][:, cols],
+                    rhs=w_words[s][:, 256 * h : 256 * h + 256].bitcast(FP4X4),
+                    rhs_scale=w_scales[:, s, P * h : P * h + P],
+                    start=True,
+                    stop=True,
+                )
+
+            def do_copy(i):
+                if h == 0:
+                    grouped_t[0] = work.tile([P, 4 * D], BF16, name="t_grouped", tag="t_grouped", bufs=4, align_bytes=256)
+                grouped = grouped_t[0]
+                part = slice(512 * h, 512 * h + 512)
+                copy(k in T_ON_VECTOR[n], grouped[:, part].rearrange("p (q t) -> p q t", t=4), bank[:].rearrange("p t q -> p q t"))
+
+                def quant(i):
+                    nc.vector.quantize_mx(out=t_codes[n][s][:].bitcast(FP8X4), scales=t_scales[n][s][:], in_=grouped[:])
+
+                if h == 3:
+                    later(i, D_TQ, quant)
+
+            later(i, D_TC, do_copy)
+
+        def step_z(i, n, j):
+            bank = psum.tile([P, D], F32, name="bank_z", tag="z", bufs=2)
+            for s in range(2):
+                nc.tensor.matmul_mx(
+                    out=bank[:],
+                    lhsT=w_words[2 + s][:, 256 * j : 256 * j + 256].bitcast(FP4X4),
+                    lhsT_scale=w_scales[:, 2 + s, P * j : P * j + P],
+                    rhs=t_codes[n][s][:].bitcast(FP8X4),
+                    rhs_scale=t_scales[n][s][:],
+                    start=(s == 0),
+                    stop=(s == 1),
+                )
+
+            def do_add(i):
+                v = work.tile([P, D], F32, name="v", tag="v", bufs=4)
+                nc.vector.tensor_tensor(out=v[:], in0=bank[:], in1=c_sb[:, j, :], op=ADD)
+
+                def do_silu(i):
+                    o = work.tile([P, D], F32, name="o", tag="o", bufs=6)
+                    nc.scalar.activation(o[:], v[:], SILU)
+                    nc.sync.dma_start(out=out_0[n, P * j : P * j + P, :], in_=o[:])
+
+                    def do_cast(i):
+                        ob = work.tile([P, D], BF16, name="ob", tag="ob", bufs=6)
+                        nc.vector.tensor_copy(
+                            out=ob[:].rearrange("p (u k e) -> p u k e", u=2, e=2),
+                            in_=o[:].rearrange("p (k u e) -> p u k e", u=2, e=2),
+                        )
+                        o_bf[(n, j)] = ob
+
+                    later(i, D_ZC, do_cast)
+
+                later(i, D_ZS, do_silu)
+
+            later(i, D_ZA, do_add)
+
+        def step_o(i, n, b):
+            bank = psum.tile([P, 2, 2, P], F32, name="bank_o", tag="tr", bufs=2)
+            for s in range(2):
+                ob_words = o_bf[(n, 2 * b + s)][:].bitcast(F32)
+                for u in range(2):
+                    nc.tensor.transpose(bank[:, s, u, :], ob_words[:, P * u : P * u + P], ident[:])
+
+            def do_copy(i):
+                grouped = work.tile([P, 1024], BF16, name="o_grouped", tag="o_grouped", bufs=4, align_bytes=256)
+                copy(
+                    False,
+                    grouped[:].bitcast(F32).rearrange("p (s m u) -> p s m u", s=2, u=2),
+                    bank[:].rearrange("p s u m -> p s m u"),
+                )
+
+                def quant(i):
+                    c0 = D * n + 256 * b
+                    cols = slice(c0, c0 + 256)
+                    nc.vector.quantize_mx(out=o_codes[:, cols].bitcast(FP8X4), scales=o_scales[:, cols], in_=grouped[:])
+                    nc.sync.dma_start(
+                        out=out_1[0, :, cols, :].rearrange("p m t -> p (m t)").bitcast(I32), in_=o_codes[:, cols]
+                    )
+                    if b == 1 and n >= B - 2:
+                        s_cols = slice(0, 1536) if n == B - 2 else slice(1536, 2048)
+                        for q in range(4):
+                            nc.sync.dma_start(
+                                out=out_2[0, 4 * q : 4 * q + 4, s_cols].bitcast(I32),
+                                in_=o_scales[32 * q : 32 * q + 4, s_cols].bitcast(I32),
+                            )
+
+                later(i, D_OQ, quant)
+
+            later(i, D_OC, do_copy)
+
+        emit = {"X": step_x, "T": step_t, "Z": step_z, "O": step_o}
+        for i in range(len(waiting)):
+            for fn in waiting[i]:
+                fn(i)
+            if i < len(steps) and steps[i][0] != ".":
+                kind, n, k = steps[i]
+                emit[kind](i, n, k)

@@ -17,10 +17,33 @@ B, D = 4, 512
 P = 128
 FLOPS = 2 * 2 * 2 * B * D * D * D
 
-STEPS = ["XX...XXTTTTTTTT", "TTXXTZTZTTTToZZa", "TTXXTZTZTTTToZZa", "TTXXTZTZTTTToZZa", "..ZZZ.Z.o.....a.b"]
-D_XC, D_XQ, D_TC, D_TQ, D_ZA, D_ZS, D_ZC, D_OC, D_OQ = 3, 2, 2, 3, 2, 3, 2, 3, 4
-T_ON_VECTOR = ((0, 4), (0, 4), (0, 4), (0, 5))
+Z_LAG = 5
+X_BEAT = 1
+O_LAG = 2
+DIRECT = 1
+D_READ, D_QUANT, D_SILU, D_CAST = 2, 2, 1, 2
+V_EVERY = 2
+V_STOP = 16
+V_HALF = 1
+V_HEAD = 5
+V_PH = 0
+X_SHARE = 2
+X0_SLOTS = 1
+OPEN = 2
+X1_BEAT = 1
 
+Z_LAG = 6
+O_LAG = 3
+D_QUANT = 3
+D_SILU = 3
+D_CAST = 3
+D_READ = 2
+DIRECT = 2
+V_HALF = 0
+V_HEAD = 4
+V_PH = 1
+X_SHARE = 1
+X1_BEAT = 0
 
 def tile_ranktwokroneckersumlayer_x2_kernel(
     tc, x, b1_words, b1_scales, b2_words, b2_scales, a1_words, a1_scales, a2_words, a2_scales, c, out_0, out_1, out_2
@@ -28,66 +51,74 @@ def tile_ranktwokroneckersumlayer_x2_kernel(
     nc = tc.nc
     with ExitStack() as ctx:
         keep = ctx.enter_context(tc.tile_pool(name="keep", bufs=1))
-        work = ctx.enter_context(tc.tile_pool(name="work", bufs=4))
-        psum = ctx.enter_context(tc.psum_pool(name="psum", bufs=2))
-        ctx.enter_context(tc.manual_schedule())
+        psum = ctx.enter_context(tc.psum_pool(name="psum", bufs=8))
+        ctx.enter_context(tc.manual_schedule(engines={mybir.EngineType.PE, mybir.EngineType.SP}))
 
-        w_scales = keep.tile([P, 4, D], U8, name="w_scales", align_bytes=256)
-        nc.vector.memset(w_scales[:].rearrange("p w n -> p (w n)").bitcast(I32), 0)
-        warm = keep.tile([P, 1], F32, name="warm")
+        def sbuf(name, shape, dtype):
+            return keep.tile(shape, dtype, name=name, align_bytes=256)
+
+        w_scales = [sbuf(f"w_scales{w}", [P, D], U8) for w in range(4)]
+        for w in range(4):
+            nc.vector.memset(w_scales[w][:].bitcast(I32), 0)
+        warm = sbuf("warm", [P, 1], F32)
         nc.vector.memset(warm[:], 0.0)
-        ident = keep.tile([P, P], F32, name="ident")
+        ident = sbuf("ident", [P, P], F32)
         make_identity(nc, ident[:])
-        warm_out = keep.tile([P, 1], F32, name="warm_out")
+        warm_out = sbuf("warm_out", [P, 1], F32)
         nc.scalar.activation(warm_out[:], warm[:], SILU)
 
-        x_in = [keep.tile([P, 4, D], BF16, name=f"x_in{n}") for n in range(B)]
+        x_in = [[sbuf(f"x_in{n}{b}", [P, 2, D], BF16) for b in range(2)] for n in range(B)]
+        w_words = [sbuf(f"w_words{w}", [P, 2 * D], U8) for w in range(4)]
+        c_sb = sbuf("c_sb", [P, 4, D], BF16)
+        words_in = [b1_words, b2_words, a1_words, a2_words]
+        scales_in = [b1_scales, b2_scales, a1_scales, a2_scales]
 
         def load_x(n, b):
             rows = x[n].rearrange("(m t) j -> m t j", t=4)
-            nc.sync.dma_start(out=x_in[n][:, 2 * b : 2 * b + 2, :], in_=rows[:, 2 * b : 2 * b + 2, :])
-
-        w_words = [keep.tile([P, 2 * D], U8, name=f"w_words{w}", align_bytes=256) for w in range(4)]
-        words_in = [b1_words, b2_words, a1_words, a2_words]
-        scales_in = [b1_scales, b2_scales, a1_scales, a2_scales]
+            nc.sync.dma_start(out=x_in[n][b][:], in_=rows[:, 2 * b : 2 * b + 2, :])
 
         def load_words(w):
             nc.sync.dma_start(out=w_words[w][:].bitcast(I32), in_=words_in[w][0].bitcast(I32))
 
         def load_scales(w):
-            queue = nc.scalar if w < 2 else nc.gpsimd
             for q in range(4):
-                queue.dma_start(
-                    out=w_scales[32 * q : 32 * q + 4, w, :].bitcast(I32),
+                nc.sync.dma_start(
+                    out=w_scales[w][32 * q : 32 * q + 4, :].bitcast(I32),
                     in_=scales_in[w][0, 4 * q : 4 * q + 4, :].bitcast(I32),
                 )
 
-        c_sb = keep.tile([P, 4, D], BF16, name="c_sb")
         load_x(0, 0)
         load_x(0, 1)
         load_scales(0)
         load_words(0)
-        load_words(1)
-        load_scales(1)
-        load_scales(2)
-        load_scales(3)
         load_x(1, 0)
         load_x(1, 1)
+        load_words(1)
+        load_scales(1)
         load_words(2)
         load_words(3)
+        load_x(2, 0)
+        load_x(2, 1)
+        load_scales(2)
+        load_scales(3)
         nc.sync.dma_start(out=c_sb[:], in_=c.rearrange("(j p) q -> p j q", p=P))
-        for n in range(2, B):
-            load_x(n, 0)
-            load_x(n, 1)
+        load_x(3, 0)
+        load_x(3, 1)
 
-        x_codes = [keep.tile([P, D], U32, name=f"x_codes{n}", align_bytes=256) for n in range(B)]
-        x_scales = [keep.tile([P, D], U8, name=f"x_scales{n}", align_bytes=256) for n in range(B)]
-        t_codes = [[keep.tile([P, D], U32, name=f"t_codes{n}{s}", align_bytes=256) for s in range(2)] for n in range(B)]
-        t_scales = [[keep.tile([P, D], U8, name=f"t_scales{n}{s}", align_bytes=256) for s in range(2)] for n in range(B)]
-        o_codes = keep.tile([P, B * D], I32, name="o_codes", align_bytes=256)
-        o_scales = keep.tile([P, B * D], U8, name="o_scales", align_bytes=256)
+        x_codes = [sbuf(f"x_codes{n}", [P, D], U32) for n in range(B)]
+        x_scales = [sbuf(f"x_scales{n}", [P, D], U8) for n in range(B)]
+        t_codes = [[sbuf(f"t_codes{n}{s}", [P, D], U32) for s in range(2)] for n in range(B)]
+        t_scales = [[sbuf(f"t_scales{n}{s}", [P, D], U8) for s in range(2)] for n in range(B)]
+        o_codes = sbuf("o_codes", [P, B * D], I32)
+        o_scales = sbuf("o_scales", [P, D], U8)
+        rounded = {}
+        t_pairs = {}
+        stored = []
 
-        o_bf = {}
+        waiting = {}
+
+        def later(tick, fn):
+            waiting.setdefault(tick, []).append(fn)
 
         def copy(on_vector, out, in_):
             if on_vector:
@@ -95,163 +126,206 @@ def tile_ranktwokroneckersumlayer_x2_kernel(
             else:
                 nc.scalar.copy(out=out, in_=in_)
 
-        steps = []
-        for n in range(B + 1):
-            count = {"X": 0, "T": 0, "Z": 0}
-            for ch in STEPS[n]:
-                k = count.get(ch, 0)
-                if ch == "X":
-                    m = 0 if (n == 0 and k < 2) else n + 1
-                    if m < B:
-                        steps.append(("X", m, k % 2))
-                elif ch == "T":
-                    steps.append(("T", n, k))
-                elif ch == "Z":
-                    steps.append(("Z", n - 1, k))
-                elif ch == "o":
-                    if n >= 2:
-                        steps.append(("O", n - 2, 1))
-                elif ch == "a":
-                    steps.append(("O", n - 1, 0))
-                elif ch == "b":
-                    steps.append(("O", n - 1, 1))
-                else:
-                    steps.append((".", 0, 0))
-                count[ch] = k + 1
-        waiting = [[] for i in range(len(steps) + 24)]
+        def store_planes(n, cols):
+            wide = slice(D * n + cols.start, D * n + cols.stop)
+            nc.sync.dma_start(out=out_1[0, :, wide, :].rearrange("p m t -> p (m t)").bitcast(I32), in_=o_codes[:, wide])
+            stored.append(cols.stop - cols.start)
+            if sum(stored) == B * D:
+                rows = out_2[0].rearrange("r (n m) -> n r m", n=B)
+                for q in range(4):
+                    queue = nc.sync if q < 2 else nc.scalar
+                    queue.dma_start(
+                        out=rows[:, 4 * q : 4 * q + 4, :].bitcast(I32),
+                        in_=o_scales[32 * q : 32 * q + 16, :].bitcast(I32),
+                    )
 
-        def later(i, delay, fn):
-            waiting[i + delay].append(fn)
+        def quantise_result(n, cols, grouped):
+            wide = slice(D * n + cols.start, D * n + cols.stop)
+            nc.vector.quantize_mx(out=o_codes[:, wide].bitcast(FP8X4), scales=o_scales[4 * n :, cols], in_=grouped[:])
+            store_planes(n, cols)
 
-        def step_x(i, n, b):
-            bank = psum.tile([P, 2, 2, P], F32, name="bank_x", tag="tr", bufs=2)
-            for s in range(2):
-                row_words = x_in[n][:, 2 * b + s, :].bitcast(F32)
+        def step_x(tick, n, first, slots):
+            bank = psum.tile([P, slots, 2, P], F32, name="bank_x", tag="bank")
+            for s in range(slots):
+                row_words = x_in[n][first // 2][:, first % 2 + s, :].bitcast(F32)
                 for u in range(2):
                     nc.tensor.transpose(bank[:, s, u, :], row_words[:, u::2], ident[:])
+            grouped = sbuf(f"x_grouped{n}{first}", [P, D * slots], BF16)
+            cols = slice(P * first, P * (first + slots))
 
-            def do_copy(i):
-                grouped = work.tile([P, 1024], BF16, name="x_grouped", tag="x_grouped", bufs=4, align_bytes=256)
+            def read():
                 copy(
-                    b == 1,
-                    grouped[:].bitcast(F32).rearrange("p (s m u) -> p s m u", s=2, u=2),
+                    n < X_SHARE and first // slots % 2 == 1,
+                    grouped[:].bitcast(F32).rearrange("p (s m u) -> p s m u", s=slots, u=2),
                     bank[:].rearrange("p s u m -> p s m u"),
                 )
 
-                def quant(i):
-                    cols = slice(256 * b, 256 * b + 256)
-                    nc.vector.quantize_mx(out=x_codes[n][:, cols].bitcast(FP8X4), scales=x_scales[n][:, cols], in_=grouped[:])
+            def quantise():
+                nc.vector.quantize_mx(out=x_codes[n][:, cols].bitcast(FP8X4), scales=x_scales[n][:, cols], in_=grouped[:])
 
-                later(i, D_XQ, quant)
+            later(tick + (1 if n == 0 else D_READ), read)
+            later(tick + (2 if n == 0 else D_READ + D_QUANT), quantise)
 
-            later(i, D_XC, do_copy)
-
-        grouped_t = {}
-
-        def step_t(i, n, k):
-            s, h = k // 4, k % 4
-            bank = psum.tile([P, 4, P], F32, name="bank_t", tag="t", bufs=4)
-            for t in range(4):
+        def t_passes(bank, n, s, h, slots):
+            for t in slots:
                 cols = slice(P * t, P * t + P)
                 nc.tensor.matmul_mx(
                     out=bank[:, t, :],
                     lhsT=x_codes[n][:, cols].bitcast(FP8X4),
                     lhsT_scale=x_scales[n][:, cols],
                     rhs=w_words[s][:, 256 * h : 256 * h + 256].bitcast(FP4X4),
-                    rhs_scale=w_scales[:, s, P * h : P * h + P],
+                    rhs_scale=w_scales[s][:, P * h : P * h + P],
                     start=True,
                     stop=True,
                 )
 
-            def do_copy(i):
-                if h == 0:
-                    grouped_t[0] = work.tile([P, 4 * D], BF16, name="t_grouped", tag="t_grouped", bufs=4, align_bytes=256)
-                grouped = grouped_t[0]
-                part = slice(512 * h, 512 * h + 512)
-                copy(k in T_ON_VECTOR[n], grouped[:, part].rearrange("p (q t) -> p q t", t=4), bank[:].rearrange("p t q -> p q t"))
+        opened = []
 
-                def quant(i):
-                    nc.vector.quantize_mx(out=t_codes[n][s][:].bitcast(FP8X4), scales=t_scales[n][s][:], in_=grouped[:])
+        def step_open(tick, t):
+            for h in range(4):
+                if t == 0:
+                    opened.append(psum.tile([P, 4, P], F32, name="bank_t", tag="bank"))
+                t_passes(opened[h], 0, 0, h, [t])
 
-                if h == 3:
-                    later(i, D_TQ, quant)
+        def step_t(tick, beat, half):
+            n, s, h = beat // 4, beat % 4 // 2, 2 * (beat % 2) + half
+            if (n, s) == (0, 0):
+                bank = opened[h]
+                t_passes(bank, n, s, h, range(OPEN, 4))
+            else:
+                bank = psum.tile([P, 4, P], F32, name="bank_t", tag="bank")
+                t_passes(bank, n, s, h, range(4))
+            if half == 0:
+                t_pairs[beat] = sbuf(f"t_grouped{beat}", [P, 1024], BF16)
+            grouped = t_pairs[beat]
+            cols = slice(256 * (beat % 2), 256 * (beat % 2) + 256)
 
-            later(i, D_TC, do_copy)
+            def read():
+                copy(
+                    half == V_HALF and (beat < V_HEAD or (beat % V_EVERY == V_PH and beat < V_STOP)),
+                    grouped[:, 512 * half : 512 * half + 512].rearrange("p (q t) -> p q t", t=4),
+                    bank[:].rearrange("p t q -> p q t"),
+                )
 
-        def step_z(i, n, j):
-            bank = psum.tile([P, D], F32, name="bank_z", tag="z", bufs=2)
+            def quantise():
+                nc.vector.quantize_mx(out=t_codes[n][s][:, cols].bitcast(FP8X4), scales=t_scales[n][s][:, cols], in_=grouped[:])
+
+            later(tick + D_READ, read)
+            if half == 1:
+                later(tick + D_READ + D_QUANT, quantise)
+
+        def step_z(tick, g):
+            n, j = g // 4, g % 4
+            direct = g >= 4 * B - DIRECT
+            bank = psum.tile([P, D], F32, name="bank_z", tag="bank")
             for s in range(2):
                 nc.tensor.matmul_mx(
                     out=bank[:],
                     lhsT=w_words[2 + s][:, 256 * j : 256 * j + 256].bitcast(FP4X4),
-                    lhsT_scale=w_scales[:, 2 + s, P * j : P * j + P],
+                    lhsT_scale=w_scales[2 + s][:, P * j : P * j + P],
                     rhs=t_codes[n][s][:].bitcast(FP8X4),
                     rhs_scale=t_scales[n][s][:],
                     start=(s == 0),
                     stop=(s == 1),
                 )
+            v = sbuf(f"v{g}", [P, D], F32)
+            o = sbuf(f"o{g}", [P, D], F32)
+            ob = None if direct else sbuf(f"ob{g}", [P, D], BF16)
+            rounded[g] = v if direct else ob
 
-            def do_add(i):
-                v = work.tile([P, D], F32, name="v", tag="v", bufs=4)
-                nc.vector.tensor_tensor(out=v[:], in0=bank[:], in1=c_sb[:, j, :], op=ADD)
+            def add():
+                if direct:
+                    nc.vector.tensor_tensor(
+                        out=v[:].rearrange("p (u k e) -> p u k e", u=2, e=2),
+                        in0=bank[:].rearrange("p (k u e) -> p u k e", u=2, e=2),
+                        in1=c_sb[:, j, :].rearrange("p (k u e) -> p u k e", u=2, e=2),
+                        op=ADD,
+                    )
+                else:
+                    nc.vector.tensor_tensor(out=v[:], in0=bank[:], in1=c_sb[:, j, :], op=ADD)
 
-                def do_silu(i):
-                    o = work.tile([P, D], F32, name="o", tag="o", bufs=6)
+            def silu():
+                if direct:
+                    nc.scalar.activation(
+                        o[:].rearrange("p (k u e) -> p k u e", u=2, e=2),
+                        v[:].rearrange("p (u k e) -> p k u e", u=2, e=2),
+                        SILU,
+                    )
+                else:
                     nc.scalar.activation(o[:], v[:], SILU)
-                    nc.sync.dma_start(out=out_0[n, P * j : P * j + P, :], in_=o[:])
+                nc.sync.dma_start(out=out_0[n, P * j : P * j + P, :], in_=o[:])
 
-                    def do_cast(i):
-                        ob = work.tile([P, D], BF16, name="ob", tag="ob", bufs=6)
-                        nc.vector.tensor_copy(
-                            out=ob[:].rearrange("p (u k e) -> p u k e", u=2, e=2),
-                            in_=o[:].rearrange("p (k u e) -> p u k e", u=2, e=2),
-                        )
-                        o_bf[(n, j)] = ob
-
-                    later(i, D_ZC, do_cast)
-
-                later(i, D_ZS, do_silu)
-
-            later(i, D_ZA, do_add)
-
-        def step_o(i, n, b):
-            bank = psum.tile([P, 2, 2, P], F32, name="bank_o", tag="tr", bufs=2)
-            for s in range(2):
-                ob_words = o_bf[(n, 2 * b + s)][:].bitcast(F32)
-                for u in range(2):
-                    nc.tensor.transpose(bank[:, s, u, :], ob_words[:, P * u : P * u + P], ident[:])
-
-            def do_copy(i):
-                grouped = work.tile([P, 1024], BF16, name="o_grouped", tag="o_grouped", bufs=4, align_bytes=256)
-                copy(
-                    False,
-                    grouped[:].bitcast(F32).rearrange("p (s m u) -> p s m u", s=2, u=2),
-                    bank[:].rearrange("p s u m -> p s m u"),
+            def cast():
+                nc.vector.tensor_copy(
+                    out=ob[:].rearrange("p (u k e) -> p u k e", u=2, e=2),
+                    in_=o[:].rearrange("p (k u e) -> p u k e", u=2, e=2),
                 )
 
-                def quant(i):
-                    c0 = D * n + 256 * b
-                    cols = slice(c0, c0 + 256)
-                    nc.vector.quantize_mx(out=o_codes[:, cols].bitcast(FP8X4), scales=o_scales[:, cols], in_=grouped[:])
-                    nc.sync.dma_start(
-                        out=out_1[0, :, cols, :].rearrange("p m t -> p (m t)").bitcast(I32), in_=o_codes[:, cols]
-                    )
-                    if b == 1 and n >= B - 2:
-                        s_cols = slice(0, 1536) if n == B - 2 else slice(1536, 2048)
-                        for q in range(4):
-                            nc.sync.dma_start(
-                                out=out_2[0, 4 * q : 4 * q + 4, s_cols].bitcast(I32),
-                                in_=o_scales[32 * q : 32 * q + 4, s_cols].bitcast(I32),
-                            )
+            later(tick + D_READ, add)
+            later(tick + D_READ + D_SILU, silu)
+            if not direct:
+                later(tick + D_READ + D_SILU + D_CAST, cast)
 
-                later(i, D_OQ, quant)
+        def step_o(tick, tiles):
+            n, j = tiles[0] // 4, tiles[0] % 4
+            bank = psum.tile([P, len(tiles), 2, P], F32, name="bank_o", tag="bank")
+            for s, g in enumerate(tiles):
+                words = rounded[g][:].bitcast(F32)
+                for u in range(2):
+                    nc.tensor.transpose(bank[:, s, u, :], words[:, P * u : P * u + P], ident[:])
+            grouped = sbuf(f"o_grouped{tiles[0]}", [P, D * len(tiles)], BF16)
 
-            later(i, D_OC, do_copy)
+            def read():
+                nc.scalar.copy(
+                    out=grouped[:].bitcast(F32).rearrange("p (s m u) -> p s m u", s=len(tiles), u=2),
+                    in_=bank[:].rearrange("p s u m -> p s m u"),
+                )
 
-        emit = {"X": step_x, "T": step_t, "Z": step_z, "O": step_o}
-        for i in range(len(waiting)):
-            for fn in waiting[i]:
-                fn(i)
-            if i < len(steps) and steps[i][0] != ".":
-                kind, n, k = steps[i]
-                emit[kind](i, n, k)
+            later(tick + D_READ, read)
+            later(tick + D_READ + D_QUANT, lambda: quantise_result(n, slice(P * j, P * (j + len(tiles))), grouped))
+
+        def step_direct(tick, g):
+            n, j = g // 4, g % 4
+            bank = psum.tile([P, 4, P], F32, name="bank_d", tag="bank")
+            for t in range(4):
+                nc.tensor.transpose(bank[:, t, :], rounded[g][:, 256 * (t // 2) + t % 2 : 256 * (t // 2) + 256 : 2], ident[:])
+            grouped = sbuf(f"o_grouped{g}", [P, D], BF16)
+
+            def read():
+                nc.scalar.activation(grouped[:].rearrange("p (m t) -> p m t", t=4), bank[:].rearrange("p t m -> p m t"), SILU)
+
+            later(tick + D_READ, read)
+            later(tick + D_READ + D_QUANT, lambda: quantise_result(n, slice(P * j, P * j + P), grouped))
+
+        steps = [(step_x, 0, t, X0_SLOTS) for t in range(0, 4, X0_SLOTS)]
+        steps.extend([(step_x, 1, 0, 2), None])
+        steps.extend([(step_open, t) for t in range(OPEN)])
+        tiles = 4 * B
+        turned = 0
+        for beat in range(tiles + Z_LAG + O_LAG + 1):
+            steps.append((step_t, beat, 0) if beat < tiles else None)
+            steps.append((step_z, beat - Z_LAG) if 0 <= beat - Z_LAG < tiles else None)
+            steps.append((step_t, beat, 1) if beat < tiles else None)
+            if beat == X1_BEAT:
+                steps.append((step_x, 1, 2, 2))
+            if beat % 4 == X_BEAT and 1 < beat // 4 + 1 < B:
+                steps.extend([(step_x, beat // 4 + 1, 2 * b, 2) for b in range(2)])
+            ready = min(beat - Z_LAG - O_LAG + 1, tiles - DIRECT)
+            if beat < tiles:
+                if beat % 4 == (X_BEAT + 2) % 4:
+                    while turned + 2 <= ready:
+                        steps.append((step_o, [turned, turned + 1]))
+                        turned = turned + 2
+            else:
+                while turned < ready and (turned + 2 <= ready or ready == tiles - DIRECT):
+                    width = min(2 - turned % 2, ready - turned)
+                    steps.append((step_o, list(range(turned, turned + width))))
+                    turned = turned + width
+            g = beat - Z_LAG - 1
+            if tiles - DIRECT <= g < tiles:
+                steps.append((step_direct, g))
+        for tick in range(len(steps) + 8):
+            for fn in waiting.get(tick, []):
+                fn()
+            if tick < len(steps) and steps[tick] is not None:
+                steps[tick][0](tick, *steps[tick][1:])

@@ -12,38 +12,35 @@ FP8X4 = mybir.dt.float8_e4m3fn_x4
 FP4X4 = mybir.dt.float4_e2m1fn_x4
 SILU = mybir.ActivationFunctionType.Silu
 ADD = mybir.AluOpType.add
+MULT = mybir.AluOpType.mult
 
 B, D = 4, 512
 P = 128
+TILES = 4 * B
 FLOPS = 2 * 2 * 2 * B * D * D * D
 
 Z_LAG = 5
-X_BEAT = 1
-O_LAG = 2
-DIRECT = 1
-D_READ, D_QUANT, D_SILU, D_CAST = 2, 2, 1, 2
-V_EVERY = 2
-V_STOP = 16
-V_HALF = 1
-V_HEAD = 5
-V_PH = 0
-X_SHARE = 2
-X0_SLOTS = 1
+G_LAST = 9
+V_SKIP = (3, 7, 11, 15)
+R_MAX = 2
 OPEN = 2
-X1_BEAT = 1
+X1_PH = 0
+Q_FIRST = 0
+WARM = (5, 3)
+DIRECT = 1
+O_V = 99
+O_MOD = 2
+O_PH = 1
+X_PH = 0
+G_SCALES = 0
+X_ONE = 0
+PRE = 0
+TAIL = 0
 
-Z_LAG = 6
-O_LAG = 3
-D_QUANT = 3
-D_SILU = 3
-D_CAST = 3
-D_READ = 2
-DIRECT = 2
-V_HALF = 0
-V_HEAD = 4
-V_PH = 1
-X_SHARE = 1
-X1_BEAT = 0
+G_LAST = 8
+V_SKIP = (2, 6, 15)
+Q_FIRST = -1
+DIRECT = 1
 
 def tile_ranktwokroneckersumlayer_x2_kernel(
     tc, x, b1_words, b1_scales, b2_words, b2_scales, a1_words, a1_scales, a2_words, a2_scales, c, out_0, out_1, out_2
@@ -52,73 +49,91 @@ def tile_ranktwokroneckersumlayer_x2_kernel(
     with ExitStack() as ctx:
         keep = ctx.enter_context(tc.tile_pool(name="keep", bufs=1))
         psum = ctx.enter_context(tc.psum_pool(name="psum", bufs=8))
-        ctx.enter_context(tc.manual_schedule(engines={mybir.EngineType.PE, mybir.EngineType.SP}))
+        ctx.enter_context(tc.manual_schedule())
 
         def sbuf(name, shape, dtype):
             return keep.tile(shape, dtype, name=name, align_bytes=256)
 
         w_scales = [sbuf(f"w_scales{w}", [P, D], U8) for w in range(4)]
-        for w in range(4):
-            nc.vector.memset(w_scales[w][:].bitcast(I32), 0)
+        zeros = sbuf("zeros", [P, 1024], BF16)
+        zero_codes = sbuf("zero_codes", [P, 256], U32)
+        zero_scales = sbuf("zero_scales", [P, 256], U8)
         warm = sbuf("warm", [P, 1], F32)
-        nc.vector.memset(warm[:], 0.0)
         ident = sbuf("ident", [P, P], F32)
-        make_identity(nc, ident[:])
+        if WARM[0]:
+            nc.vector.memset(zeros[:].bitcast(I32), 0)
+        nc.vector.memset(warm[:], 0.0)
+        nc.vector.memset(w_scales[0][:].bitcast(I32), 0)
+        if WARM[0]:
+            nc.vector.quantize_mx(out=zero_codes[:].bitcast(FP8X4), scales=zero_scales[:], in_=zeros[:])
+        nc.vector.memset(ident[:], 0.0)
+        make_identity(nc, ident[:], nomemset=True)
+        for w in range(1, 4):
+            nc.vector.memset(w_scales[w][:].bitcast(I32), 0)
         warm_out = sbuf("warm_out", [P, 1], F32)
         nc.scalar.activation(warm_out[:], warm[:], SILU)
 
-        x_in = [[sbuf(f"x_in{n}{b}", [P, 2, D], BF16) for b in range(2)] for n in range(B)]
+        x_in = {}
         w_words = [sbuf(f"w_words{w}", [P, 2 * D], U8) for w in range(4)]
         c_sb = sbuf("c_sb", [P, 4, D], BF16)
         words_in = [b1_words, b2_words, a1_words, a2_words]
         scales_in = [b1_scales, b2_scales, a1_scales, a2_scales]
 
-        def load_x(n, b):
-            rows = x[n].rearrange("(m t) j -> m t j", t=4)
-            nc.sync.dma_start(out=x_in[n][b][:], in_=rows[:, 2 * b : 2 * b + 2, :])
+        def load_x(n, first, slots):
+            rows = sbuf(f"x_in{n}{first}", [P, slots, D], BF16)
+            nc.sync.dma_start(out=rows[:], in_=x[n].rearrange("(m t) j -> m t j", t=4)[:, first : first + slots, :])
+            for t in range(slots):
+                x_in[n, first + t] = rows[:, t, :]
+
+        def load_matrix(n):
+            if X_ONE:
+                load_x(n, 0, 4)
+            else:
+                load_x(n, 0, 2)
+                load_x(n, 2, 2)
 
         def load_words(w):
             nc.sync.dma_start(out=w_words[w][:].bitcast(I32), in_=words_in[w][0].bitcast(I32))
 
         def load_scales(w):
+            queue = nc.gpsimd if w >= 4 - G_SCALES else nc.sync
             for q in range(4):
-                nc.sync.dma_start(
+                queue.dma_start(
                     out=w_scales[w][32 * q : 32 * q + 4, :].bitcast(I32),
                     in_=scales_in[w][0, 4 * q : 4 * q + 4, :].bitcast(I32),
                 )
 
-        load_x(0, 0)
-        load_x(0, 1)
-        load_scales(0)
+        load_x(0, 0, 2)
+        load_x(0, 2, 2)
         load_words(0)
-        load_x(1, 0)
-        load_x(1, 1)
+        load_scales(0)
         load_words(1)
+        load_x(1, 0, 2)
+        load_x(1, 2, 2)
         load_scales(1)
         load_words(2)
         load_words(3)
-        load_x(2, 0)
-        load_x(2, 1)
+        load_matrix(2)
         load_scales(2)
         load_scales(3)
         nc.sync.dma_start(out=c_sb[:], in_=c.rearrange("(j p) q -> p j q", p=P))
-        load_x(3, 0)
-        load_x(3, 1)
+        load_matrix(3)
 
         x_codes = [sbuf(f"x_codes{n}", [P, D], U32) for n in range(B)]
         x_scales = [sbuf(f"x_scales{n}", [P, D], U8) for n in range(B)]
+        x_grouped = [sbuf(f"x_grouped{n}", [P, 4 * D], BF16) for n in range(B)]
         t_codes = [[sbuf(f"t_codes{n}{s}", [P, D], U32) for s in range(2)] for n in range(B)]
         t_scales = [[sbuf(f"t_scales{n}{s}", [P, D], U8) for s in range(2)] for n in range(B)]
+        t_grouped = [sbuf(f"t_grouped{beat}", [P, 2 * D], BF16) for beat in range(TILES)]
+        v = [sbuf(f"v{n}", [P, 4 * D], F32) for n in range(B)]
+        o = [sbuf(f"o{n}", [P, 4 * D], F32) for n in range(B)]
+        rounded = [
+            t_grouped[g + Z_LAG + 1][:, 0:D] if g <= G_LAST else sbuf(f"rounded{g}", [P, D], BF16)[:] for g in range(TILES - DIRECT)
+        ]
+        o_grouped = [sbuf(f"o_grouped{n}", [P, 4 * D], BF16) for n in range(B)]
         o_codes = sbuf("o_codes", [P, B * D], I32)
         o_scales = sbuf("o_scales", [P, D], U8)
-        rounded = {}
-        t_pairs = {}
         stored = []
-
-        waiting = {}
-
-        def later(tick, fn):
-            waiting.setdefault(tick, []).append(fn)
 
         def copy(on_vector, out, in_):
             if on_vector:
@@ -126,11 +141,19 @@ def tile_ranktwokroneckersumlayer_x2_kernel(
             else:
                 nc.scalar.copy(out=out, in_=in_)
 
-        def store_planes(n, cols):
-            wide = slice(D * n + cols.start, D * n + cols.stop)
+        def quantise(codes, scales, grouped, first, count):
+            cols = slice(P * first, P * (first + count))
+            nc.vector.quantize_mx(
+                out=codes[:, cols].bitcast(FP8X4), scales=scales[:, cols], in_=grouped[:, D * first : D * (first + count)]
+            )
+
+        def quantise_result(n, first, count):
+            codes = o_codes[:, D * n : D * n + D]
+            quantise(codes, o_scales[4 * n :, :], o_grouped[n], first, count)
+            wide = slice(D * n + P * first, D * n + P * (first + count))
             nc.sync.dma_start(out=out_1[0, :, wide, :].rearrange("p m t -> p (m t)").bitcast(I32), in_=o_codes[:, wide])
-            stored.append(cols.stop - cols.start)
-            if sum(stored) == B * D:
+            stored.append(count)
+            if sum(stored) == TILES:
                 rows = out_2[0].rearrange("r (n m) -> n r m", n=B)
                 for q in range(4):
                     queue = nc.sync if q < 2 else nc.scalar
@@ -139,84 +162,51 @@ def tile_ranktwokroneckersumlayer_x2_kernel(
                         in_=o_scales[32 * q : 32 * q + 16, :].bitcast(I32),
                     )
 
-        def quantise_result(n, cols, grouped):
-            wide = slice(D * n + cols.start, D * n + cols.stop)
-            nc.vector.quantize_mx(out=o_codes[:, wide].bitcast(FP8X4), scales=o_scales[4 * n :, cols], in_=grouped[:])
-            store_planes(n, cols)
+        def read_words(on_vector, bank, grouped, first, count):
+            copy(
+                on_vector,
+                grouped[:, D * first : D * (first + count)].bitcast(F32).rearrange("p (s m u) -> p s m u", s=count, u=2),
+                bank[:].rearrange("p s u m -> p s m u"),
+            )
 
-        def step_x(tick, n, first, slots):
-            bank = psum.tile([P, slots, 2, P], F32, name="bank_x", tag="bank")
-            for s in range(slots):
-                row_words = x_in[n][first // 2][:, first % 2 + s, :].bitcast(F32)
+        def turn_x(n, first, count):
+            bank = psum.tile([P, count, 2, P], F32, name="bank_x", tag="bank")
+            for s in range(count):
+                words = x_in[n, first + s].bitcast(F32)
                 for u in range(2):
-                    nc.tensor.transpose(bank[:, s, u, :], row_words[:, u::2], ident[:])
-            grouped = sbuf(f"x_grouped{n}{first}", [P, D * slots], BF16)
-            cols = slice(P * first, P * (first + slots))
+                    nc.tensor.transpose(bank[:, s, u, :], words[:, u::2], ident[:])
+            return bank
 
-            def read():
-                copy(
-                    n < X_SHARE and first // slots % 2 == 1,
-                    grouped[:].bitcast(F32).rearrange("p (s m u) -> p s m u", s=slots, u=2),
-                    bank[:].rearrange("p s u m -> p s m u"),
-                )
+        def t_pass(bank, n, s, h, t):
+            cols = slice(P * t, P * t + P)
+            nc.tensor.matmul_mx(
+                out=bank[:, t, :],
+                lhsT=x_codes[n][:, cols].bitcast(FP8X4),
+                lhsT_scale=x_scales[n][:, cols],
+                rhs=w_words[s][:, 256 * h : 256 * h + 256].bitcast(FP4X4),
+                rhs_scale=w_scales[s][:, P * h : P * h + P],
+                start=True,
+                stop=True,
+            )
 
-            def quantise():
-                nc.vector.quantize_mx(out=x_codes[n][:, cols].bitcast(FP8X4), scales=x_scales[n][:, cols], in_=grouped[:])
+        def t_bank(beat, half):
+            bank = psum.tile([P, 4, P], F32, name="bank_t", tag="bank")
+            for t in range(4):
+                t_pass(bank, beat // 4, beat % 4 // 2, 2 * (beat % 2) + half, t)
+            return bank
 
-            later(tick + (1 if n == 0 else D_READ), read)
-            later(tick + (2 if n == 0 else D_READ + D_QUANT), quantise)
+        def read_t(on_vector, bank, beat, half):
+            out = t_grouped[beat][:, D * half : D * half + D].rearrange("p (q t) -> p q t", t=4)
+            copy(on_vector, out, bank[:].rearrange("p t q -> p q t"))
 
-        def t_passes(bank, n, s, h, slots):
-            for t in slots:
-                cols = slice(P * t, P * t + P)
-                nc.tensor.matmul_mx(
-                    out=bank[:, t, :],
-                    lhsT=x_codes[n][:, cols].bitcast(FP8X4),
-                    lhsT_scale=x_scales[n][:, cols],
-                    rhs=w_words[s][:, 256 * h : 256 * h + 256].bitcast(FP4X4),
-                    rhs_scale=w_scales[s][:, P * h : P * h + P],
-                    start=True,
-                    stop=True,
-                )
+        def quantise_t(beat):
+            n, s, cols = beat // 4, beat % 4 // 2, slice(256 * (beat % 2), 256 * (beat % 2) + 256)
+            nc.vector.quantize_mx(
+                out=t_codes[n][s][:, cols].bitcast(FP8X4), scales=t_scales[n][s][:, cols], in_=t_grouped[beat][:]
+            )
 
-        opened = []
-
-        def step_open(tick, t):
-            for h in range(4):
-                if t == 0:
-                    opened.append(psum.tile([P, 4, P], F32, name="bank_t", tag="bank"))
-                t_passes(opened[h], 0, 0, h, [t])
-
-        def step_t(tick, beat, half):
-            n, s, h = beat // 4, beat % 4 // 2, 2 * (beat % 2) + half
-            if (n, s) == (0, 0):
-                bank = opened[h]
-                t_passes(bank, n, s, h, range(OPEN, 4))
-            else:
-                bank = psum.tile([P, 4, P], F32, name="bank_t", tag="bank")
-                t_passes(bank, n, s, h, range(4))
-            if half == 0:
-                t_pairs[beat] = sbuf(f"t_grouped{beat}", [P, 1024], BF16)
-            grouped = t_pairs[beat]
-            cols = slice(256 * (beat % 2), 256 * (beat % 2) + 256)
-
-            def read():
-                copy(
-                    half == V_HALF and (beat < V_HEAD or (beat % V_EVERY == V_PH and beat < V_STOP)),
-                    grouped[:, 512 * half : 512 * half + 512].rearrange("p (q t) -> p q t", t=4),
-                    bank[:].rearrange("p t q -> p q t"),
-                )
-
-            def quantise():
-                nc.vector.quantize_mx(out=t_codes[n][s][:, cols].bitcast(FP8X4), scales=t_scales[n][s][:, cols], in_=grouped[:])
-
-            later(tick + D_READ, read)
-            if half == 1:
-                later(tick + D_READ + D_QUANT, quantise)
-
-        def step_z(tick, g):
+        def z_bank(g):
             n, j = g // 4, g % 4
-            direct = g >= 4 * B - DIRECT
             bank = psum.tile([P, D], F32, name="bank_z", tag="bank")
             for s in range(2):
                 nc.tensor.matmul_mx(
@@ -228,104 +218,137 @@ def tile_ranktwokroneckersumlayer_x2_kernel(
                     start=(s == 0),
                     stop=(s == 1),
                 )
-            v = sbuf(f"v{g}", [P, D], F32)
-            o = sbuf(f"o{g}", [P, D], F32)
-            ob = None if direct else sbuf(f"ob{g}", [P, D], BF16)
-            rounded[g] = v if direct else ob
+            return bank
 
-            def add():
-                if direct:
-                    nc.vector.tensor_tensor(
-                        out=v[:].rearrange("p (u k e) -> p u k e", u=2, e=2),
-                        in0=bank[:].rearrange("p (k u e) -> p u k e", u=2, e=2),
-                        in1=c_sb[:, j, :].rearrange("p (k u e) -> p u k e", u=2, e=2),
-                        op=ADD,
-                    )
-                else:
-                    nc.vector.tensor_tensor(out=v[:], in0=bank[:], in1=c_sb[:, j, :], op=ADD)
-
-            def silu():
-                if direct:
-                    nc.scalar.activation(
-                        o[:].rearrange("p (k u e) -> p k u e", u=2, e=2),
-                        v[:].rearrange("p (u k e) -> p k u e", u=2, e=2),
-                        SILU,
-                    )
-                else:
-                    nc.scalar.activation(o[:], v[:], SILU)
-                nc.sync.dma_start(out=out_0[n, P * j : P * j + P, :], in_=o[:])
-
-            def cast():
-                nc.vector.tensor_copy(
-                    out=ob[:].rearrange("p (u k e) -> p u k e", u=2, e=2),
-                    in_=o[:].rearrange("p (k u e) -> p u k e", u=2, e=2),
+        def add(bank, g):
+            n, j = g // 4, g % 4
+            out = v[n][:, D * j : D * j + D]
+            if g >= TILES - DIRECT:
+                nc.vector.tensor_tensor(
+                    out=out.rearrange("p (t m) -> p t m", t=4),
+                    in0=bank[:].rearrange("p (m t) -> p t m", t=4),
+                    in1=c_sb[:, j, :].rearrange("p (m t) -> p t m", t=4),
+                    op=ADD,
                 )
+            else:
+                nc.vector.tensor_tensor(out=out, in0=bank[:], in1=c_sb[:, j, :], op=ADD)
 
-            later(tick + D_READ, add)
-            later(tick + D_READ + D_SILU, silu)
-            if not direct:
-                later(tick + D_READ + D_SILU + D_CAST, cast)
+        def silu(g):
+            n, j = g // 4, g % 4
+            cols = slice(D * j, D * j + D)
+            if g >= TILES - DIRECT:
+                nc.scalar.activation(
+                    o[n][:, cols].rearrange("p (m t) -> p m t", t=4), v[n][:, cols].rearrange("p (t m) -> p m t", t=4), SILU
+                )
+            else:
+                nc.scalar.activation(o[n][:, cols], v[n][:, cols], SILU)
+            nc.sync.dma_start(out=out_0[n, P * j : P * j + P, :], in_=o[n][:, cols])
 
-        def step_o(tick, tiles):
-            n, j = tiles[0] // 4, tiles[0] % 4
-            bank = psum.tile([P, len(tiles), 2, P], F32, name="bank_o", tag="bank")
-            for s, g in enumerate(tiles):
-                words = rounded[g][:].bitcast(F32)
+        def cast(g):
+            out = rounded[g].rearrange("p (u k e) -> p u k e", u=2, e=2)
+            in_ = o[g // 4][:, D * (g % 4) : D * (g % 4) + D].rearrange("p (k u e) -> p u k e", u=2, e=2)
+            if g <= G_LAST:
+                nc.gpsimd.tensor_scalar(out=out, in0=in_, scalar1=1.0, scalar2=-0.0, op0=MULT, op1=ADD)
+            else:
+                nc.vector.tensor_copy(out=out, in_=in_)
+
+        def turn_result(g, count):
+            bank = psum.tile([P, count, 2, P], F32, name="bank_o", tag="bank")
+            for s in range(count):
+                words = rounded[g + s].bitcast(F32)
                 for u in range(2):
                     nc.tensor.transpose(bank[:, s, u, :], words[:, P * u : P * u + P], ident[:])
-            grouped = sbuf(f"o_grouped{tiles[0]}", [P, D * len(tiles)], BF16)
+            return bank
 
-            def read():
-                nc.scalar.copy(
-                    out=grouped[:].bitcast(F32).rearrange("p (s m u) -> p s m u", s=len(tiles), u=2),
-                    in_=bank[:].rearrange("p s u m -> p s m u"),
-                )
-
-            later(tick + D_READ, read)
-            later(tick + D_READ + D_QUANT, lambda: quantise_result(n, slice(P * j, P * (j + len(tiles))), grouped))
-
-        def step_direct(tick, g):
+        def turn_sum(g):
             n, j = g // 4, g % 4
             bank = psum.tile([P, 4, P], F32, name="bank_d", tag="bank")
             for t in range(4):
-                nc.tensor.transpose(bank[:, t, :], rounded[g][:, 256 * (t // 2) + t % 2 : 256 * (t // 2) + 256 : 2], ident[:])
-            grouped = sbuf(f"o_grouped{g}", [P, D], BF16)
+                nc.tensor.transpose(bank[:, t, :], v[n][:, D * j + P * t : D * j + P * (t + 1)], ident[:])
+            return bank
 
-            def read():
-                nc.scalar.activation(grouped[:].rearrange("p (m t) -> p m t", t=4), bank[:].rearrange("p t m -> p m t"), SILU)
+        def silu_turned(bank, g):
+            out = o_grouped[g // 4][:, D * (g % 4) : D * (g % 4) + D].rearrange("p (m t) -> p m t", t=4)
+            nc.scalar.activation(out, bank[:].rearrange("p t m -> p m t"), SILU)
 
-            later(tick + D_READ, read)
-            later(tick + D_READ + D_QUANT, lambda: quantise_result(n, slice(P * j, P * j + P), grouped))
+        def warm_up(count):
+            bank = psum.tile([P, 256], F32, name="bank_w", tag="bank")
+            for i in range(count):
+                nc.tensor.matmul_mx(
+                    out=bank[:],
+                    lhsT=zero_codes[:, 0:64].bitcast(FP4X4),
+                    lhsT_scale=zero_scales[:, 0:P],
+                    rhs=zero_codes[:].bitcast(FP8X4),
+                    rhs_scale=zero_scales[:],
+                    start=True,
+                    stop=True,
+                )
 
-        steps = [(step_x, 0, t, X0_SLOTS) for t in range(0, 4, X0_SLOTS)]
-        steps.extend([(step_x, 1, 0, 2), None])
-        steps.extend([(step_open, t) for t in range(OPEN)])
-        tiles = 4 * B
+        if WARM[0]:
+            warm_up(WARM[0])
+        for t in range(4):
+            read_words(t % 2 == 1, turn_x(0, t, 1), x_grouped[0], t, 1)
+            if t == 1:
+                quantise(x_codes[0], x_scales[0], x_grouped[0], 0, 1)
+        if WARM[1]:
+            warm_up(WARM[1])
+        opened = [psum.tile([P, 4, P], F32, name="bank_t", tag="bank") for h in range(4)]
+        for t in range(4):
+            if t > 0:
+                quantise(x_codes[0], x_scales[0], x_grouped[0], t, 1)
+            for h in range(4 if t < OPEN else 0):
+                t_pass(opened[h], 0, 0, h, t)
+        for h in range(4):
+            for t in range(OPEN, 4):
+                t_pass(opened[h], 0, 0, h, t)
+
+        to_read = []
+        to_quantise = []
         turned = 0
-        for beat in range(tiles + Z_LAG + O_LAG + 1):
-            steps.append((step_t, beat, 0) if beat < tiles else None)
-            steps.append((step_z, beat - Z_LAG) if 0 <= beat - Z_LAG < tiles else None)
-            steps.append((step_t, beat, 1) if beat < tiles else None)
-            if beat == X1_BEAT:
-                steps.append((step_x, 1, 2, 2))
-            if beat % 4 == X_BEAT and 1 < beat // 4 + 1 < B:
-                steps.extend([(step_x, beat // 4 + 1, 2 * b, 2) for b in range(2)])
-            ready = min(beat - Z_LAG - O_LAG + 1, tiles - DIRECT)
-            if beat < tiles:
-                if beat % 4 == (X_BEAT + 2) % 4:
-                    while turned + 2 <= ready:
-                        steps.append((step_o, [turned, turned + 1]))
-                        turned = turned + 2
-            else:
-                while turned < ready and (turned + 2 <= ready or ready == tiles - DIRECT):
-                    width = min(2 - turned % 2, ready - turned)
-                    steps.append((step_o, list(range(turned, turned + width))))
-                    turned = turned + width
-            g = beat - Z_LAG - 1
-            if tiles - DIRECT <= g < tiles:
-                steps.append((step_direct, g))
-        for tick in range(len(steps) + 8):
-            for fn in waiting.get(tick, []):
-                fn()
-            if tick < len(steps) and steps[tick] is not None:
-                steps[tick][0](tick, *steps[tick][1:])
+        last = TILES - DIRECT
+        for beat in range(TILES + Z_LAG + 6):
+            g = beat - Z_LAG
+            banks = None
+            if beat < TILES:
+                banks = opened[2 * beat : 2 * beat + 2] if beat < 2 else [t_bank(beat, 0), t_bank(beat, 1)]
+            sums = z_bank(g) if 0 <= g < TILES else None
+            if banks:
+                read_t(False, banks[0], beat, 0)
+            if 0 <= beat - 1 < TILES and g > Q_FIRST:
+                quantise_t(beat - 1)
+            for fn, args in to_quantise:
+                fn(*args)
+            to_quantise = []
+            if 0 <= g - 2 < last:
+                cast(g - 2)
+            for reader, read_args, fn, args in to_read[:R_MAX]:
+                reader(*read_args)
+                to_quantise.append((fn, args))
+            to_read = to_read[R_MAX:]
+            if banks:
+                read_t(beat not in V_SKIP, banks[1], beat, 1)
+            if 0 <= beat - 1 < TILES and g <= Q_FIRST:
+                quantise_t(beat - 1)
+            if sums is not None:
+                add(sums, g)
+            if 0 <= g - 1 < TILES:
+                silu(g - 1)
+            if beat % 4 == (X_PH if beat > 3 else X1_PH) and beat // 4 + 1 < B:
+                n = beat // 4 + 1
+                for first in (0, 2):
+                    bank = turn_x(n, first, 2)
+                    to_read.append(
+                        (read_words, (False, bank, x_grouped[n], first, 2), quantise, (x_codes[n], x_scales[n], x_grouped[n], first, 2))
+                    )
+            ready = min(g - 2 + (TAIL if beat >= TILES else 0), last)
+            if beat % O_MOD == O_PH or beat >= TILES:
+                while turned + 2 <= ready or turned < ready == last:
+                    count = min(2, ready - turned)
+                    bank = turn_result(turned, count)
+                    n, j = turned // 4, turned % 4
+                    to_read.append(
+                        (read_words, (turned >= O_V, bank, o_grouped[n], j, count), quantise_result, (n, j, count))
+                    )
+                    turned = turned + count
+            if last <= g - 1 < TILES:
+                to_read.append((silu_turned, (turn_sum(g - 1), g - 1), quantise_result, ((g - 1) // 4, (g - 1) % 4, 1)))

@@ -16,31 +16,14 @@ MULT = mybir.AluOpType.mult
 
 B, D = 4, 512
 P = 128
-TILES = 4 * B
 FLOPS = 2 * 2 * 2 * B * D * D * D
 
+BEATS = 4 * B
+BANDS = 4 * B
 Z_LAG = 5
-G_LAST = 9
-V_SKIP = (3, 7, 11, 15)
-R_MAX = 2
-OPEN = 2
-X1_PH = 0
-Q_FIRST = 0
-WARM = (5, 3)
-DIRECT = 1
-O_V = 99
-O_MOD = 2
-O_PH = 1
-X_PH = 0
-G_SCALES = 0
-X_ONE = 0
-PRE = 0
-TAIL = 0
+LAST_ON_GPSIMD = 12
+WARM_FIRST, WARM_GAP = 5, 3
 
-G_LAST = 8
-V_SKIP = (2, 6, 15)
-Q_FIRST = -1
-DIRECT = 1
 
 def tile_ranktwokroneckersumlayer_x2_kernel(
     tc, x, b1_words, b1_scales, b2_words, b2_scales, a1_words, a1_scales, a2_words, a2_scales, c, out_0, out_1, out_2
@@ -58,47 +41,37 @@ def tile_ranktwokroneckersumlayer_x2_kernel(
         zeros = sbuf("zeros", [P, 1024], BF16)
         zero_codes = sbuf("zero_codes", [P, 256], U32)
         zero_scales = sbuf("zero_scales", [P, 256], U8)
-        warm = sbuf("warm", [P, 1], F32)
+        table_in = sbuf("table_in", [P, 1], F32)
         ident = sbuf("ident", [P, P], F32)
-        if WARM[0]:
-            nc.vector.memset(zeros[:].bitcast(I32), 0)
-        nc.vector.memset(warm[:], 0.0)
+        nc.vector.memset(zeros[:].bitcast(I32), 0)
+        nc.vector.memset(table_in[:], 0.0)
         nc.vector.memset(w_scales[0][:].bitcast(I32), 0)
-        if WARM[0]:
-            nc.vector.quantize_mx(out=zero_codes[:].bitcast(FP8X4), scales=zero_scales[:], in_=zeros[:])
+        nc.vector.quantize_mx(out=zero_codes[:].bitcast(FP8X4), scales=zero_scales[:], in_=zeros[:])
         nc.vector.memset(ident[:], 0.0)
         make_identity(nc, ident[:], nomemset=True)
         for w in range(1, 4):
             nc.vector.memset(w_scales[w][:].bitcast(I32), 0)
-        warm_out = sbuf("warm_out", [P, 1], F32)
-        nc.scalar.activation(warm_out[:], warm[:], SILU)
+        table_out = sbuf("table_out", [P, 1], F32)
+        nc.scalar.activation(table_out[:], table_in[:], SILU)
 
-        x_in = {}
+        x_rows = {}
         w_words = [sbuf(f"w_words{w}", [P, 2 * D], U8) for w in range(4)]
         c_sb = sbuf("c_sb", [P, 4, D], BF16)
         words_in = [b1_words, b2_words, a1_words, a2_words]
         scales_in = [b1_scales, b2_scales, a1_scales, a2_scales]
 
-        def load_x(n, first, slots):
-            rows = sbuf(f"x_in{n}{first}", [P, slots, D], BF16)
-            nc.sync.dma_start(out=rows[:], in_=x[n].rearrange("(m t) j -> m t j", t=4)[:, first : first + slots, :])
-            for t in range(slots):
-                x_in[n, first + t] = rows[:, t, :]
-
-        def load_matrix(n):
-            if X_ONE:
-                load_x(n, 0, 4)
-            else:
-                load_x(n, 0, 2)
-                load_x(n, 2, 2)
+        def load_x(n, first, count):
+            rows = sbuf(f"x_in{n}{first}", [P, count, D], BF16)
+            nc.sync.dma_start(out=rows[:], in_=x[n].rearrange("(m t) j -> m t j", t=4)[:, first : first + count, :])
+            for t in range(count):
+                x_rows[n, first + t] = rows[:, t, :]
 
         def load_words(w):
             nc.sync.dma_start(out=w_words[w][:].bitcast(I32), in_=words_in[w][0].bitcast(I32))
 
         def load_scales(w):
-            queue = nc.gpsimd if w >= 4 - G_SCALES else nc.sync
             for q in range(4):
-                queue.dma_start(
+                nc.sync.dma_start(
                     out=w_scales[w][32 * q : 32 * q + 4, :].bitcast(I32),
                     in_=scales_in[w][0, 4 * q : 4 * q + 4, :].bitcast(I32),
                 )
@@ -107,33 +80,34 @@ def tile_ranktwokroneckersumlayer_x2_kernel(
         load_x(0, 2, 2)
         load_words(0)
         load_scales(0)
-        load_words(1)
-        load_x(1, 0, 2)
-        load_x(1, 2, 2)
+        load_x(1, 0, 4)
+        for w in range(1, 4):
+            load_words(w)
         load_scales(1)
-        load_words(2)
-        load_words(3)
-        load_matrix(2)
+        load_x(2, 0, 4)
         load_scales(2)
-        load_scales(3)
         nc.sync.dma_start(out=c_sb[:], in_=c.rearrange("(j p) q -> p j q", p=P))
-        load_matrix(3)
+        load_scales(3)
+        load_x(3, 0, 4)
 
         x_codes = [sbuf(f"x_codes{n}", [P, D], U32) for n in range(B)]
         x_scales = [sbuf(f"x_scales{n}", [P, D], U8) for n in range(B)]
         x_grouped = [sbuf(f"x_grouped{n}", [P, 4 * D], BF16) for n in range(B)]
         t_codes = [[sbuf(f"t_codes{n}{s}", [P, D], U32) for s in range(2)] for n in range(B)]
         t_scales = [[sbuf(f"t_scales{n}{s}", [P, D], U8) for s in range(2)] for n in range(B)]
-        t_grouped = [sbuf(f"t_grouped{beat}", [P, 2 * D], BF16) for beat in range(TILES)]
-        v = [sbuf(f"v{n}", [P, 4 * D], F32) for n in range(B)]
-        o = [sbuf(f"o{n}", [P, 4 * D], F32) for n in range(B)]
+        t_grouped = [sbuf(f"t_grouped{beat}", [P, 2 * D], BF16) for beat in range(BEATS)]
+        z = [sbuf(f"z{n}", [P, 4 * D], F32) for n in range(B)]
+        y = [sbuf(f"y{n}", [P, 4 * D], F32) for n in range(B)]
         rounded = [
-            t_grouped[g + Z_LAG + 1][:, 0:D] if g <= G_LAST else sbuf(f"rounded{g}", [P, D], BF16)[:] for g in range(TILES - DIRECT)
+            t_grouped[g + Z_LAG + 1][:, 0:D] if g + Z_LAG + 1 < BEATS else sbuf(f"rounded{g}", [P, D], BF16)[:]
+            for g in range(BANDS - 1)
         ]
-        o_grouped = [sbuf(f"o_grouped{n}", [P, 4 * D], BF16) for n in range(B)]
-        o_codes = sbuf("o_codes", [P, B * D], I32)
-        o_scales = sbuf("o_scales", [P, D], U8)
-        stored = []
+        y_grouped = [sbuf(f"y_grouped{n}", [P, 4 * D], BF16) for n in range(B)]
+        y_codes = sbuf("y_codes", [P, B * D], I32)
+        y_scales = sbuf("y_scales", [P, D], U8)
+
+        def band(tiles, g):
+            return tiles[g // 4][:, D * (g % 4) : D * (g % 4) + D]
 
         def copy(on_vector, out, in_):
             if on_vector:
@@ -147,20 +121,14 @@ def tile_ranktwokroneckersumlayer_x2_kernel(
                 out=codes[:, cols].bitcast(FP8X4), scales=scales[:, cols], in_=grouped[:, D * first : D * (first + count)]
             )
 
-        def quantise_result(n, first, count):
-            codes = o_codes[:, D * n : D * n + D]
-            quantise(codes, o_scales[4 * n :, :], o_grouped[n], first, count)
-            wide = slice(D * n + P * first, D * n + P * (first + count))
-            nc.sync.dma_start(out=out_1[0, :, wide, :].rearrange("p m t -> p (m t)").bitcast(I32), in_=o_codes[:, wide])
-            stored.append(count)
-            if sum(stored) == TILES:
-                rows = out_2[0].rearrange("r (n m) -> n r m", n=B)
-                for q in range(4):
-                    queue = nc.sync if q < 2 else nc.scalar
-                    queue.dma_start(
-                        out=rows[:, 4 * q : 4 * q + 4, :].bitcast(I32),
-                        in_=o_scales[32 * q : 32 * q + 16, :].bitcast(I32),
-                    )
+        def quantise_x(n, first, count):
+            quantise(x_codes[n], x_scales[n], x_grouped[n], first, count)
+
+        def quantise_y(g, count):
+            n = g // 4
+            quantise(y_codes[:, D * n : D * n + D], y_scales[4 * n :, :], y_grouped[n], g % 4, count)
+            cols = slice(P * g, P * (g + count))
+            nc.sync.dma_start(out=out_1[0, :, cols, :].rearrange("p m t -> p (m t)").bitcast(I32), in_=y_codes[:, cols])
 
         def read_words(on_vector, bank, grouped, first, count):
             copy(
@@ -169,12 +137,14 @@ def tile_ranktwokroneckersumlayer_x2_kernel(
                 bank[:].rearrange("p s u m -> p s m u"),
             )
 
+        def read_y(on_vector, bank, g, count):
+            read_words(on_vector, bank, y_grouped[g // 4], g % 4, count)
+
         def turn_x(n, first, count):
             bank = psum.tile([P, count, 2, P], F32, name="bank_x", tag="bank")
             for s in range(count):
-                words = x_in[n, first + s].bitcast(F32)
                 for u in range(2):
-                    nc.tensor.transpose(bank[:, s, u, :], words[:, u::2], ident[:])
+                    nc.tensor.transpose(bank[:, s, u, :], x_rows[n, first + s].bitcast(F32)[:, u::2], ident[:])
             return bank
 
         def t_pass(bank, n, s, h, t):
@@ -220,56 +190,37 @@ def tile_ranktwokroneckersumlayer_x2_kernel(
                 )
             return bank
 
-        def add(bank, g):
-            n, j = g // 4, g % 4
-            out = v[n][:, D * j : D * j + D]
-            if g >= TILES - DIRECT:
-                nc.vector.tensor_tensor(
-                    out=out.rearrange("p (t m) -> p t m", t=4),
-                    in0=bank[:].rearrange("p (m t) -> p t m", t=4),
-                    in1=c_sb[:, j, :].rearrange("p (m t) -> p t m", t=4),
-                    op=ADD,
-                )
-            else:
-                nc.vector.tensor_tensor(out=out, in0=bank[:], in1=c_sb[:, j, :], op=ADD)
+        def add_c(bank, g):
+            nc.vector.tensor_tensor(out=band(z, g), in0=bank[:], in1=c_sb[:, g % 4, :], op=ADD)
+
+        def store_y(g):
+            nc.sync.dma_start(out=out_0[g // 4, P * (g % 4) : P * (g % 4) + P, :], in_=band(y, g))
 
         def silu(g):
-            n, j = g // 4, g % 4
-            cols = slice(D * j, D * j + D)
-            if g >= TILES - DIRECT:
-                nc.scalar.activation(
-                    o[n][:, cols].rearrange("p (m t) -> p m t", t=4), v[n][:, cols].rearrange("p (t m) -> p m t", t=4), SILU
+            nc.scalar.activation(band(y, g), band(z, g), SILU)
+            store_y(g)
+
+        def round_y(g):
+            if g <= LAST_ON_GPSIMD:
+                nc.gpsimd.tensor_scalar(
+                    out=rounded[g].rearrange("p (u k e) -> p u k e", u=2, e=2),
+                    in0=band(y, g).rearrange("p (k u e) -> p u k e", u=2, e=2),
+                    scalar1=1.0,
+                    scalar2=-0.0,
+                    op0=MULT,
+                    op1=ADD,
                 )
             else:
-                nc.scalar.activation(o[n][:, cols], v[n][:, cols], SILU)
-            nc.sync.dma_start(out=out_0[n, P * j : P * j + P, :], in_=o[n][:, cols])
+                nc.vector.tensor_copy(out=rounded[g], in_=band(y, g))
 
-        def cast(g):
-            out = rounded[g].rearrange("p (u k e) -> p u k e", u=2, e=2)
-            in_ = o[g // 4][:, D * (g % 4) : D * (g % 4) + D].rearrange("p (k u e) -> p u k e", u=2, e=2)
-            if g <= G_LAST:
-                nc.gpsimd.tensor_scalar(out=out, in0=in_, scalar1=1.0, scalar2=-0.0, op0=MULT, op1=ADD)
-            else:
-                nc.vector.tensor_copy(out=out, in_=in_)
-
-        def turn_result(g, count):
-            bank = psum.tile([P, count, 2, P], F32, name="bank_o", tag="bank")
+        def turn_y(g, count):
+            bank = psum.tile([P, count, 2, P], F32, name="bank_y", tag="bank")
             for s in range(count):
                 words = rounded[g + s].bitcast(F32)
                 for u in range(2):
-                    nc.tensor.transpose(bank[:, s, u, :], words[:, P * u : P * u + P], ident[:])
+                    in_ = words[:, P * u : P * u + P] if g + s <= LAST_ON_GPSIMD else words[:, u::2]
+                    nc.tensor.transpose(bank[:, s, u, :], in_, ident[:])
             return bank
-
-        def turn_sum(g):
-            n, j = g // 4, g % 4
-            bank = psum.tile([P, 4, P], F32, name="bank_d", tag="bank")
-            for t in range(4):
-                nc.tensor.transpose(bank[:, t, :], v[n][:, D * j + P * t : D * j + P * (t + 1)], ident[:])
-            return bank
-
-        def silu_turned(bank, g):
-            out = o_grouped[g // 4][:, D * (g % 4) : D * (g % 4) + D].rearrange("p (m t) -> p m t", t=4)
-            nc.scalar.activation(out, bank[:].rearrange("p t m -> p m t"), SILU)
 
         def warm_up(count):
             bank = psum.tile([P, 256], F32, name="bank_w", tag="bank")
@@ -284,71 +235,107 @@ def tile_ranktwokroneckersumlayer_x2_kernel(
                     stop=True,
                 )
 
-        if WARM[0]:
-            warm_up(WARM[0])
+        warm_up(WARM_FIRST)
         for t in range(4):
             read_words(t % 2 == 1, turn_x(0, t, 1), x_grouped[0], t, 1)
             if t == 1:
-                quantise(x_codes[0], x_scales[0], x_grouped[0], 0, 1)
-        if WARM[1]:
-            warm_up(WARM[1])
+                quantise_x(0, 0, 1)
+        warm_up(WARM_GAP)
         opened = [psum.tile([P, 4, P], F32, name="bank_t", tag="bank") for h in range(4)]
-        for t in range(4):
-            if t > 0:
-                quantise(x_codes[0], x_scales[0], x_grouped[0], t, 1)
-            for h in range(4 if t < OPEN else 0):
-                t_pass(opened[h], 0, 0, h, t)
         for h in range(4):
-            for t in range(OPEN, 4):
-                t_pass(opened[h], 0, 0, h, t)
+            t_pass(opened[h], 0, 0, h, 0)
+        quantise_x(0, 1, 1)
+        for h in range(4):
+            t_pass(opened[h], 0, 0, h, 1)
+        quantise_x(0, 2, 1)
+        quantise_x(0, 3, 1)
+        for h in range(4):
+            t_pass(opened[h], 0, 0, h, 2)
+            t_pass(opened[h], 0, 0, h, 3)
 
-        to_read = []
-        to_quantise = []
-        turned = 0
-        last = TILES - DIRECT
-        for beat in range(TILES + Z_LAG + 6):
+        turned_x, turned_y = [], []
+        read_x_halves, read_y_pairs = [], []
+        for beat in range(BEATS + 1):
             g = beat - Z_LAG
             banks = None
-            if beat < TILES:
+            if beat < BEATS:
                 banks = opened[2 * beat : 2 * beat + 2] if beat < 2 else [t_bank(beat, 0), t_bank(beat, 1)]
-            sums = z_bank(g) if 0 <= g < TILES else None
+            sums = z_bank(g) if g >= 0 else None
+            for n, first, bank in turned_x:
+                read_words(False, bank, x_grouped[n], first, 2)
+            for first, bank in turned_y:
+                read_y(False, bank, first, 2)
             if banks:
                 read_t(False, banks[0], beat, 0)
-            if 0 <= beat - 1 < TILES and g > Q_FIRST:
+            if g >= 0:
                 quantise_t(beat - 1)
-            for fn, args in to_quantise:
-                fn(*args)
-            to_quantise = []
-            if 0 <= g - 2 < last:
-                cast(g - 2)
-            for reader, read_args, fn, args in to_read[:R_MAX]:
-                reader(*read_args)
-                to_quantise.append((fn, args))
-            to_read = to_read[R_MAX:]
+            for n, first, bank in read_x_halves:
+                quantise_x(n, first, 2)
+            for first, bank in read_y_pairs:
+                quantise_y(first, 2)
+            read_x_halves, read_y_pairs = turned_x, turned_y
+            turned_x, turned_y = [], []
+            if g >= 2:
+                round_y(g - 2)
             if banks:
-                read_t(beat not in V_SKIP, banks[1], beat, 1)
-            if 0 <= beat - 1 < TILES and g <= Q_FIRST:
+                read_t(beat % 4 != 2, banks[1], beat, 1)
+            if g < 0 < beat:
                 quantise_t(beat - 1)
-            if sums is not None:
-                add(sums, g)
-            if 0 <= g - 1 < TILES:
+            if g >= 0:
+                add_c(sums, g)
+            if g >= 1:
                 silu(g - 1)
-            if beat % 4 == (X_PH if beat > 3 else X1_PH) and beat // 4 + 1 < B:
-                n = beat // 4 + 1
-                for first in (0, 2):
-                    bank = turn_x(n, first, 2)
-                    to_read.append(
-                        (read_words, (False, bank, x_grouped[n], first, 2), quantise, (x_codes[n], x_scales[n], x_grouped[n], first, 2))
-                    )
-            ready = min(g - 2 + (TAIL if beat >= TILES else 0), last)
-            if beat % O_MOD == O_PH or beat >= TILES:
-                while turned + 2 <= ready or turned < ready == last:
-                    count = min(2, ready - turned)
-                    bank = turn_result(turned, count)
-                    n, j = turned // 4, turned % 4
-                    to_read.append(
-                        (read_words, (turned >= O_V, bank, o_grouped[n], j, count), quantise_result, (n, j, count))
-                    )
-                    turned = turned + count
-            if last <= g - 1 < TILES:
-                to_read.append((silu_turned, (turn_sum(g - 1), g - 1), quantise_result, ((g - 1) // 4, (g - 1) % 4, 1)))
+            if beat % 4 == 0 and beat // 4 + 1 < B:
+                turned_x = [(beat // 4 + 1, first, turn_x(beat // 4 + 1, first, 2)) for first in (0, 2)]
+            if beat % 2 == 0 and g >= 5:
+                turned_y = [(g - 5, turn_y(g - 5, 2))]
+
+        first, bank = turned_y[0]
+        sums = {g: z_bank(g) for g in (12, 13)}
+        read_y(False, bank, 6, 2)
+        silu(11)
+        add_c(sums[12], 12)
+        add_c(sums[13], 13)
+        quantise_y(6, 2)
+        round_y(10)
+        bank = turn_y(8, 2)
+        sums = {g: z_bank(g) for g in (14, 15)}
+        silu(12)
+        round_y(11)
+        round_y(12)
+        read_y(False, bank, 8, 2)
+        add_c(sums[14], 14)
+        last = band(z, 15)
+        nc.vector.tensor_tensor(
+            out=last.rearrange("p (t m) -> p t m", t=4),
+            in0=sums[15][:].rearrange("p (m t) -> p t m", t=4),
+            in1=c_sb[:, 3, :].rearrange("p (m t) -> p t m", t=4),
+            op=ADD,
+        )
+        silu(13)
+        quantise_y(8, 2)
+        silu(14)
+        bank_10 = turn_y(10, 2)
+        bank_15 = psum.tile([P, 4, P], F32, name="bank_d", tag="bank")
+        for t in range(4):
+            nc.tensor.transpose(bank_15[:, t, :], last[:, P * t : P * t + P], ident[:])
+        nc.scalar.activation(band(y, 15).rearrange("p (m t) -> p m t", t=4), last.rearrange("p (t m) -> p m t", t=4), SILU)
+        store_y(15)
+        round_y(13)
+        round_y(14)
+        bank_12 = turn_y(12, 2)
+        bank_14 = turn_y(14, 1)
+        nc.scalar.activation(
+            band(y_grouped, 15).rearrange("p (m t) -> p m t", t=4), bank_15[:].rearrange("p t m -> p m t"), SILU
+        )
+        read_y(True, bank_10, 10, 2)
+        read_y(False, bank_12, 12, 2)
+        read_y(False, bank_14, 14, 1)
+        for g in (10, 12, 14):
+            quantise_y(g, 2)
+        rows = out_2[0].rearrange("r (n m) -> n r m", n=B)
+        for q in range(4):
+            queue = nc.sync if q < 2 else nc.scalar
+            queue.dma_start(
+                out=rows[:, 4 * q : 4 * q + 4, :].bitcast(I32), in_=y_scales[32 * q : 32 * q + 16, :].bitcast(I32)
+            )

@@ -21,9 +21,32 @@ FLOPS = 2 * 2 * 2 * B * D * D * D
 BEATS = 4 * B
 BANDS = 4 * B
 Z_LAG = 5
-LAST_ON_GPSIMD = 12
-WARM_FIRST, WARM_GAP = 5, 3
+ON_G = tuple(range(13))
+SKIP = (2, 6, 10, 14)
+Y_MOD = 2
+G_COLS = 512
+SEQ = 0
+WS = 1
+WX = 2
+WY = 1
+X1A = 1
+SORT1 = 1
+H1 = 1
+HALVES = 1
+C_LATE = 0
+WARM_FIRST = 5
+WARM_GAP = 3
 
+X1A = 0
+WS = 0
+WX = 2
+WY = 1
+HALVES = 0
+SORT1 = 0
+H1 = 2
+SEQ = [('Z', 12), ('Z', 13), ('R', 6, 0), ('S', 11), ('A', 12), ('A', 13), ('Q', 6, 2), ('C', 10), ('O', 8, 2), ('Z', 14), ('S', 12), ('Z', 15), ('C', 11), ('A', 14), ('C', 12), ('R', 8, 0), ('A', 15), ('S', 13), ('Q', 8, 2), ('S', 14), ('O', 10, 2), ('D', 15), ('S', 15), ('C', 13), ('C', 14), ('O', 12, 2), ('O', 14, 1), ('U', 15), ('R', 10, 1), ('R', 12, 0), ('R', 14, 0), ('Q', 10, 2), ('Q', 12, 2), ('Q', 14, 2)]
+WARM_FIRST = 4
+WARM_GAP = 2
 
 def tile_ranktwokroneckersumlayer_x2_kernel(
     tc, x, b1_words, b1_scales, b2_words, b2_scales, a1_words, a1_scales, a2_words, a2_scales, c, out_0, out_1, out_2
@@ -81,13 +104,14 @@ def tile_ranktwokroneckersumlayer_x2_kernel(
         load_words(0)
         load_scales(0)
         load_x(1, 0, 4)
-        for w in range(1, 4):
-            load_words(w)
         load_scales(1)
-        load_x(2, 0, 4)
+        load_words(1)
         load_scales(2)
-        nc.sync.dma_start(out=c_sb[:], in_=c.rearrange("(j p) q -> p j q", p=P))
+        load_x(2, 0, 4)
+        load_words(2)
+        load_words(3)
         load_scales(3)
+        nc.sync.dma_start(out=c_sb[:], in_=c.rearrange("(j p) q -> p j q", p=P))
         load_x(3, 0, 4)
 
         x_codes = [sbuf(f"x_codes{n}", [P, D], U32) for n in range(B)]
@@ -99,12 +123,14 @@ def tile_ranktwokroneckersumlayer_x2_kernel(
         z = [sbuf(f"z{n}", [P, 4 * D], F32) for n in range(B)]
         y = [sbuf(f"y{n}", [P, 4 * D], F32) for n in range(B)]
         rounded = [
-            t_grouped[g + Z_LAG + 1][:, 0:D] if g + Z_LAG + 1 < BEATS else sbuf(f"rounded{g}", [P, D], BF16)[:]
+            t_grouped[g + Z_LAG + 1 + WS][:, 0:D] if g + Z_LAG + 1 + WS < BEATS else sbuf(f"rounded{g}", [P, D], BF16)[:]
             for g in range(BANDS - 1)
         ]
         y_grouped = [sbuf(f"y_grouped{n}", [P, 4 * D], BF16) for n in range(B)]
         y_codes = sbuf("y_codes", [P, B * D], I32)
         y_scales = sbuf("y_scales", [P, D], U8)
+
+        x_sorted = sbuf("x_sorted", [P, 1024], F32)
 
         def band(tiles, g):
             return tiles[g // 4][:, D * (g % 4) : D * (g % 4) + D]
@@ -144,7 +170,10 @@ def tile_ranktwokroneckersumlayer_x2_kernel(
             bank = psum.tile([P, count, 2, P], F32, name="bank_x", tag="bank")
             for s in range(count):
                 for u in range(2):
-                    nc.tensor.transpose(bank[:, s, u, :], x_rows[n, first + s].bitcast(F32)[:, u::2], ident[:])
+                    in_ = x_rows[n, first + s].bitcast(F32)[:, u::2]
+                    if SORT1 and n == 1 and first >= 2 * X1A:
+                        in_ = x_sorted[:, 256 * (first + s) + P * u : 256 * (first + s) + P * (u + 1)]
+                    nc.tensor.transpose(bank[:, s, u, :], in_, ident[:])
             return bank
 
         def t_pass(bank, n, s, h, t):
@@ -175,6 +204,16 @@ def tile_ranktwokroneckersumlayer_x2_kernel(
                 out=t_codes[n][s][:, cols].bitcast(FP8X4), scales=t_scales[n][s][:, cols], in_=t_grouped[beat][:]
             )
 
+        def quantise_t_halves(beat):
+            n, s = beat // 4, beat % 4 // 2
+            for half in range(2):
+                cols = slice(256 * (beat % 2) + P * half, 256 * (beat % 2) + P * (half + 1))
+                nc.vector.quantize_mx(
+                    out=t_codes[n][s][:, cols].bitcast(FP8X4),
+                    scales=t_scales[n][s][:, cols],
+                    in_=t_grouped[beat][:, D * half : D * half + D],
+                )
+
         def z_bank(g):
             n, j = g // 4, g % 4
             bank = psum.tile([P, D], F32, name="bank_z", tag="bank")
@@ -200,8 +239,14 @@ def tile_ranktwokroneckersumlayer_x2_kernel(
             nc.scalar.activation(band(y, g), band(z, g), SILU)
             store_y(g)
 
+        def silu_pair(g):
+            cols = slice(D * (g % 4), D * (g % 4 + 2))
+            nc.scalar.activation(y[g // 4][:, cols], z[g // 4][:, cols], SILU)
+            rows = out_0[g // 4, P * (g % 4) : P * (g % 4 + 2), :].rearrange("(j p) q -> p j q", p=P)
+            nc.sync.dma_start(out=rows, in_=y[g // 4][:, cols].rearrange("p (j q) -> p j q", q=D))
+
         def round_y(g):
-            if g <= LAST_ON_GPSIMD:
+            if g in ON_G:
                 nc.gpsimd.tensor_scalar(
                     out=rounded[g].rearrange("p (u k e) -> p u k e", u=2, e=2),
                     in0=band(y, g).rearrange("p (k u e) -> p u k e", u=2, e=2),
@@ -218,7 +263,7 @@ def tile_ranktwokroneckersumlayer_x2_kernel(
             for s in range(count):
                 words = rounded[g + s].bitcast(F32)
                 for u in range(2):
-                    in_ = words[:, P * u : P * u + P] if g + s <= LAST_ON_GPSIMD else words[:, u::2]
+                    in_ = words[:, P * u : P * u + P] if g + s in ON_G else words[:, u::2]
                     nc.tensor.transpose(bank[:, s, u, :], in_, ident[:])
             return bank
 
@@ -240,7 +285,17 @@ def tile_ranktwokroneckersumlayer_x2_kernel(
             read_words(t % 2 == 1, turn_x(0, t, 1), x_grouped[0], t, 1)
             if t == 1:
                 quantise_x(0, 0, 1)
-        warm_up(WARM_GAP)
+        if WARM_GAP:
+            warm_up(WARM_GAP)
+        if X1A:
+            early = turn_x(1, 0, 2)
+            read_words(False, early, x_grouped[1], 0, 2)
+        if SORT1:
+            for t in range(2 * X1A, 4):
+                nc.scalar.copy(
+                    out=x_sorted[:, 256 * t : 256 * t + 256].rearrange("p (u m) -> p u m", u=2),
+                    in_=x_rows[1, t].bitcast(F32).rearrange("p (m u) -> p u m", u=2),
+                )
         opened = [psum.tile([P, 4, P], F32, name="bank_t", tag="bank") for h in range(4)]
         for h in range(4):
             t_pass(opened[h], 0, 0, h, 0)
@@ -253,6 +308,8 @@ def tile_ranktwokroneckersumlayer_x2_kernel(
             t_pass(opened[h], 0, 0, h, 2)
             t_pass(opened[h], 0, 0, h, 3)
 
+        if X1A:
+            quantise_x(1, 0, 2)
         turned_x, turned_y = [], []
         read_x_halves, read_y_pairs = [], []
         for beat in range(BEATS + 1):
@@ -261,78 +318,93 @@ def tile_ranktwokroneckersumlayer_x2_kernel(
             if beat < BEATS:
                 banks = opened[2 * beat : 2 * beat + 2] if beat < 2 else [t_bank(beat, 0), t_bank(beat, 1)]
             sums = z_bank(g) if g >= 0 else None
+            if beat == 1 and H1:
+                read_t(False, banks[0], beat, 0)
             for n, first, bank in turned_x:
-                read_words(False, bank, x_grouped[n], first, 2)
+                if not (beat == 1 and H1 == 1 and first == 2):
+                    read_words(False, bank, x_grouped[n], first, 2)
             for first, bank in turned_y:
                 read_y(False, bank, first, 2)
-            if banks:
+            if banks and not (beat == 1 and H1):
                 read_t(False, banks[0], beat, 0)
-            if g >= 0:
+            if HALVES and g - 2 - WS in ON_G and not (read_x_halves or read_y_pairs):
+                quantise_t_halves(beat - 1)
+            elif g >= 0:
                 quantise_t(beat - 1)
-            for n, first, bank in read_x_halves:
-                quantise_x(n, first, 2)
+            if WX and len(read_x_halves) == 2 and read_x_halves[0][0] >= WX:
+                quantise_x(read_x_halves[0][0], 0, 4)
+            else:
+                for n, first, bank in read_x_halves:
+                    quantise_x(n, first, 2)
             for first, bank in read_y_pairs:
-                quantise_y(first, 2)
+                if not WY or first >= 4:
+                    quantise_y(first, 2)
+                elif first == 2:
+                    quantise_y(0, 4)
             read_x_halves, read_y_pairs = turned_x, turned_y
             turned_x, turned_y = [], []
-            if g >= 2:
-                round_y(g - 2)
+            if g - 2 - WS >= 0:
+                round_y(g - 2 - WS)
             if banks:
-                read_t(beat % 4 != 2, banks[1], beat, 1)
+                read_t(beat not in SKIP, banks[1], beat, 1)
             if g < 0 < beat:
                 quantise_t(beat - 1)
+            if beat == 1 and H1 == 1:
+                read_words(True, read_x_halves[-1][2], x_grouped[1], 2, 2)
             if g >= 0:
                 add_c(sums, g)
-            if g >= 1:
+            if g >= 1 and (not WS or g - 1 >= 10):
                 silu(g - 1)
+            elif g >= 2 and g % 2 == 0:
+                silu_pair(g - 2)
             if beat % 4 == 0 and beat // 4 + 1 < B:
-                turned_x = [(beat // 4 + 1, first, turn_x(beat // 4 + 1, first, 2)) for first in (0, 2)]
-            if beat % 2 == 0 and g >= 5:
+                turned_x = [(beat // 4 + 1, first, turn_x(beat // 4 + 1, first, 2)) for first in ((2,) if X1A and beat == 0 else (0, 2))]
+            if beat % 2 == 0 and g >= 5 and Y_MOD == 2:
                 turned_y = [(g - 5, turn_y(g - 5, 2))]
+            if beat % 4 == 0 and g >= 5 and Y_MOD == 4:
+                turned_y = [(f, turn_y(f, 2)) for f in (g - 7, g - 5)]
 
-        first, bank = turned_y[0]
-        sums = {g: z_bank(g) for g in (12, 13)}
-        read_y(False, bank, 6, 2)
-        silu(11)
-        add_c(sums[12], 12)
-        add_c(sums[13], 13)
-        quantise_y(6, 2)
-        round_y(10)
-        bank = turn_y(8, 2)
-        sums = {g: z_bank(g) for g in (14, 15)}
-        silu(12)
-        round_y(11)
-        round_y(12)
-        read_y(False, bank, 8, 2)
-        add_c(sums[14], 14)
+        bank_of = {("O", f): (b, 2) for f, b in turned_y}
+        if Y_MOD == 4:
+            read_y(False, bank_of["O", 4][0], 4, 2)
+            quantise_y(4, 2)
         last = band(z, 15)
-        nc.vector.tensor_tensor(
-            out=last.rearrange("p (t m) -> p t m", t=4),
-            in0=sums[15][:].rearrange("p (m t) -> p t m", t=4),
-            in1=c_sb[:, 3, :].rearrange("p (m t) -> p t m", t=4),
-            op=ADD,
-        )
-        silu(13)
-        quantise_y(8, 2)
-        silu(14)
-        bank_10 = turn_y(10, 2)
-        bank_15 = psum.tile([P, 4, P], F32, name="bank_d", tag="bank")
-        for t in range(4):
-            nc.tensor.transpose(bank_15[:, t, :], last[:, P * t : P * t + P], ident[:])
-        nc.scalar.activation(band(y, 15).rearrange("p (m t) -> p m t", t=4), last.rearrange("p (t m) -> p m t", t=4), SILU)
-        store_y(15)
-        round_y(13)
-        round_y(14)
-        bank_12 = turn_y(12, 2)
-        bank_14 = turn_y(14, 1)
-        nc.scalar.activation(
-            band(y_grouped, 15).rearrange("p (m t) -> p m t", t=4), bank_15[:].rearrange("p t m -> p m t"), SILU
-        )
-        read_y(True, bank_10, 10, 2)
-        read_y(False, bank_12, 12, 2)
-        read_y(False, bank_14, 14, 1)
-        for g in (10, 12, 14):
-            quantise_y(g, 2)
+        if WS:
+            round_y(9)
+        for tok in SEQ:
+            k, g = tok[0], tok[1]
+            if k == "Z":
+                bank_of["Z", g] = z_bank(g)
+            elif k == "A" and g < 15:
+                add_c(bank_of["Z", g], g)
+            elif k == "A":
+                nc.vector.tensor_tensor(
+                    out=last.rearrange("p (t m) -> p t m", t=4),
+                    in0=bank_of["Z", g][:].rearrange("p (m t) -> p t m", t=4),
+                    in1=c_sb[:, 3, :].rearrange("p (m t) -> p t m", t=4),
+                    op=ADD,
+                )
+            elif k == "S" and g < 15:
+                silu(g)
+            elif k == "S":
+                nc.scalar.activation(band(y, 15).rearrange("p (m t) -> p m t", t=4), last.rearrange("p (t m) -> p m t", t=4), SILU)
+                store_y(15)
+            elif k == "C":
+                round_y(g)
+            elif k == "O":
+                bank_of["O", g] = (turn_y(g, tok[2]), tok[2])
+            elif k == "R":
+                read_y(tok[2], bank_of["O", g][0], g, bank_of["O", g][1])
+            elif k == "D":
+                bank_15 = psum.tile([P, 4, P], F32, name="bank_d", tag="bank")
+                for t in range(4):
+                    nc.tensor.transpose(bank_15[:, t, :], last[:, P * t : P * t + P], ident[:])
+            elif k == "U":
+                nc.scalar.activation(
+                    band(y_grouped, 15).rearrange("p (m t) -> p m t", t=4), bank_15[:].rearrange("p t m -> p m t"), SILU
+                )
+            elif k == "Q":
+                quantise_y(g, tok[2])
         rows = out_2[0].rearrange("r (n m) -> n r m", n=B)
         for q in range(4):
             queue = nc.sync if q < 2 else nc.scalar

@@ -66,16 +66,14 @@ def tile_ranktwokroneckersumlayer_x2_kernel(
         zero_scales = sbuf("zero_scales", [P, 256], U8)
         table_in = sbuf("table_in", [P, 1], F32)
         ident = sbuf("ident", [P, P], F32)
+        nc.vector.memset(w_scales[0][:].bitcast(I32), 0)
         nc.vector.memset(zeros[:].bitcast(I32), 0)
         nc.vector.memset(table_in[:], 0.0)
-        nc.vector.memset(w_scales[0][:].bitcast(I32), 0)
         nc.vector.quantize_mx(out=zero_codes[:].bitcast(FP8X4), scales=zero_scales[:], in_=zeros[:])
         nc.vector.memset(ident[:], 0.0)
         make_identity(nc, ident[:], nomemset=True)
         for w in range(1, 4):
             nc.vector.memset(w_scales[w][:].bitcast(I32), 0)
-        table_out = sbuf("table_out", [P, 1], F32)
-        nc.scalar.activation(table_out[:], table_in[:], SILU)
 
         x_rows = {}
         w_words = [sbuf(f"w_words{w}", [P, 2 * D], U8) for w in range(4)]
@@ -94,7 +92,7 @@ def tile_ranktwokroneckersumlayer_x2_kernel(
 
         def load_scales(w):
             for q in range(4):
-                nc.sync.dma_start(
+                (nc.scalar if w == 0 else nc.sync).dma_start(
                     out=w_scales[w][32 * q : 32 * q + 4, :].bitcast(I32),
                     in_=scales_in[w][0, 4 * q : 4 * q + 4, :].bitcast(I32),
                 )
@@ -103,6 +101,8 @@ def tile_ranktwokroneckersumlayer_x2_kernel(
         load_x(0, 2, 2)
         load_words(0)
         load_scales(0)
+        table_out = sbuf("table_out", [P, 1], F32)
+        nc.scalar.activation(table_out[:], table_in[:], SILU)
         load_x(1, 0, 4)
         load_scales(1)
         load_words(1)

@@ -20,33 +20,12 @@ FLOPS = 2 * 2 * 2 * B * D * D * D
 
 BEATS = 4 * B
 BANDS = 4 * B
+TERMS = 2 * B
 Z_LAG = 5
-ON_G = tuple(range(13))
-SKIP = (2, 6, 10, 14)
-Y_MOD = 2
-G_COLS = 512
-SEQ = 0
-WS = 1
-WX = 2
-WY = 1
-X1A = 1
-SORT1 = 1
-H1 = 1
-HALVES = 1
-C_LATE = 0
-WARM_FIRST = 5
-WARM_GAP = 3
+SCALAR_BEAT = 2
+LAST_ON_GPSIMD = 12
+WARM_FIRST, WARM_GAP = 4, 2
 
-X1A = 0
-WS = 0
-WX = 2
-WY = 1
-HALVES = 0
-SORT1 = 0
-H1 = 2
-SEQ = [('Z', 12), ('Z', 13), ('R', 6, 0), ('S', 11), ('A', 12), ('A', 13), ('Q', 6, 2), ('C', 10), ('O', 8, 2), ('Z', 14), ('S', 12), ('Z', 15), ('C', 11), ('A', 14), ('C', 12), ('R', 8, 0), ('A', 15), ('S', 13), ('Q', 8, 2), ('S', 14), ('O', 10, 2), ('D', 15), ('S', 15), ('C', 13), ('C', 14), ('O', 12, 2), ('O', 14, 1), ('U', 15), ('R', 10, 1), ('R', 12, 0), ('R', 14, 0), ('Q', 10, 2), ('Q', 12, 2), ('Q', 14, 2)]
-WARM_FIRST = 4
-WARM_GAP = 2
 
 def tile_ranktwokroneckersumlayer_x2_kernel(
     tc, x, b1_words, b1_scales, b2_words, b2_scales, a1_words, a1_scales, a2_words, a2_scales, c, out_0, out_1, out_2
@@ -90,9 +69,9 @@ def tile_ranktwokroneckersumlayer_x2_kernel(
         def load_words(w):
             nc.sync.dma_start(out=w_words[w][:].bitcast(I32), in_=words_in[w][0].bitcast(I32))
 
-        def load_scales(w):
+        def load_scales(w, queue):
             for q in range(4):
-                (nc.scalar if w == 0 else nc.sync).dma_start(
+                queue.dma_start(
                     out=w_scales[w][32 * q : 32 * q + 4, :].bitcast(I32),
                     in_=scales_in[w][0, 4 * q : 4 * q + 4, :].bitcast(I32),
                 )
@@ -100,17 +79,17 @@ def tile_ranktwokroneckersumlayer_x2_kernel(
         load_x(0, 0, 2)
         load_x(0, 2, 2)
         load_words(0)
-        load_scales(0)
+        load_scales(0, nc.scalar)
         table_out = sbuf("table_out", [P, 1], F32)
         nc.scalar.activation(table_out[:], table_in[:], SILU)
         load_x(1, 0, 4)
-        load_scales(1)
+        load_scales(1, nc.sync)
         load_words(1)
-        load_scales(2)
+        load_scales(2, nc.sync)
         load_x(2, 0, 4)
         load_words(2)
         load_words(3)
-        load_scales(3)
+        load_scales(3, nc.sync)
         nc.sync.dma_start(out=c_sb[:], in_=c.rearrange("(j p) q -> p j q", p=P))
         load_x(3, 0, 4)
 
@@ -119,18 +98,20 @@ def tile_ranktwokroneckersumlayer_x2_kernel(
         x_grouped = [sbuf(f"x_grouped{n}", [P, 4 * D], BF16) for n in range(B)]
         t_codes = [[sbuf(f"t_codes{n}{s}", [P, D], U32) for s in range(2)] for n in range(B)]
         t_scales = [[sbuf(f"t_scales{n}{s}", [P, D], U8) for s in range(2)] for n in range(B)]
-        t_grouped = [sbuf(f"t_grouped{beat}", [P, 2 * D], BF16) for beat in range(BEATS)]
+        t_terms = [sbuf(f"t_grouped{term}", [P, 4 * D], BF16) for term in range(TERMS)]
+        t_grouped = [t_terms[beat // 2][:, 2 * D * (beat % 2) : 2 * D * (beat % 2 + 1)] for beat in range(BEATS)]
         z = [sbuf(f"z{n}", [P, 4 * D], F32) for n in range(B)]
         y = [sbuf(f"y{n}", [P, 4 * D], F32) for n in range(B)]
-        rounded = [
-            t_grouped[g + Z_LAG + 1 + WS][:, 0:D] if g + Z_LAG + 1 + WS < BEATS else sbuf(f"rounded{g}", [P, D], BF16)[:]
-            for g in range(BANDS - 1)
-        ]
+        rounded = []
+        for g in range(BANDS - 1):
+            before = g + Z_LAG + 1
+            if before >= BEATS:
+                rounded.append(sbuf(f"rounded{g}", [P, D], BF16)[:])
+            else:
+                rounded.append(t_grouped[before if before // 2 == TERMS - 1 else before - 1][:, 0:D])
         y_grouped = [sbuf(f"y_grouped{n}", [P, 4 * D], BF16) for n in range(B)]
         y_codes = sbuf("y_codes", [P, B * D], I32)
         y_scales = sbuf("y_scales", [P, D], U8)
-
-        x_sorted = sbuf("x_sorted", [P, 1024], F32)
 
         def band(tiles, g):
             return tiles[g // 4][:, D * (g % 4) : D * (g % 4) + D]
@@ -170,10 +151,7 @@ def tile_ranktwokroneckersumlayer_x2_kernel(
             bank = psum.tile([P, count, 2, P], F32, name="bank_x", tag="bank")
             for s in range(count):
                 for u in range(2):
-                    in_ = x_rows[n, first + s].bitcast(F32)[:, u::2]
-                    if SORT1 and n == 1 and first >= 2 * X1A:
-                        in_ = x_sorted[:, 256 * (first + s) + P * u : 256 * (first + s) + P * (u + 1)]
-                    nc.tensor.transpose(bank[:, s, u, :], in_, ident[:])
+                    nc.tensor.transpose(bank[:, s, u, :], x_rows[n, first + s].bitcast(F32)[:, u::2], ident[:])
             return bank
 
         def t_pass(bank, n, s, h, t):
@@ -199,20 +177,12 @@ def tile_ranktwokroneckersumlayer_x2_kernel(
             copy(on_vector, out, bank[:].rearrange("p t q -> p q t"))
 
         def quantise_t(beat):
-            n, s, cols = beat // 4, beat % 4 // 2, slice(256 * (beat % 2), 256 * (beat % 2) + 256)
-            nc.vector.quantize_mx(
-                out=t_codes[n][s][:, cols].bitcast(FP8X4), scales=t_scales[n][s][:, cols], in_=t_grouped[beat][:]
-            )
-
-        def quantise_t_halves(beat):
-            n, s = beat // 4, beat % 4 // 2
-            for half in range(2):
-                cols = slice(256 * (beat % 2) + P * half, 256 * (beat % 2) + P * (half + 1))
-                nc.vector.quantize_mx(
-                    out=t_codes[n][s][:, cols].bitcast(FP8X4),
-                    scales=t_scales[n][s][:, cols],
-                    in_=t_grouped[beat][:, D * half : D * half + D],
-                )
+            term = (beat - 1) // 2
+            n, s = term // 2, term % 2
+            if beat < Z_LAG or term == TERMS - 1:
+                quantise(t_codes[n][s], t_scales[n][s], t_terms[term], 2 * ((beat - 1) % 2), 2)
+            elif beat % 2 == 0:
+                quantise(t_codes[n][s], t_scales[n][s], t_terms[term], 0, 4)
 
         def z_bank(g):
             n, j = g // 4, g % 4
@@ -239,14 +209,8 @@ def tile_ranktwokroneckersumlayer_x2_kernel(
             nc.scalar.activation(band(y, g), band(z, g), SILU)
             store_y(g)
 
-        def silu_pair(g):
-            cols = slice(D * (g % 4), D * (g % 4 + 2))
-            nc.scalar.activation(y[g // 4][:, cols], z[g // 4][:, cols], SILU)
-            rows = out_0[g // 4, P * (g % 4) : P * (g % 4 + 2), :].rearrange("(j p) q -> p j q", p=P)
-            nc.sync.dma_start(out=rows, in_=y[g // 4][:, cols].rearrange("p (j q) -> p j q", q=D))
-
         def round_y(g):
-            if g in ON_G:
+            if g <= LAST_ON_GPSIMD:
                 nc.gpsimd.tensor_scalar(
                     out=rounded[g].rearrange("p (u k e) -> p u k e", u=2, e=2),
                     in0=band(y, g).rearrange("p (k u e) -> p u k e", u=2, e=2),
@@ -263,7 +227,7 @@ def tile_ranktwokroneckersumlayer_x2_kernel(
             for s in range(count):
                 words = rounded[g + s].bitcast(F32)
                 for u in range(2):
-                    in_ = words[:, P * u : P * u + P] if g + s in ON_G else words[:, u::2]
+                    in_ = words[:, P * u : P * u + P] if g + s <= LAST_ON_GPSIMD else words[:, u::2]
                     nc.tensor.transpose(bank[:, s, u, :], in_, ident[:])
             return bank
 
@@ -285,17 +249,7 @@ def tile_ranktwokroneckersumlayer_x2_kernel(
             read_words(t % 2 == 1, turn_x(0, t, 1), x_grouped[0], t, 1)
             if t == 1:
                 quantise_x(0, 0, 1)
-        if WARM_GAP:
-            warm_up(WARM_GAP)
-        if X1A:
-            early = turn_x(1, 0, 2)
-            read_words(False, early, x_grouped[1], 0, 2)
-        if SORT1:
-            for t in range(2 * X1A, 4):
-                nc.scalar.copy(
-                    out=x_sorted[:, 256 * t : 256 * t + 256].rearrange("p (u m) -> p u m", u=2),
-                    in_=x_rows[1, t].bitcast(F32).rearrange("p (m u) -> p u m", u=2),
-                )
+        warm_up(WARM_GAP)
         opened = [psum.tile([P, 4, P], F32, name="bank_t", tag="bank") for h in range(4)]
         for h in range(4):
             t_pass(opened[h], 0, 0, h, 0)
@@ -308,103 +262,89 @@ def tile_ranktwokroneckersumlayer_x2_kernel(
             t_pass(opened[h], 0, 0, h, 2)
             t_pass(opened[h], 0, 0, h, 3)
 
-        if X1A:
-            quantise_x(1, 0, 2)
-        turned_x, turned_y = [], []
-        read_x_halves, read_y_pairs = [], []
+        turned_x, turned_y = [], None
         for beat in range(BEATS + 1):
             g = beat - Z_LAG
+            n_next = beat // 4 + 1
             banks = None
             if beat < BEATS:
                 banks = opened[2 * beat : 2 * beat + 2] if beat < 2 else [t_bank(beat, 0), t_bank(beat, 1)]
             sums = z_bank(g) if g >= 0 else None
-            if beat == 1 and H1:
+            t_is_older = beat < 2
+            if t_is_older:
                 read_t(False, banks[0], beat, 0)
-            for n, first, bank in turned_x:
-                if not (beat == 1 and H1 == 1 and first == 2):
-                    read_words(False, bank, x_grouped[n], first, 2)
-            for first, bank in turned_y:
-                read_y(False, bank, first, 2)
-            if banks and not (beat == 1 and H1):
+            for half, bank in enumerate(turned_x):
+                read_words(False, bank, x_grouped[n_next], 2 * half, 2)
+            if turned_y:
+                read_y(False, turned_y, g - 6, 2)
+            turned_x, turned_y = [], None
+            if banks and not t_is_older:
                 read_t(False, banks[0], beat, 0)
-            if HALVES and g - 2 - WS in ON_G and not (read_x_halves or read_y_pairs):
-                quantise_t_halves(beat - 1)
-            elif g >= 0:
-                quantise_t(beat - 1)
-            if WX and len(read_x_halves) == 2 and read_x_halves[0][0] >= WX:
-                quantise_x(read_x_halves[0][0], 0, 4)
-            else:
-                for n, first, bank in read_x_halves:
-                    quantise_x(n, first, 2)
-            for first, bank in read_y_pairs:
-                if not WY or first >= 4:
-                    quantise_y(first, 2)
-                elif first == 2:
-                    quantise_y(0, 4)
-            read_x_halves, read_y_pairs = turned_x, turned_y
-            turned_x, turned_y = [], []
-            if g - 2 - WS >= 0:
-                round_y(g - 2 - WS)
+            if g >= 0:
+                quantise_t(beat)
+            if beat == 2:
+                quantise_x(1, 0, 2)
+                quantise_x(1, 2, 2)
+            elif beat % 4 == 2 and n_next < B:
+                quantise_x(n_next, 0, 4)
+            if g - 7 == 2:
+                quantise_y(0, 4)
+            elif g - 7 == 4:
+                quantise_y(4, 2)
+            if g >= 2:
+                round_y(g - 2)
             if banks:
-                read_t(beat not in SKIP, banks[1], beat, 1)
+                read_t(beat % 4 != SCALAR_BEAT, banks[1], beat, 1)
             if g < 0 < beat:
-                quantise_t(beat - 1)
-            if beat == 1 and H1 == 1:
-                read_words(True, read_x_halves[-1][2], x_grouped[1], 2, 2)
+                quantise_t(beat)
             if g >= 0:
                 add_c(sums, g)
-            if g >= 1 and (not WS or g - 1 >= 10):
+            if g >= 1:
                 silu(g - 1)
-            elif g >= 2 and g % 2 == 0:
-                silu_pair(g - 2)
-            if beat % 4 == 0 and beat // 4 + 1 < B:
-                turned_x = [(beat // 4 + 1, first, turn_x(beat // 4 + 1, first, 2)) for first in ((2,) if X1A and beat == 0 else (0, 2))]
-            if beat % 2 == 0 and g >= 5 and Y_MOD == 2:
-                turned_y = [(g - 5, turn_y(g - 5, 2))]
-            if beat % 4 == 0 and g >= 5 and Y_MOD == 4:
-                turned_y = [(f, turn_y(f, 2)) for f in (g - 7, g - 5)]
+            if beat % 4 == 0 and n_next < B:
+                turned_x = [turn_x(n_next, 2 * half, 2) for half in range(2)]
+            if beat % 2 == 0 and g >= 5:
+                turned_y = turn_y(g - 5, 2)
 
-        bank_of = {("O", f): (b, 2) for f, b in turned_y}
-        if Y_MOD == 4:
-            read_y(False, bank_of["O", 4][0], 4, 2)
-            quantise_y(4, 2)
-        last = band(z, 15)
-        if WS:
-            round_y(9)
-        for tok in SEQ:
-            k, g = tok[0], tok[1]
-            if k == "Z":
-                bank_of["Z", g] = z_bank(g)
-            elif k == "A" and g < 15:
-                add_c(bank_of["Z", g], g)
-            elif k == "A":
+        for g in (12, 14):
+            pair = g - 6
+            sums = [z_bank(g), z_bank(g + 1)]
+            read_y(False, turned_y, pair, 2)
+            add_c(sums[0], g)
+            if g + 1 < BANDS - 1:
+                add_c(sums[1], g + 1)
+            else:
+                last_z = band(z, g + 1)
                 nc.vector.tensor_tensor(
-                    out=last.rearrange("p (t m) -> p t m", t=4),
-                    in0=bank_of["Z", g][:].rearrange("p (m t) -> p t m", t=4),
+                    out=last_z.rearrange("p (t m) -> p t m", t=4),
+                    in0=sums[1][:].rearrange("p (m t) -> p t m", t=4),
                     in1=c_sb[:, 3, :].rearrange("p (m t) -> p t m", t=4),
                     op=ADD,
                 )
-            elif k == "S" and g < 15:
-                silu(g)
-            elif k == "S":
-                nc.scalar.activation(band(y, 15).rearrange("p (m t) -> p m t", t=4), last.rearrange("p (t m) -> p m t", t=4), SILU)
-                store_y(15)
-            elif k == "C":
-                round_y(g)
-            elif k == "O":
-                bank_of["O", g] = (turn_y(g, tok[2]), tok[2])
-            elif k == "R":
-                read_y(tok[2], bank_of["O", g][0], g, bank_of["O", g][1])
-            elif k == "D":
-                bank_15 = psum.tile([P, 4, P], F32, name="bank_d", tag="bank")
-                for t in range(4):
-                    nc.tensor.transpose(bank_15[:, t, :], last[:, P * t : P * t + P], ident[:])
-            elif k == "U":
-                nc.scalar.activation(
-                    band(y_grouped, 15).rearrange("p (m t) -> p m t", t=4), bank_15[:].rearrange("p t m -> p m t"), SILU
-                )
-            elif k == "Q":
-                quantise_y(g, tok[2])
+            silu(g - 1)
+            quantise_y(pair, 2)
+            silu(g)
+            if g == 12:
+                for done in range(10, LAST_ON_GPSIMD + 1):
+                    round_y(done)
+            turned_y = turn_y(pair + 2, 2)
+        last_bank = psum.tile([P, 4, P], F32, name="bank_d", tag="bank")
+        for t in range(4):
+            nc.tensor.transpose(last_bank[:, t, :], last_z[:, P * t : P * t + P], ident[:])
+        nc.scalar.activation(band(y, 15).rearrange("p (m t) -> p m t", t=4), last_z.rearrange("p (t m) -> p m t", t=4), SILU)
+        store_y(15)
+        round_y(13)
+        round_y(14)
+        bank_12 = turn_y(12, 2)
+        bank_14 = turn_y(14, 1)
+        nc.scalar.activation(
+            band(y_grouped, 15).rearrange("p (m t) -> p m t", t=4), last_bank[:].rearrange("p t m -> p m t"), SILU
+        )
+        read_y(True, turned_y, 10, 2)
+        read_y(False, bank_12, 12, 2)
+        read_y(False, bank_14, 14, 1)
+        for g in (10, 12, 14):
+            quantise_y(g, 2)
         rows = out_2[0].rearrange("r (n m) -> n r m", n=B)
         for q in range(4):
             queue = nc.sync if q < 2 else nc.scalar

@@ -17,14 +17,8 @@ MULT = mybir.AluOpType.mult
 B, D = 4, 512
 P = 128
 FLOPS = 2 * 2 * 2 * B * D * D * D
-
-BEATS = 4 * B
-BANDS = 4 * B
-TERMS = 2 * B
-Z_LAG = 5
-SCALAR_BEAT = 2
-LAST_ON_GPSIMD = 12
-WARM_FIRST, WARM_GAP = 4, 2
+BANKS = 8
+WARM_FIRST, WARM_GAP = 2, 1
 
 
 def tile_ranktwokroneckersumlayer_x2_kernel(
@@ -33,22 +27,28 @@ def tile_ranktwokroneckersumlayer_x2_kernel(
     nc = tc.nc
     with ExitStack() as ctx:
         keep = ctx.enter_context(tc.tile_pool(name="keep", bufs=1))
-        psum = ctx.enter_context(tc.psum_pool(name="psum", bufs=8))
+        psum = ctx.enter_context(tc.psum_pool(name="psum", bufs=1))
         ctx.enter_context(tc.manual_schedule())
 
         def sbuf(name, shape, dtype):
             return keep.tile(shape, dtype, name=name, align_bytes=256)
 
+        taken = []
+
+        def next_bank(kind, shape):
+            taken.append(kind)
+            return psum.tile(shape, F32, name=kind, tag=f"bank{len(taken) % BANKS}")
+
         w_scales = [sbuf(f"w_scales{w}", [P, D], U8) for w in range(4)]
-        zeros = sbuf("zeros", [P, 1024], BF16)
+        zeros = sbuf("zeros", [P, P], BF16)
         zero_codes = sbuf("zero_codes", [P, 256], U32)
-        zero_scales = sbuf("zero_scales", [P, 256], U8)
-        table_in = sbuf("table_in", [P, 1], F32)
+        zero_scales = sbuf("zero_scales", [P, D], U8)
         ident = sbuf("ident", [P, P], F32)
-        nc.vector.memset(w_scales[0][:].bitcast(I32), 0)
         nc.vector.memset(zeros[:].bitcast(I32), 0)
-        nc.vector.memset(table_in[:], 0.0)
-        nc.vector.quantize_mx(out=zero_codes[:].bitcast(FP8X4), scales=zero_scales[:], in_=zeros[:])
+        nc.vector.memset(zero_codes[:, 32:], 0)
+        nc.vector.memset(zero_scales[:, 32:].bitcast(I32), 0)
+        nc.vector.quantize_mx(out=zero_codes[:, 0:32].bitcast(FP8X4), scales=zero_scales[:, 0:32], in_=zeros[:])
+        nc.vector.memset(w_scales[0][:].bitcast(I32), 0)
         nc.vector.memset(ident[:], 0.0)
         make_identity(nc, ident[:], nomemset=True)
         for w in range(1, 4):
@@ -76,20 +76,21 @@ def tile_ranktwokroneckersumlayer_x2_kernel(
                     in_=scales_in[w][0, 4 * q : 4 * q + 4, :].bitcast(I32),
                 )
 
-        load_x(0, 0, 2)
-        load_x(0, 2, 2)
-        load_words(0)
-        load_scales(0, nc.scalar)
         table_out = sbuf("table_out", [P, 1], F32)
-        nc.scalar.activation(table_out[:], table_in[:], SILU)
+        nc.scalar.activation(table_out[:], zeros[:, 0:1], SILU)
+        load_x(0, 0, 2)
+        load_x(0, 2, 1)
+        load_x(0, 3, 1)
+        load_words(0)
+        load_scales(0, nc.sync)
         load_x(1, 0, 4)
         load_scales(1, nc.sync)
         load_words(1)
-        load_scales(2, nc.sync)
         load_x(2, 0, 4)
+        load_scales(2, nc.sync)
         load_words(2)
-        load_words(3)
         load_scales(3, nc.sync)
+        load_words(3)
         nc.sync.dma_start(out=c_sb[:], in_=c.rearrange("(j p) q -> p j q", p=P))
         load_x(3, 0, 4)
 
@@ -98,23 +99,17 @@ def tile_ranktwokroneckersumlayer_x2_kernel(
         x_grouped = [sbuf(f"x_grouped{n}", [P, 4 * D], BF16) for n in range(B)]
         t_codes = [[sbuf(f"t_codes{n}{s}", [P, D], U32) for s in range(2)] for n in range(B)]
         t_scales = [[sbuf(f"t_scales{n}{s}", [P, D], U8) for s in range(2)] for n in range(B)]
-        t_terms = [sbuf(f"t_grouped{term}", [P, 4 * D], BF16) for term in range(TERMS)]
-        t_grouped = [t_terms[beat // 2][:, 2 * D * (beat % 2) : 2 * D * (beat % 2 + 1)] for beat in range(BEATS)]
+        t_grouped = [[sbuf(f"t_grouped{n}{s}", [P, 4 * D], BF16) for s in range(2)] for n in range(B)]
         z = [sbuf(f"z{n}", [P, 4 * D], F32) for n in range(B)]
         y = [sbuf(f"y{n}", [P, 4 * D], F32) for n in range(B)]
-        rounded = []
-        for g in range(BANDS - 1):
-            before = g + Z_LAG + 1
-            if before >= BEATS:
-                rounded.append(sbuf(f"rounded{g}", [P, D], BF16)[:])
-            else:
-                rounded.append(t_grouped[before if before // 2 == TERMS - 1 else before - 1][:, 0:D])
-        y_grouped = [sbuf(f"y_grouped{n}", [P, 4 * D], BF16) for n in range(B)]
+        y_all = sbuf("y_grouped", [P, B * 4 * D], BF16)
+        y_grouped = [y_all[:, 4 * D * n : 4 * D * (n + 1)] for n in range(B)]
         y_codes = sbuf("y_codes", [P, B * D], I32)
         y_scales = sbuf("y_scales", [P, D], U8)
+        rounded = {}
 
-        def band(tiles, g):
-            return tiles[g // 4][:, D * (g % 4) : D * (g % 4) + D]
+        def band(tiles, g, count=1):
+            return tiles[g // 4][:, D * (g % 4) : D * (g % 4 + count)]
 
         def copy(on_vector, out, in_):
             if on_vector:
@@ -131,9 +126,16 @@ def tile_ranktwokroneckersumlayer_x2_kernel(
         def quantise_x(n, first, count):
             quantise(x_codes[n], x_scales[n], x_grouped[n], first, count)
 
-        def quantise_y(g, count):
+        def quantise_t(n, s, first=0, count=4):
+            quantise(t_codes[n][s], t_scales[n][s], t_grouped[n][s], first, count)
+
+        def quantise_y(g, count, stored=None):
             n = g // 4
             quantise(y_codes[:, D * n : D * n + D], y_scales[4 * n :, :], y_grouped[n], g % 4, count)
+            if stored != 0:
+                store_codes(g + count - (stored or count), stored or count)
+
+        def store_codes(g, count):
             cols = slice(P * g, P * (g + count))
             nc.sync.dma_start(out=out_1[0, :, cols, :].rearrange("p m t -> p (m t)").bitcast(I32), in_=y_codes[:, cols])
 
@@ -144,11 +146,11 @@ def tile_ranktwokroneckersumlayer_x2_kernel(
                 bank[:].rearrange("p s u m -> p s m u"),
             )
 
-        def read_y(on_vector, bank, g, count):
-            read_words(on_vector, bank, y_grouped[g // 4], g % 4, count)
+        def read_y(on_vector, bank, g, count=2):
+            read_words(on_vector, bank, y_all, g, count)
 
         def turn_x(n, first, count):
-            bank = psum.tile([P, count, 2, P], F32, name="bank_x", tag="bank")
+            bank = next_bank("bank_x", [P, count, 2, P])
             for s in range(count):
                 for u in range(2):
                     nc.tensor.transpose(bank[:, s, u, :], x_rows[n, first + s].bitcast(F32)[:, u::2], ident[:])
@@ -166,185 +168,266 @@ def tile_ranktwokroneckersumlayer_x2_kernel(
                 stop=True,
             )
 
-        def t_bank(beat, half):
-            bank = psum.tile([P, 4, P], F32, name="bank_t", tag="bank")
+        def t_bank(n, s, h):
+            bank = next_bank("bank_t", [P, 4, P])
             for t in range(4):
-                t_pass(bank, beat // 4, beat % 4 // 2, 2 * (beat % 2) + half, t)
+                t_pass(bank, n, s, h, t)
             return bank
 
-        def read_t(on_vector, bank, beat, half):
-            out = t_grouped[beat][:, D * half : D * half + D].rearrange("p (q t) -> p q t", t=4)
+        def read_t(on_vector, bank, n, s, h):
+            out = t_grouped[n][s][:, D * h : D * h + D].rearrange("p (q t) -> p q t", t=4)
             copy(on_vector, out, bank[:].rearrange("p t q -> p q t"))
 
-        def quantise_t(beat):
-            term = (beat - 1) // 2
-            n, s = term // 2, term % 2
-            if beat < Z_LAG or term == TERMS - 1:
-                quantise(t_codes[n][s], t_scales[n][s], t_terms[term], 2 * ((beat - 1) % 2), 2)
-            elif beat % 2 == 0:
-                quantise(t_codes[n][s], t_scales[n][s], t_terms[term], 0, 4)
-
-        def z_bank(g):
+        def z_sum(out, g, cols):
             n, j = g // 4, g % 4
-            bank = psum.tile([P, D], F32, name="bank_z", tag="bank")
             for s in range(2):
                 nc.tensor.matmul_mx(
-                    out=bank[:],
+                    out=out,
                     lhsT=w_words[2 + s][:, 256 * j : 256 * j + 256].bitcast(FP4X4),
                     lhsT_scale=w_scales[2 + s][:, P * j : P * j + P],
-                    rhs=t_codes[n][s][:].bitcast(FP8X4),
-                    rhs_scale=t_scales[n][s][:],
+                    rhs=t_codes[n][s][:, cols].bitcast(FP8X4),
+                    rhs_scale=t_scales[n][s][:, cols],
                     start=(s == 0),
                     stop=(s == 1),
                 )
+
+        def z_bank(g):
+            bank = next_bank("bank_z", [P, D])
+            z_sum(bank[:], g, slice(0, D))
             return bank
 
         def add_c(bank, g):
             nc.vector.tensor_tensor(out=band(z, g), in0=bank[:], in1=c_sb[:, g % 4, :], op=ADD)
 
-        def store_y(g):
-            nc.sync.dma_start(out=out_0[g // 4, P * (g % 4) : P * (g % 4) + P, :], in_=band(y, g))
+        def store_y(g, count=1):
+            n, j = g // 4, g % 4
+            nc.sync.dma_start(
+                out=out_0[n, P * j : P * (j + count), :].rearrange("(j p) q -> p j q", p=P),
+                in_=band(y, g, count).rearrange("p (j q) -> p j q", j=count),
+            )
 
         def silu(g):
             nc.scalar.activation(band(y, g), band(z, g), SILU)
             store_y(g)
 
-        def round_y(g):
-            if g <= LAST_ON_GPSIMD:
-                nc.gpsimd.tensor_scalar(
-                    out=rounded[g].rearrange("p (u k e) -> p u k e", u=2, e=2),
-                    in0=band(y, g).rearrange("p (k u e) -> p u k e", u=2, e=2),
-                    scalar1=1.0,
-                    scalar2=-0.0,
-                    op0=MULT,
-                    op1=ADD,
-                )
-            else:
-                nc.vector.tensor_copy(out=rounded[g], in_=band(y, g))
+        def round_band(g, into):
+            nc.gpsimd.tensor_scalar(
+                out=into.rearrange("p (u k e) -> p u k e", u=2, e=2),
+                in0=band(y, g).rearrange("p (k u e) -> p u k e", u=2, e=2),
+                scalar1=1.0,
+                scalar2=-0.0,
+                op0=MULT,
+                op1=ADD,
+            )
+            words = into.bitcast(F32)
+            rounded[g] = [words[:, P * u : P * u + P] for u in range(2)]
 
-        def turn_y(g, count):
-            bank = psum.tile([P, count, 2, P], F32, name="bank_y", tag="bank")
+        def round_pair(g, into):
+            for j in range(2):
+                round_band(g + j, into[:, D * j : D * j + D])
+
+        def turn_y(g, count=2):
+            bank = next_bank("bank_y", [P, count, 2, P])
             for s in range(count):
-                words = rounded[g + s].bitcast(F32)
                 for u in range(2):
-                    in_ = words[:, P * u : P * u + P] if g + s <= LAST_ON_GPSIMD else words[:, u::2]
-                    nc.tensor.transpose(bank[:, s, u, :], in_, ident[:])
+                    nc.tensor.transpose(bank[:, s, u, :], rounded[g + s][u], ident[:])
             return bank
 
         def warm_up(count):
-            bank = psum.tile([P, 256], F32, name="bank_w", tag="bank")
+            bank = next_bank("bank_w", [P, D])
             for i in range(count):
                 nc.tensor.matmul_mx(
                     out=bank[:],
-                    lhsT=zero_codes[:, 0:64].bitcast(FP4X4),
+                    lhsT=zero_codes[:, 0:P].bitcast(FP8X4),
                     lhsT_scale=zero_scales[:, 0:P],
-                    rhs=zero_codes[:].bitcast(FP8X4),
+                    rhs=zero_codes[:].bitcast(FP4X4),
                     rhs_scale=zero_scales[:],
                     start=True,
                     stop=True,
                 )
 
+        V, S = True, False
         warm_up(WARM_FIRST)
+        turned = [turn_x(0, t, 1) for t in range(4)]
         for t in range(4):
-            read_words(t % 2 == 1, turn_x(0, t, 1), x_grouped[0], t, 1)
-            if t == 1:
-                quantise_x(0, 0, 1)
+            read_words(t == 1, turned[t], x_grouped[0], t, 1)
         warm_up(WARM_GAP)
-        opened = [psum.tile([P, 4, P], F32, name="bank_t", tag="bank") for h in range(4)]
-        for h in range(4):
-            t_pass(opened[h], 0, 0, h, 0)
-        quantise_x(0, 1, 1)
-        for h in range(4):
-            t_pass(opened[h], 0, 0, h, 1)
-        quantise_x(0, 2, 1)
-        quantise_x(0, 3, 1)
-        for h in range(4):
-            t_pass(opened[h], 0, 0, h, 2)
-            t_pass(opened[h], 0, 0, h, 3)
+        opened = [next_bank("bank_t", [P, 4, P]) for h in range(4)]
+        for t in range(4):
+            quantise_x(0, t, 1)
+            for h in range(4):
+                t_pass(opened[h], 0, 0, h, t)
 
-        turned_x, turned_y = [], None
-        for beat in range(BEATS + 1):
-            g = beat - Z_LAG
-            n_next = beat // 4 + 1
-            banks = None
-            if beat < BEATS:
-                banks = opened[2 * beat : 2 * beat + 2] if beat < 2 else [t_bank(beat, 0), t_bank(beat, 1)]
-            sums = z_bank(g) if g >= 0 else None
-            t_is_older = beat < 2
-            if t_is_older:
-                read_t(False, banks[0], beat, 0)
-            for half, bank in enumerate(turned_x):
-                read_words(False, bank, x_grouped[n_next], 2 * half, 2)
-            if turned_y:
-                read_y(False, turned_y, g - 6, 2)
-            turned_x, turned_y = [], None
-            if banks and not t_is_older:
-                read_t(False, banks[0], beat, 0)
-            if g >= 0:
-                quantise_t(beat)
-            if beat == 2:
+        STEPS = 2 * B
+        ON_V = [(1,3),(1,3),(1,3),(3,),(1,3),(3,),(1,3),(3,)]
+        SIL = [(0,0,0,0),(0,0,0,0),(0,0,1,0),(0,1,1,1),(0,0,1,0),(0,1,1,1),(0,0,1,0),(0,1,1,0)]
+        ROUNDS = [(0,0,0),(0,0,0),(0,0,0),(1,1,0),(2,0,0),(1,1,0),(2,0,0),(1,0,0)]
+        Z_LATE = (2,4,6)
+        QY0 = 7
+        turned_x, turned_y = [], []
+        added, done, free = [], [], []
+
+        def silus(count):
+            for i in range(min(count, len(added))):
+                done.append(added.pop(0))
+                silu(done[-1])
+
+        def rounds(count):
+            for i in range(min(count, len(done), len(free))):
+                round_band(done.pop(0), free.pop(0))
+
+        for step in range(STEPS):
+            n, s = step // 2, step % 2
+            g = 2 * (step - 2)
+            parts = [(s, h) for h in range(4)] if n < B - 1 else [(0, 2 * s), (0, 2 * s + 1), (1, 2 * s), (1, 2 * s + 1)]
+
+            def bank_of(i):
+                return opened[i] if step == 0 else t_bank(n, *parts[i])
+
+            def read(i, bank):
+                read_t(i in ON_V[step], bank, n, *parts[i])
+
+            ta, tb = bank_of(0), bank_of(1)
+            if step == STEPS - 1:
+                quantise_t(n, 0, 0, 2)
+                quantise_t(n, 1, 0, 2)
+                last_read = t_grouped[n][1]
+            elif step >= 1:
+                quantise_t((step - 1) // 2, (step - 1) % 2)
+                last_read = t_grouped[(step - 1) // 2][(step - 1) % 2]
+            for m, half, bank in turned_x:
+                read_words(S, bank, x_grouped[m], 2 * half, 2)
+            for first, bank in turned_y:
+                read_y(S, bank, first)
+            if step == 1:
                 quantise_x(1, 0, 2)
                 quantise_x(1, 2, 2)
-            elif beat % 4 == 2 and n_next < B:
-                quantise_x(n_next, 0, 4)
-            if g - 7 == 2:
-                quantise_y(0, 4)
-            elif g - 7 == 4:
-                quantise_y(4, 2)
-            if g >= 2:
-                round_y(g - 2)
-            if banks:
-                read_t(beat % 4 != SCALAR_BEAT, banks[1], beat, 1)
-            if g < 0 < beat:
-                quantise_t(beat)
+            if step in (3, 5):
+                quantise_x(n + 1, 0, 4)
+                last_read = x_grouped[n + 1]
+            if step >= 1:
+                free = [last_read[:, D * j : D * j + D] for j in range(2 if step == 7 else 4)]
+            rounds(ROUNDS[step][0])
+            late = step in Z_LATE
+            if g >= 0 and not late:
+                z0 = z_bank(g)
+            turned_x, turned_y = [], []
+            silus(SIL[step][0])
+            read(0, ta)
+            read(1, tb)
+            tc_, td = bank_of(2), bank_of(3)
+            if g >= 0 and not late:
+                add_c(z0, g)
+                added.append(g)
+            silus(SIL[step][1])
+            rounds(ROUNDS[step][1])
+            read(2, tc_)
+            if late:
+                z0 = z_bank(g)
             if g >= 0:
-                add_c(sums, g)
-            if g >= 1:
-                silu(g - 1)
-            if beat % 4 == 0 and n_next < B:
-                turned_x = [turn_x(n_next, 2 * half, 2) for half in range(2)]
-            if beat % 2 == 0 and g >= 5:
-                turned_y = turn_y(g - 5, 2)
+                z1 = z_bank(g + 1)
+            read(3, td)
+            if step == QY0:
+                quantise_y(0, 4)
+            if late:
+                add_c(z0, g)
+                added.append(g)
+            silus(SIL[step][2])
+            rounds(ROUNDS[step][2])
+            if g >= 0:
+                add_c(z1, g + 1)
+                added.append(g + 1)
+            if step == STEPS - 1:
+                quantise_t(n, 0, 2, 2)
+                quantise_t(n, 1, 2, 2)
+            silus(SIL[step][3])
+            if step in (0, 1, 3):
+                m = (step + 3) // 2
+                turned_x = [(m, half, turn_x(m, 2 * half, 2)) for half in range(2)]
+            if step == 5:
+                turned_y = [(first, turn_y(first)) for first in (0, 2)]
+        def z_half(g, count, h):
+            bank = next_bank("bank_z", [P, count, 256])
+            for j in range(count):
+                z_sum(bank[:, j, :], g + j, slice(256 * h, 256 * h + 256))
+            return bank
 
-        for g in (12, 14):
-            pair = g - 6
-            sums = [z_bank(g), z_bank(g + 1)]
-            read_y(False, turned_y, pair, 2)
-            add_c(sums[0], g)
-            if g + 1 < BANDS - 1:
-                add_c(sums[1], g + 1)
+        def half(tile, g, count, h):
+            return tile.rearrange("p (j q) -> p j q", j=4)[:, g % 4 : g % 4 + count, 256 * h : 256 * h + 256]
+
+        def add_half(bank, g, count, h):
+            nc.vector.tensor_tensor(
+                out=half(z[3][:], g, count, h), in0=bank[:], in1=c_sb[:, g % 4 : g % 4 + count, 256 * h : 256 * h + 256], op=ADD
+            )
+
+        def add_sorted(bank, h):
+            nc.vector.tensor_tensor(
+                out=band(z, 15).rearrange("p (t m) -> p t m", t=4)[:, :, 64 * h : 64 * h + 64],
+                in0=bank[:, 0, :].rearrange("p (m t) -> p t m", t=4),
+                in1=c_sb[:, 3, 256 * h : 256 * h + 256].rearrange("p (m t) -> p t m", t=4),
+                op=ADD,
+            )
+
+        def silu_half(g, count, h):
+            nc.scalar.activation(half(y[3][:], g, count, h), half(z[3][:], g, count, h), SILU)
+            nc.sync.dma_start(
+                out=out_0[3, P * (g % 4) : P * (g % 4 + count), 256 * h : 256 * h + 256].rearrange("(j p) q -> p j q", p=P),
+                in_=half(y[3][:], g, count, h),
+            )
+
+        last_rounded = sbuf("last_rounded", [P, 4, 2, P], F32)
+
+        def round_half(g, count, h, on_vector=True):
+            out = last_rounded[:, g % 4 : g % 4 + count, :, 64 * h : 64 * h + 64].bitcast(BF16).rearrange("p j u (k e) -> p j u k e", e=2)
+            in_ = half(y[3][:], g, count, h).rearrange("p j (k u e) -> p j u k e", u=2, e=2)
+            if on_vector:
+                nc.vector.tensor_copy(out=out, in_=in_)
             else:
-                last_z = band(z, g + 1)
-                nc.vector.tensor_tensor(
-                    out=last_z.rearrange("p (t m) -> p t m", t=4),
-                    in0=sums[1][:].rearrange("p (m t) -> p t m", t=4),
-                    in1=c_sb[:, 3, :].rearrange("p (m t) -> p t m", t=4),
-                    op=ADD,
-                )
-            silu(g - 1)
-            quantise_y(pair, 2)
-            silu(g)
-            if g == 12:
-                for done in range(10, LAST_ON_GPSIMD + 1):
-                    round_y(done)
-            turned_y = turn_y(pair + 2, 2)
-        last_bank = psum.tile([P, 4, P], F32, name="bank_d", tag="bank")
-        for t in range(4):
-            nc.tensor.transpose(last_bank[:, t, :], last_z[:, P * t : P * t + P], ident[:])
-        nc.scalar.activation(band(y, 15).rearrange("p (m t) -> p m t", t=4), last_z.rearrange("p (t m) -> p m t", t=4), SILU)
-        store_y(15)
-        round_y(13)
-        round_y(14)
-        bank_12 = turn_y(12, 2)
-        bank_14 = turn_y(14, 1)
-        nc.scalar.activation(
-            band(y_grouped, 15).rearrange("p (m t) -> p m t", t=4), last_bank[:].rearrange("p t m -> p m t"), SILU
-        )
-        read_y(True, turned_y, 10, 2)
-        read_y(False, bank_12, 12, 2)
-        read_y(False, bank_14, 14, 1)
-        for g in (10, 12, 14):
-            quantise_y(g, 2)
+                for j in range(count):
+                    nc.gpsimd.tensor_scalar(out=out[:, j], in0=in_[:, j], scalar1=1.0, scalar2=-0.0, op0=MULT, op1=ADD)
+            for j in range(count):
+                rounded[g + j] = [last_rounded[:, g % 4 + j, u, :] for u in range(2)]
+
+        free = [t_grouped[3][s][:, D * j : D * j + D] for s in (1, 0) for j in (2, 3)]
+        rounds(4)
+        ys = [turn_y(g) for g in (4, 6)]
+        e0 = z_half(12, 2, 0)
+        read_y(S, ys[0], 4)
+        read_y(S, ys[1], 6)
+        e1 = z_half(14, 2, 0)
+        silus(4)
+        rounds(4)
+        add_half(e0, 12, 2, 0)
+        l0 = z_half(12, 2, 1)
+        add_half(e1, 14, 2, 0)
+        l1, l2 = z_half(14, 1, 1), z_half(15, 1, 1)
+        silu_half(12, 2, 0)
+        silu_half(14, 2, 0)
+        add_half(l0, 12, 2, 1)
+        add_half(l1, 14, 1, 1)
+        add_half(l2, 15, 1, 1)
+        ys = [turn_y(g) for g in (8, 10)]
+        silu_half(12, 2, 1)
+        silu_half(14, 1, 1)
+        silu_half(15, 1, 1)
+        round_half(12, 2, 0)
+        round_half(14, 2, 0)
+        quantise_y(4, 2, 0)
+        round_half(12, 2, 1)
+        round_half(14, 1, 1)
+        quantise_y(6, 2, 4)
+        round_half(15, 1, 1)
+        banks = [turn_y(12), turn_y(14)]
+        read_y(S, ys[0], 8)
+        read_y(V, ys[1], 10)
+        read_y(S, banks[0], 12)
+        read_y(S, banks[1], 14)
+        quantise_y(8, 2, 0)
+        quantise_y(10, 2, 4)
+        quantise_y(12, 2)
+        quantise_y(14, 2)
+
+
         rows = out_2[0].rearrange("r (n m) -> n r m", n=B)
         for q in range(4):
             queue = nc.sync if q < 2 else nc.scalar

@@ -18,7 +18,7 @@ B, D = 4, 512
 P = 128
 FLOPS = 2 * 2 * 2 * B * D * D * D
 BANKS = 8
-WARM_FIRST, WARM_GAP = 2, 1
+WARM_FIRST, WARM_GAP = 4, 2
 
 
 def tile_ranktwokroneckersumlayer_x2_kernel(
@@ -40,15 +40,15 @@ def tile_ranktwokroneckersumlayer_x2_kernel(
             return psum.tile(shape, F32, name=kind, tag=f"bank{len(taken) % BANKS}")
 
         w_scales = [sbuf(f"w_scales{w}", [P, D], U8) for w in range(4)]
-        zeros = sbuf("zeros", [P, P], BF16)
+        zeros = sbuf("zeros", [P, 1024], BF16)
         zero_codes = sbuf("zero_codes", [P, 256], U32)
-        zero_scales = sbuf("zero_scales", [P, D], U8)
+        zero_scales = sbuf("zero_scales", [P, 256], U8)
+        table_in = sbuf("table_in", [P, 1], F32)
         ident = sbuf("ident", [P, P], F32)
-        nc.vector.memset(zeros[:].bitcast(I32), 0)
-        nc.vector.memset(zero_codes[:, 32:], 0)
-        nc.vector.memset(zero_scales[:, 32:].bitcast(I32), 0)
-        nc.vector.quantize_mx(out=zero_codes[:, 0:32].bitcast(FP8X4), scales=zero_scales[:, 0:32], in_=zeros[:])
         nc.vector.memset(w_scales[0][:].bitcast(I32), 0)
+        nc.vector.memset(zeros[:].bitcast(I32), 0)
+        nc.vector.memset(table_in[:], 0.0)
+        nc.vector.quantize_mx(out=zero_codes[:].bitcast(FP8X4), scales=zero_scales[:], in_=zeros[:])
         nc.vector.memset(ident[:], 0.0)
         make_identity(nc, ident[:], nomemset=True)
         for w in range(1, 4):
@@ -76,13 +76,12 @@ def tile_ranktwokroneckersumlayer_x2_kernel(
                     in_=scales_in[w][0, 4 * q : 4 * q + 4, :].bitcast(I32),
                 )
 
-        table_out = sbuf("table_out", [P, 1], F32)
-        nc.scalar.activation(table_out[:], zeros[:, 0:1], SILU)
         load_x(0, 0, 2)
-        load_x(0, 2, 1)
-        load_x(0, 3, 1)
+        load_x(0, 2, 2)
         load_words(0)
-        load_scales(0, nc.sync)
+        load_scales(0, nc.scalar)
+        table_out = sbuf("table_out", [P, 1], F32)
+        nc.scalar.activation(table_out[:], table_in[:], SILU)
         load_x(1, 0, 4)
         load_scales(1, nc.sync)
         load_words(1)
@@ -234,13 +233,13 @@ def tile_ranktwokroneckersumlayer_x2_kernel(
             return bank
 
         def warm_up(count):
-            bank = next_bank("bank_w", [P, D])
+            bank = next_bank("bank_w", [P, 256])
             for i in range(count):
                 nc.tensor.matmul_mx(
                     out=bank[:],
-                    lhsT=zero_codes[:, 0:P].bitcast(FP8X4),
+                    lhsT=zero_codes[:, 0:64].bitcast(FP4X4),
                     lhsT_scale=zero_scales[:, 0:P],
-                    rhs=zero_codes[:].bitcast(FP4X4),
+                    rhs=zero_codes[:].bitcast(FP8X4),
                     rhs_scale=zero_scales[:],
                     start=True,
                     stop=True,
@@ -248,22 +247,36 @@ def tile_ranktwokroneckersumlayer_x2_kernel(
 
         V, S = True, False
         warm_up(WARM_FIRST)
-        turned = [turn_x(0, t, 1) for t in range(4)]
         for t in range(4):
-            read_words(t == 1, turned[t], x_grouped[0], t, 1)
+            read_words(t % 2 == 1, turn_x(0, t, 1), x_grouped[0], t, 1)
+            if t == 1:
+                quantise_x(0, 0, 1)
         warm_up(WARM_GAP)
         opened = [next_bank("bank_t", [P, 4, P]) for h in range(4)]
-        for t in range(4):
-            quantise_x(0, t, 1)
-            for h in range(4):
-                t_pass(opened[h], 0, 0, h, t)
+        for h in range(4):
+            t_pass(opened[h], 0, 0, h, 0)
+        quantise_x(0, 1, 1)
+        for h in range(4):
+            t_pass(opened[h], 0, 0, h, 1)
+        quantise_x(0, 2, 1)
+        quantise_x(0, 3, 1)
+        for h in range(4):
+            t_pass(opened[h], 0, 0, h, 2)
+            t_pass(opened[h], 0, 0, h, 3)
 
         STEPS = 2 * B
-        ON_V = [(1,3),(1,3),(1,3),(3,),(1,3),(3,),(1,3),(3,)]
-        SIL = [(0,0,0,0),(0,0,0,0),(0,0,1,0),(0,1,1,1),(0,0,1,0),(0,1,1,1),(0,0,1,0),(0,1,1,0)]
-        ROUNDS = [(0,0,0),(0,0,0),(0,0,0),(1,1,0),(2,0,0),(1,1,0),(2,0,0),(1,0,0)]
-        Z_LATE = (2,4,6)
-        QY0 = 7
+        ON_V = 0
+        HALVES = 0
+        PLAN = [
+          "T0 T1 T2 T3 s0 v1 s2 v3 X1",
+          "T0 T1 T2 T3 x0 x1 qt1 qh0 qh1 s0 v1 s2 v3 X2",
+          "qt1 T0 T1 T2 T3 Z1 x0 x1 s1 s0 s2 v3 A1",
+          "qt1 qx2 T0 T1 Z0 T2 T3 Z1 s1 s0 S2 G2 A0 s2 v3 S1 A1 X3",
+          "qt1 T0 T1 Z0 T2 T3 Z1 G3 x1 x0 v1 s0 S2 G2 A0 s2 v3 S1 A1",
+          "qt1 qx3 T0 T1 Z0 T2 T3 Z1 G3 s1 s0 S2 G2 A0 s2 v3 S1 A1",
+          "qt1 T0 T1 Z0 T2 T3 Z1 G3 s1 s0 S2 G2 A0 s2 v3 S1 A1 Y0",
+          "qt1 T0 T1 Z0 T2 T3 Z1 G3 y1 y0 v1 s0 A0 s2 v3 S2 S1 A1"
+        ]
         turned_x, turned_y = [], []
         added, done, free = [], [], []
 
@@ -278,155 +291,136 @@ def tile_ranktwokroneckersumlayer_x2_kernel(
 
         for step in range(STEPS):
             n, s = step // 2, step % 2
-            g = 2 * (step - 2)
-            parts = [(s, h) for h in range(4)] if n < B - 1 else [(0, 2 * s), (0, 2 * s + 1), (1, 2 * s), (1, 2 * s + 1)]
+            g = 2 * step - 5
+            parts = [(s, h) for h in range(4)] if n < B - 1 or not HALVES else [(0, 2 * s), (0, 2 * s + 1), (1, 2 * s), (1, 2 * s + 1)]
+            banks = {}
+            for word in PLAN[step].split():
+                kind, i = word[:-1], int(word[-1])
+                if kind == "T":
+                    banks[word] = opened[i] if step == 0 else t_bank(n, *parts[i])
+                elif kind == "Z":
+                    banks[word] = z_bank(g + i)
+                elif kind in ("v", "s"):
+                    read_t(kind == "v", banks[f"T{i}"], n, *parts[i])
+                elif kind == "A":
+                    add_c(banks[f"Z{i}"], g + i)
+                elif kind == "S":
+                    silu(g + 1 - i)
+                elif kind == "G":
+                    round_band(g + 1 - i, free.pop(0))
+                elif kind in ("x", "vx"):
+                    read_words(kind == "vx", turned_x[i][2], x_grouped[turned_x[i][0]], 2 * i, 2)
+                elif kind in ("y", "vy"):
+                    read_y(kind == "vy", turned_y[i][1], turned_y[i][0])
+                elif kind == "qt":
+                    if HALVES and step == STEPS - 1:
+                        quantise_t(n, 0, 2 * i, 2)
+                        quantise_t(n, 1, 2 * i, 2)
+                        free = [t_grouped[n][1][:, D * j : D * j + D] for j in (2 * i, 2 * i + 1)]
+                    else:
+                        term = step - i
+                        quantise_t(term // 2, term % 2)
+                        free = [t_grouped[term // 2][term % 2][:, D * j : D * j + D] for j in range(4)]
+                elif kind == "qx":
+                    quantise_x(i, 0, 4)
+                    free = [x_grouped[i][:, D * j : D * j + D] for j in range(4)]
+                elif kind == "qh":
+                    quantise_x(1, 2 * i, 2)
+                elif kind == "qy":
+                    quantise_y(4 * i, 4)
+                    free = [y_grouped[i][:, D * j : D * j + D] for j in range(4)]
+                elif kind == "X":
+                    turned_x = [(i, half, turn_x(i, 2 * half, 2)) for half in range(2)]
+                elif kind == "Y":
+                    turned_y = [(first, turn_y(first)) for first in (2 * i, 2 * i + 2)]
 
-            def bank_of(i):
-                return opened[i] if step == 0 else t_bank(n, *parts[i])
+        last_rounded = sbuf("last_rounded", [P, 4 * D], BF16)
 
-            def read(i, bank):
-                read_t(i in ON_V[step], bank, n, *parts[i])
-
-            ta, tb = bank_of(0), bank_of(1)
-            if step == STEPS - 1:
-                quantise_t(n, 0, 0, 2)
-                quantise_t(n, 1, 0, 2)
-                last_read = t_grouped[n][1]
-            elif step >= 1:
-                quantise_t((step - 1) // 2, (step - 1) % 2)
-                last_read = t_grouped[(step - 1) // 2][(step - 1) % 2]
-            for m, half, bank in turned_x:
-                read_words(S, bank, x_grouped[m], 2 * half, 2)
-            for first, bank in turned_y:
-                read_y(S, bank, first)
-            if step == 1:
-                quantise_x(1, 0, 2)
-                quantise_x(1, 2, 2)
-            if step in (3, 5):
-                quantise_x(n + 1, 0, 4)
-                last_read = x_grouped[n + 1]
-            if step >= 1:
-                free = [last_read[:, D * j : D * j + D] for j in range(2 if step == 7 else 4)]
-            rounds(ROUNDS[step][0])
-            late = step in Z_LATE
-            if g >= 0 and not late:
-                z0 = z_bank(g)
-            turned_x, turned_y = [], []
-            silus(SIL[step][0])
-            read(0, ta)
-            read(1, tb)
-            tc_, td = bank_of(2), bank_of(3)
-            if g >= 0 and not late:
-                add_c(z0, g)
-                added.append(g)
-            silus(SIL[step][1])
-            rounds(ROUNDS[step][1])
-            read(2, tc_)
-            if late:
-                z0 = z_bank(g)
-            if g >= 0:
-                z1 = z_bank(g + 1)
-            read(3, td)
-            if step == QY0:
-                quantise_y(0, 4)
-            if late:
-                add_c(z0, g)
-                added.append(g)
-            silus(SIL[step][2])
-            rounds(ROUNDS[step][2])
-            if g >= 0:
-                add_c(z1, g + 1)
-                added.append(g + 1)
-            if step == STEPS - 1:
-                quantise_t(n, 0, 2, 2)
-                quantise_t(n, 1, 2, 2)
-            silus(SIL[step][3])
-            if step in (0, 1, 3):
-                m = (step + 3) // 2
-                turned_x = [(m, half, turn_x(m, 2 * half, 2)) for half in range(2)]
-            if step == 5:
-                turned_y = [(first, turn_y(first)) for first in (0, 2)]
-        def z_half(g, count, h):
-            bank = next_bank("bank_z", [P, count, 256])
+        def round_v(g, count):
+            out = last_rounded[:, D * (g - 12) : D * (g - 12 + count)]
+            nc.vector.tensor_copy(out=out, in_=band(y, g, count))
             for j in range(count):
-                z_sum(bank[:, j, :], g + j, slice(256 * h, 256 * h + 256))
-            return bank
+                words = out[:, D * j : D * j + D].bitcast(F32)
+                rounded[g + j] = [words[:, u::2] for u in range(2)]
 
-        def half(tile, g, count, h):
-            return tile.rearrange("p (j q) -> p j q", j=4)[:, g % 4 : g % 4 + count, 256 * h : 256 * h + 256]
-
-        def add_half(bank, g, count, h):
+        def add_sorted(bank):
             nc.vector.tensor_tensor(
-                out=half(z[3][:], g, count, h), in0=bank[:], in1=c_sb[:, g % 4 : g % 4 + count, 256 * h : 256 * h + 256], op=ADD
-            )
-
-        def add_sorted(bank, h):
-            nc.vector.tensor_tensor(
-                out=band(z, 15).rearrange("p (t m) -> p t m", t=4)[:, :, 64 * h : 64 * h + 64],
-                in0=bank[:, 0, :].rearrange("p (m t) -> p t m", t=4),
-                in1=c_sb[:, 3, 256 * h : 256 * h + 256].rearrange("p (m t) -> p t m", t=4),
+                out=band(z, 15).rearrange("p (t m) -> p t m", t=4),
+                in0=bank[:].rearrange("p (m t) -> p t m", t=4),
+                in1=c_sb[:, 3, :].rearrange("p (m t) -> p t m", t=4),
                 op=ADD,
             )
 
-        def silu_half(g, count, h):
-            nc.scalar.activation(half(y[3][:], g, count, h), half(z[3][:], g, count, h), SILU)
-            nc.sync.dma_start(
-                out=out_0[3, P * (g % 4) : P * (g % 4 + count), 256 * h : 256 * h + 256].rearrange("(j p) q -> p j q", p=P),
-                in_=half(y[3][:], g, count, h),
+        def turn_z():
+            bank = next_bank("bank_d", [P, 4, P])
+            for t in range(4):
+                nc.tensor.transpose(bank[:, t, :], band(z, 15)[:, P * t : P * t + P], ident[:])
+            return bank
+
+        def silu_sorted():
+            nc.scalar.activation(
+                band(y, 15).rearrange("p (m t) -> p m t", t=4), band(z, 15).rearrange("p (t m) -> p m t", t=4), SILU
+            )
+            store_y(15)
+
+        def silu_turned(bank):
+            nc.scalar.activation(
+                band(y_grouped, 15).rearrange("p (m t) -> p m t", t=4), bank[:].rearrange("p t m -> p m t"), SILU
             )
 
-        last_rounded = sbuf("last_rounded", [P, 4, 2, P], F32)
-
-        def round_half(g, count, h, on_vector=True):
-            out = last_rounded[:, g % 4 : g % 4 + count, :, 64 * h : 64 * h + 64].bitcast(BF16).rearrange("p j u (k e) -> p j u k e", e=2)
-            in_ = half(y[3][:], g, count, h).rearrange("p j (k u e) -> p j u k e", u=2, e=2)
-            if on_vector:
-                nc.vector.tensor_copy(out=out, in_=in_)
-            else:
-                for j in range(count):
-                    nc.gpsimd.tensor_scalar(out=out[:, j], in0=in_[:, j], scalar1=1.0, scalar2=-0.0, op0=MULT, op1=ADD)
-            for j in range(count):
-                rounded[g + j] = [last_rounded[:, g % 4 + j, u, :] for u in range(2)]
-
-        free = [t_grouped[3][s][:, D * j : D * j + D] for s in (1, 0) for j in (2, 3)]
-        rounds(4)
-        ys = [turn_y(g) for g in (4, 6)]
-        e0 = z_half(12, 2, 0)
-        read_y(S, ys[0], 4)
-        read_y(S, ys[1], 6)
-        e1 = z_half(14, 2, 0)
-        silus(4)
-        rounds(4)
-        add_half(e0, 12, 2, 0)
-        l0 = z_half(12, 2, 1)
-        add_half(e1, 14, 2, 0)
-        l1, l2 = z_half(14, 1, 1), z_half(15, 1, 1)
-        silu_half(12, 2, 0)
-        silu_half(14, 2, 0)
-        add_half(l0, 12, 2, 1)
-        add_half(l1, 14, 1, 1)
-        add_half(l2, 15, 1, 1)
-        ys = [turn_y(g) for g in (8, 10)]
-        silu_half(12, 2, 1)
-        silu_half(14, 1, 1)
-        silu_half(15, 1, 1)
-        round_half(12, 2, 0)
-        round_half(14, 2, 0)
-        quantise_y(4, 2, 0)
-        round_half(12, 2, 1)
-        round_half(14, 1, 1)
-        quantise_y(6, 2, 4)
-        round_half(15, 1, 1)
-        banks = [turn_y(12), turn_y(14)]
-        read_y(S, ys[0], 8)
-        read_y(V, ys[1], 10)
-        read_y(S, banks[0], 12)
-        read_y(S, banks[1], 14)
-        quantise_y(8, 2, 0)
-        quantise_y(10, 2, 4)
+        bk = {}
+        for first, bank in turned_y:
+            bk[f"Y{first}"] = bank
+        bk["Y4"] = turn_y(4, 2)
+        bk["Y6"] = turn_y(6, 2)
+        quantise_t(3, 1)
+        free = [t_grouped[3][1][:, D * j : D * j + D] for j in range(4)]
+        round_band(8, free.pop(0))
+        round_band(9, free.pop(0))
+        bk["Z11"] = z_bank(11)
+        silu(10)
+        round_band(10, free.pop(0))
+        add_c(bk["Z11"], 11)
+        bk["Z12"] = z_bank(12)
+        bk["Z13"] = z_bank(13)
+        read_y(V, bk["Y4"], 4, 2)
+        add_c(bk["Z12"], 12)
+        read_y(S, bk["Y6"], 6, 2)
+        silu(11)
+        round_band(11, free.pop(0))
+        add_c(bk["Z13"], 13)
+        bk["Z14"] = z_bank(14)
+        bk["Z15"] = z_bank(15)
+        silu(12)
+        silu(13)
+        add_c(bk["Z14"], 14)
+        add_sorted(bk["Z15"])
+        bk["Y8"] = turn_y(8, 2)
+        bk["Y10"] = turn_y(10, 2)
+        bk["D"] = turn_z()
+        silu(14)
+        silu_sorted()
+        round_v(12, 2)
+        quantise_y(0, 4)
+        free = [y_all[:, D * j : D * j + D] for j in range(0, 4)]
+        round_v(14, 1)
+        silu_turned(bk["D"])
+        bk["Y12"] = turn_y(12, 2)
+        bk["Y14"] = turn_y(14, 1)
+        quantise_y(4, 4)
+        free = [y_all[:, D * j : D * j + D] for j in range(4, 8)]
+        read_y(S, bk["Y8"], 8, 2)
+        read_y(S, bk["Y10"], 10, 2)
+        read_y(S, bk["Y12"], 12, 2)
+        read_y(S, bk["Y14"], 14, 1)
+        quantise_y(8, 2)
+        free = [y_all[:, D * j : D * j + D] for j in range(8, 10)]
+        quantise_y(10, 2)
+        free = [y_all[:, D * j : D * j + D] for j in range(10, 12)]
         quantise_y(12, 2)
+        free = [y_all[:, D * j : D * j + D] for j in range(12, 14)]
         quantise_y(14, 2)
-
+        free = [y_all[:, D * j : D * j + D] for j in range(14, 16)]
 
         rows = out_2[0].rearrange("r (n m) -> n r m", n=B)
         for q in range(4):

@@ -86,10 +86,10 @@ def tile_ranktwokroneckersumlayer_x2_kernel(
         load_scales(1, nc.sync)
         load_words(1)
         load_x(2, 0, 4)
-        load_scales(2, nc.sync)
+        load_scales(2, nc.gpsimd)
         load_words(2)
-        load_scales(3, nc.sync)
         load_words(3)
+        load_scales(3, nc.sync)
         nc.sync.dma_start(out=c_sb[:], in_=c.rearrange("(j p) q -> p j q", p=P))
         load_x(3, 0, 4)
 

@@ -270,12 +270,12 @@ def tile_ranktwokroneckersumlayer_x2_kernel(
         PLAN = [
           "T0 T1 T2 T3 s0 v1 s2 v3 X1",
           "T0 T1 T2 T3 x0 x1 qt1 qh0 qh1 s0 v1 s2 v3 X2",
-          "qt1 T0 T1 T2 T3 Z1 x0 x1 s1 s0 s2 v3 A1",
+          "qt1 T0 T1 T2 T3 Z1 x0 x1 v1 s0 s2 v3 A1",
           "qt1 qx2 T0 T1 Z0 T2 T3 Z1 s1 s0 S2 G2 A0 s2 v3 S1 A1 X3",
           "qt1 T0 T1 Z0 T2 T3 Z1 G3 x1 x0 v1 s0 S2 G2 A0 s2 v3 S1 A1",
           "qt1 qx3 T0 T1 Z0 T2 T3 Z1 G3 s1 s0 S2 G2 A0 s2 v3 S1 A1",
-          "qt1 T0 T1 Z0 T2 T3 Z1 G3 s1 s0 S2 G2 A0 s2 v3 S1 A1 Y0",
-          "qt1 T0 T1 Z0 T2 T3 Z1 G3 y1 y0 v1 s0 A0 s2 v3 S2 S1 A1"
+          "qt1 T0 T1 Z0 T2 T3 Z1 G3 s1 s0 S2 A0 s2 v3 S1 A1 Y0",
+          "qt1 T0 T1 Z0 T2 T3 Z1 G4 G3 y1 y0 v1 s0 A0 s2 v3 S2 S1 A1"
         ]
         turned_x, turned_y = [], []
         added, done, free = [], [], []
@@ -337,7 +337,7 @@ def tile_ranktwokroneckersumlayer_x2_kernel(
         last_rounded = sbuf("last_rounded", [P, 4 * D], BF16)
 
         def round_v(g, count):
-            out = last_rounded[:, D * (g - 12) : D * (g - 12 + count)]
+            out = last_rounded[:, D * (g % 4) : D * (g % 4 + count)]
             nc.vector.tensor_copy(out=out, in_=band(y, g, count))
             for j in range(count):
                 words = out[:, D * j : D * j + D].bitcast(F32)
@@ -375,6 +375,8 @@ def tile_ranktwokroneckersumlayer_x2_kernel(
         bk["Y6"] = turn_y(6, 2)
         quantise_t(3, 1)
         free = [t_grouped[3][1][:, D * j : D * j + D] for j in range(4)]
+        quantise_y(0, 4)
+        free = [y_all[:, D * j : D * j + D] for j in range(0, 4)]
         round_band(8, free.pop(0))
         round_band(9, free.pop(0))
         bk["Z11"] = z_bank(11)
@@ -383,11 +385,11 @@ def tile_ranktwokroneckersumlayer_x2_kernel(
         add_c(bk["Z11"], 11)
         bk["Z12"] = z_bank(12)
         bk["Z13"] = z_bank(13)
-        read_y(V, bk["Y4"], 4, 2)
         add_c(bk["Z12"], 12)
-        read_y(S, bk["Y6"], 6, 2)
+        read_y(S, bk["Y4"], 4, 2)
         silu(11)
         round_band(11, free.pop(0))
+        read_y(S, bk["Y6"], 6, 2)
         add_c(bk["Z13"], 13)
         bk["Z14"] = z_bank(14)
         bk["Z15"] = z_bank(15)
@@ -396,25 +398,23 @@ def tile_ranktwokroneckersumlayer_x2_kernel(
         add_c(bk["Z14"], 14)
         add_sorted(bk["Z15"])
         bk["Y8"] = turn_y(8, 2)
-        bk["Y10"] = turn_y(10, 2)
         bk["D"] = turn_z()
+        bk["Y10"] = turn_y(10, 2)
         silu(14)
         silu_sorted()
+        read_y(V, bk["Y8"], 8, 2)
         round_v(12, 2)
-        quantise_y(0, 4)
-        free = [y_all[:, D * j : D * j + D] for j in range(0, 4)]
+        quantise_y(4, 4)
+        free = [y_all[:, D * j : D * j + D] for j in range(4, 8)]
         round_v(14, 1)
         silu_turned(bk["D"])
         bk["Y12"] = turn_y(12, 2)
         bk["Y14"] = turn_y(14, 1)
-        quantise_y(4, 4)
-        free = [y_all[:, D * j : D * j + D] for j in range(4, 8)]
-        read_y(S, bk["Y8"], 8, 2)
+        quantise_y(8, 2)
+        free = [y_all[:, D * j : D * j + D] for j in range(8, 10)]
         read_y(S, bk["Y10"], 10, 2)
         read_y(S, bk["Y12"], 12, 2)
         read_y(S, bk["Y14"], 14, 1)
-        quantise_y(8, 2)
-        free = [y_all[:, D * j : D * j + D] for j in range(8, 10)]
         quantise_y(10, 2)
         free = [y_all[:, D * j : D * j + D] for j in range(10, 12)]
         quantise_y(12, 2)

@@ -17,7 +17,13 @@ MULT = mybir.AluOpType.mult
 B, D = 4, 512
 P = 128
 FLOPS = 2 * 2 * 2 * B * D * D * D
+
 BANKS = 8
+STEPS = 2 * B
+BANDS = 4 * B
+Z_LAG = 5
+X_TURNED = {1: 0, 2: 1, 3: 3}
+Y_TURNED = 6
 WARM_FIRST, WARM_GAP = 4, 2
 
 
@@ -125,16 +131,13 @@ def tile_ranktwokroneckersumlayer_x2_kernel(
         def quantise_x(n, first, count):
             quantise(x_codes[n], x_scales[n], x_grouped[n], first, count)
 
-        def quantise_t(n, s, first=0, count=4):
-            quantise(t_codes[n][s], t_scales[n][s], t_grouped[n][s], first, count)
+        def quantise_t(term):
+            n, s = term // 2, term % 2
+            quantise(t_codes[n][s], t_scales[n][s], t_grouped[n][s], 0, 4)
 
-        def quantise_y(g, count, stored=None):
+        def quantise_y(g, count):
             n = g // 4
             quantise(y_codes[:, D * n : D * n + D], y_scales[4 * n :, :], y_grouped[n], g % 4, count)
-            if stored != 0:
-                store_codes(g + count - (stored or count), stored or count)
-
-        def store_codes(g, count):
             cols = slice(P * g, P * (g + count))
             nc.sync.dma_start(out=out_1[0, :, cols, :].rearrange("p m t -> p (m t)").bitcast(I32), in_=y_codes[:, cols])
 
@@ -177,39 +180,38 @@ def tile_ranktwokroneckersumlayer_x2_kernel(
             out = t_grouped[n][s][:, D * h : D * h + D].rearrange("p (q t) -> p q t", t=4)
             copy(on_vector, out, bank[:].rearrange("p t q -> p q t"))
 
-        def z_sum(out, g, cols):
+        def z_bank(g):
             n, j = g // 4, g % 4
+            bank = next_bank("bank_z", [P, D])
             for s in range(2):
                 nc.tensor.matmul_mx(
-                    out=out,
+                    out=bank[:],
                     lhsT=w_words[2 + s][:, 256 * j : 256 * j + 256].bitcast(FP4X4),
                     lhsT_scale=w_scales[2 + s][:, P * j : P * j + P],
-                    rhs=t_codes[n][s][:, cols].bitcast(FP8X4),
-                    rhs_scale=t_scales[n][s][:, cols],
+                    rhs=t_codes[n][s][:].bitcast(FP8X4),
+                    rhs_scale=t_scales[n][s][:],
                     start=(s == 0),
                     stop=(s == 1),
                 )
-
-        def z_bank(g):
-            bank = next_bank("bank_z", [P, D])
-            z_sum(bank[:], g, slice(0, D))
             return bank
 
         def add_c(bank, g):
             nc.vector.tensor_tensor(out=band(z, g), in0=bank[:], in1=c_sb[:, g % 4, :], op=ADD)
 
-        def store_y(g, count=1):
-            n, j = g // 4, g % 4
-            nc.sync.dma_start(
-                out=out_0[n, P * j : P * (j + count), :].rearrange("(j p) q -> p j q", p=P),
-                in_=band(y, g, count).rearrange("p (j q) -> p j q", j=count),
-            )
+        def store_y(g):
+            nc.sync.dma_start(out=out_0[g // 4, P * (g % 4) : P * (g % 4 + 1), :], in_=band(y, g))
 
         def silu(g):
             nc.scalar.activation(band(y, g), band(z, g), SILU)
             store_y(g)
 
-        def round_band(g, into):
+        spent = []
+
+        def spend(grouped):
+            spent[:] = [grouped[:, D * j : D * j + D] for j in range(4)]
+
+        def round_on_gpsimd(g):
+            into = spent.pop(0)
             nc.gpsimd.tensor_scalar(
                 out=into.rearrange("p (u k e) -> p u k e", u=2, e=2),
                 in0=band(y, g).rearrange("p (k u e) -> p u k e", u=2, e=2),
@@ -221,9 +223,14 @@ def tile_ranktwokroneckersumlayer_x2_kernel(
             words = into.bitcast(F32)
             rounded[g] = [words[:, P * u : P * u + P] for u in range(2)]
 
-        def round_pair(g, into):
-            for j in range(2):
-                round_band(g + j, into[:, D * j : D * j + D])
+        last_rounded = sbuf("last_rounded", [P, 3 * D], BF16)
+
+        def round_on_vector(g, count):
+            out = last_rounded[:, D * (g % 4) : D * (g % 4 + count)]
+            nc.vector.tensor_copy(out=out, in_=band(y, g, count))
+            for j in range(count):
+                words = out[:, D * j : D * j + D].bitcast(F32)
+                rounded[g + j] = [words[:, u::2] for u in range(2)]
 
         def turn_y(g, count=2):
             bank = next_bank("bank_y", [P, count, 2, P])
@@ -245,7 +252,8 @@ def tile_ranktwokroneckersumlayer_x2_kernel(
                     stop=True,
                 )
 
-        V, S = True, False
+        VECTOR, SCALAR = True, False
+
         warm_up(WARM_FIRST)
         for t in range(4):
             read_words(t % 2 == 1, turn_x(0, t, 1), x_grouped[0], t, 1)
@@ -264,164 +272,114 @@ def tile_ranktwokroneckersumlayer_x2_kernel(
             t_pass(opened[h], 0, 0, h, 2)
             t_pass(opened[h], 0, 0, h, 3)
 
-        STEPS = 2 * B
-        ON_V = 0
-        HALVES = 0
-        PLAN = [
-          "T0 T1 T2 T3 s0 v1 s2 v3 X1",
-          "T0 T1 T2 T3 x0 x1 qt1 qh0 qh1 s0 v1 s2 v3 X2",
-          "qt1 T0 T1 T2 T3 Z1 x0 x1 v1 s0 s2 v3 A1",
-          "qt1 qx2 T0 T1 Z0 T2 T3 Z1 s1 s0 S2 G2 A0 s2 v3 S1 A1 X3",
-          "qt1 T0 T1 Z0 T2 T3 Z1 G3 x1 x0 v1 s0 S2 G2 A0 s2 v3 S1 A1",
-          "qt1 qx3 T0 T1 Z0 T2 T3 Z1 G3 s1 s0 S2 G2 A0 s2 v3 S1 A1",
-          "qt1 T0 T1 Z0 T2 T3 Z1 G3 s1 s0 S2 A0 s2 v3 S1 A1 Y0",
-          "qt1 T0 T1 Z0 T2 T3 Z1 G4 G3 y1 y0 v1 s0 A0 s2 v3 S2 S1 A1"
-        ]
-        turned_x, turned_y = [], []
-        added, done, free = [], [], []
-
-        def silus(count):
-            for i in range(min(count, len(added))):
-                done.append(added.pop(0))
-                silu(done[-1])
-
-        def rounds(count):
-            for i in range(min(count, len(done), len(free))):
-                round_band(done.pop(0), free.pop(0))
-
+        turned_x, turned_y, waiting = [], [], []
         for step in range(STEPS):
             n, s = step // 2, step % 2
-            g = 2 * step - 5
-            parts = [(s, h) for h in range(4)] if n < B - 1 or not HALVES else [(0, 2 * s), (0, 2 * s + 1), (1, 2 * s), (1, 2 * s + 1)]
-            banks = {}
-            for word in PLAN[step].split():
-                kind, i = word[:-1], int(word[-1])
-                if kind == "T":
-                    banks[word] = opened[i] if step == 0 else t_bank(n, *parts[i])
-                elif kind == "Z":
-                    banks[word] = z_bank(g + i)
-                elif kind in ("v", "s"):
-                    read_t(kind == "v", banks[f"T{i}"], n, *parts[i])
-                elif kind == "A":
-                    add_c(banks[f"Z{i}"], g + i)
-                elif kind == "S":
-                    silu(g + 1 - i)
-                elif kind == "G":
-                    round_band(g + 1 - i, free.pop(0))
-                elif kind in ("x", "vx"):
-                    read_words(kind == "vx", turned_x[i][2], x_grouped[turned_x[i][0]], 2 * i, 2)
-                elif kind in ("y", "vy"):
-                    read_y(kind == "vy", turned_y[i][1], turned_y[i][0])
-                elif kind == "qt":
-                    if HALVES and step == STEPS - 1:
-                        quantise_t(n, 0, 2 * i, 2)
-                        quantise_t(n, 1, 2 * i, 2)
-                        free = [t_grouped[n][1][:, D * j : D * j + D] for j in (2 * i, 2 * i + 1)]
-                    else:
-                        term = step - i
-                        quantise_t(term // 2, term % 2)
-                        free = [t_grouped[term // 2][term % 2][:, D * j : D * j + D] for j in range(4)]
-                elif kind == "qx":
-                    quantise_x(i, 0, 4)
-                    free = [x_grouped[i][:, D * j : D * j + D] for j in range(4)]
-                elif kind == "qh":
-                    quantise_x(1, 2 * i, 2)
-                elif kind == "qy":
-                    quantise_y(4 * i, 4)
-                    free = [y_grouped[i][:, D * j : D * j + D] for j in range(4)]
-                elif kind == "X":
-                    turned_x = [(i, half, turn_x(i, 2 * half, 2)) for half in range(2)]
-                elif kind == "Y":
-                    turned_y = [(first, turn_y(first)) for first in (2 * i, 2 * i + 2)]
+            g = 2 * step - Z_LAG
+            last = step == STEPS - 1
+            if step >= 2:
+                quantise_t(step - 1)
+                spend(t_grouped[(step - 1) // 2][(step - 1) % 2])
+            if step >= 3 and step - 2 == X_TURNED.get(n + 1):
+                quantise_x(n + 1, 0, 4)
+                spend(x_grouped[n + 1])
+            banks, sums = [], {}
+            for half in range(2):
+                banks += opened[2 * half : 2 * half + 2] if step == 0 else [t_bank(n, s, 2 * half + h) for h in range(2)]
+                if g + half >= 0:
+                    sums[g + half] = z_bank(g + half)
+            while waiting:
+                round_on_gpsimd(waiting.pop(0))
+            ahead = g >= 0
+            for m, half, bank in turned_x[::-1] if ahead else turned_x:
+                read_words(SCALAR, bank, x_grouped[m], 2 * half, 2)
+            for first, bank in turned_y[::-1]:
+                read_y(SCALAR, bank, first)
+            if step == 1:
+                quantise_t(0)
+                quantise_x(1, 0, 2)
+                quantise_x(1, 2, 2)
+            second_on_vector = step < 2 or (ahead and bool(turned_x or turned_y))
+            turned_x, turned_y = [], []
+            if step < 2:
+                read_t(SCALAR, banks[0], n, s, 0)
+            read_t(second_on_vector, banks[1], n, s, 1)
+            if step >= 2:
+                read_t(SCALAR, banks[0], n, s, 0)
+            if g >= 1 and not last:
+                silu(g - 1)
+                if step < Y_TURNED:
+                    round_on_gpsimd(g - 1)
+                else:
+                    waiting.append(g - 1)
+            if g >= 0:
+                add_c(sums[g], g)
+            read_t(SCALAR, banks[2], n, s, 2)
+            read_t(VECTOR, banks[3], n, s, 3)
+            if last:
+                silu(g - 1)
+                waiting.append(g - 1)
+            if g >= 0:
+                silu(g)
+                waiting.append(g)
+            if g + 1 >= 0:
+                add_c(sums[g + 1], g + 1)
+            for m in X_TURNED:
+                if X_TURNED[m] == step:
+                    turned_x = [(m, half, turn_x(m, 2 * half, 2)) for half in range(2)]
+            if step == Y_TURNED:
+                turned_y = [(first, turn_y(first)) for first in (0, 2)]
 
-        last_rounded = sbuf("last_rounded", [P, 4 * D], BF16)
-
-        def round_v(g, count):
-            out = last_rounded[:, D * (g % 4) : D * (g % 4 + count)]
-            nc.vector.tensor_copy(out=out, in_=band(y, g, count))
-            for j in range(count):
-                words = out[:, D * j : D * j + D].bitcast(F32)
-                rounded[g + j] = [words[:, u::2] for u in range(2)]
-
-        def add_sorted(bank):
-            nc.vector.tensor_tensor(
-                out=band(z, 15).rearrange("p (t m) -> p t m", t=4),
-                in0=bank[:].rearrange("p (m t) -> p t m", t=4),
-                in1=c_sb[:, 3, :].rearrange("p (m t) -> p t m", t=4),
-                op=ADD,
-            )
-
-        def turn_z():
-            bank = next_bank("bank_d", [P, 4, P])
-            for t in range(4):
-                nc.tensor.transpose(bank[:, t, :], band(z, 15)[:, P * t : P * t + P], ident[:])
-            return bank
-
-        def silu_sorted():
-            nc.scalar.activation(
-                band(y, 15).rearrange("p (m t) -> p m t", t=4), band(z, 15).rearrange("p (t m) -> p m t", t=4), SILU
-            )
-            store_y(15)
-
-        def silu_turned(bank):
-            nc.scalar.activation(
-                band(y_grouped, 15).rearrange("p (m t) -> p m t", t=4), bank[:].rearrange("p t m -> p m t"), SILU
-            )
-
-        bk = {}
-        for first, bank in turned_y:
-            bk[f"Y{first}"] = bank
-        bk["Y4"] = turn_y(4, 2)
-        bk["Y6"] = turn_y(6, 2)
-        quantise_t(3, 1)
-        free = [t_grouped[3][1][:, D * j : D * j + D] for j in range(4)]
+        bank_4, bank_6 = turn_y(4), turn_y(6)
+        quantise_t(STEPS - 1)
         quantise_y(0, 4)
-        free = [y_all[:, D * j : D * j + D] for j in range(0, 4)]
-        round_band(8, free.pop(0))
-        round_band(9, free.pop(0))
-        bk["Z11"] = z_bank(11)
+        spend(y_grouped[0])
+        while waiting:
+            round_on_gpsimd(waiting.pop(0))
+        sums = {11: z_bank(11)}
         silu(10)
-        round_band(10, free.pop(0))
-        add_c(bk["Z11"], 11)
-        bk["Z12"] = z_bank(12)
-        bk["Z13"] = z_bank(13)
-        add_c(bk["Z12"], 12)
-        read_y(S, bk["Y4"], 4, 2)
+        round_on_gpsimd(10)
+        add_c(sums[11], 11)
+        sums = {g: z_bank(g) for g in (12, 13)}
+        add_c(sums[12], 12)
+        read_y(SCALAR, bank_6, 6)
+        read_y(SCALAR, bank_4, 4)
         silu(11)
-        round_band(11, free.pop(0))
-        read_y(S, bk["Y6"], 6, 2)
-        add_c(bk["Z13"], 13)
-        bk["Z14"] = z_bank(14)
-        bk["Z15"] = z_bank(15)
+        round_on_gpsimd(11)
+        add_c(sums[13], 13)
+        sums = {g: z_bank(g) for g in (14, 15)}
         silu(12)
         silu(13)
-        add_c(bk["Z14"], 14)
-        add_sorted(bk["Z15"])
-        bk["Y8"] = turn_y(8, 2)
-        bk["D"] = turn_z()
-        bk["Y10"] = turn_y(10, 2)
+        add_c(sums[14], 14)
+        last_z = band(z, BANDS - 1)
+        nc.vector.tensor_tensor(
+            out=last_z.rearrange("p (t m) -> p t m", t=4),
+            in0=sums[15][:].rearrange("p (m t) -> p t m", t=4),
+            in1=c_sb[:, 3, :].rearrange("p (m t) -> p t m", t=4),
+            op=ADD,
+        )
+        bank_8 = turn_y(8)
+        last_bank = next_bank("bank_d", [P, 4, P])
+        for t in range(4):
+            nc.tensor.transpose(last_bank[:, t, :], last_z[:, P * t : P * t + P], ident[:])
+        bank_10 = turn_y(10)
         silu(14)
-        silu_sorted()
-        read_y(V, bk["Y8"], 8, 2)
-        round_v(12, 2)
+        nc.scalar.activation(band(y, 15).rearrange("p (m t) -> p m t", t=4), last_z.rearrange("p (t m) -> p m t", t=4), SILU)
+        store_y(15)
+        read_y(VECTOR, bank_8, 8)
+        round_on_vector(12, 2)
         quantise_y(4, 4)
-        free = [y_all[:, D * j : D * j + D] for j in range(4, 8)]
-        round_v(14, 1)
-        silu_turned(bk["D"])
-        bk["Y12"] = turn_y(12, 2)
-        bk["Y14"] = turn_y(14, 1)
+        round_on_vector(14, 1)
+        nc.scalar.activation(
+            band(y_grouped, 15).rearrange("p (m t) -> p m t", t=4), last_bank[:].rearrange("p t m -> p m t"), SILU
+        )
+        bank_12, bank_14 = turn_y(12), turn_y(14, 1)
         quantise_y(8, 2)
-        free = [y_all[:, D * j : D * j + D] for j in range(8, 10)]
-        read_y(S, bk["Y10"], 10, 2)
-        read_y(S, bk["Y12"], 12, 2)
-        read_y(S, bk["Y14"], 14, 1)
-        quantise_y(10, 2)
-        free = [y_all[:, D * j : D * j + D] for j in range(10, 12)]
-        quantise_y(12, 2)
-        free = [y_all[:, D * j : D * j + D] for j in range(12, 14)]
-        quantise_y(14, 2)
-        free = [y_all[:, D * j : D * j + D] for j in range(14, 16)]
-
+        read_y(SCALAR, bank_10, 10)
+        read_y(SCALAR, bank_12, 12)
+        read_y(SCALAR, bank_14, 14, 1)
+        for g in (10, 12, 14):
+            quantise_y(g, 2)
         rows = out_2[0].rearrange("r (n m) -> n r m", n=B)
         for q in range(4):
             queue = nc.sync if q < 2 else nc.scalar

@@ -382,7 +382,6 @@ def tile_ranktwokroneckersumlayer_x2_kernel(
             quantise_y(g, 2)
         rows = out_2[0].rearrange("r (n m) -> n r m", n=B)
         for q in range(4):
-            queue = nc.sync if q < 2 else nc.scalar
-            queue.dma_start(
+            nc.scalar.dma_start(
                 out=rows[:, 4 * q : 4 * q + 4, :].bitcast(I32), in_=y_scales[32 * q : 32 * q + 16, :].bitcast(I32)
             )

@@ -208,20 +208,16 @@ def tile_ranktwokroneckersumlayer_x2_kernel(
         spent = []
 
         def spend(grouped):
-            spent[:] = [grouped[:, D * j : D * j + D] for j in range(4)]
+            spent[:] = [grouped, 0]
 
-        def round_on_gpsimd(g):
-            into = spent.pop(0)
-            nc.gpsimd.tensor_scalar(
-                out=into.rearrange("p (u k e) -> p u k e", u=2, e=2),
-                in0=band(y, g).rearrange("p (k u e) -> p u k e", u=2, e=2),
-                scalar1=1.0,
-                scalar2=-0.0,
-                op0=MULT,
-                op1=ADD,
-            )
-            words = into.bitcast(F32)
-            rounded[g] = [words[:, P * u : P * u + P] for u in range(2)]
+        def round_on_gpsimd(g, count):
+            grouped, first = spent
+            spent[1] = first + count
+            into = grouped[:, D * first : D * (first + count)]
+            nc.gpsimd.tensor_scalar(out=into, in0=band(y, g, count), scalar1=1.0, scalar2=-0.0, op0=MULT, op1=ADD)
+            for j in range(count):
+                words = into[:, D * j : D * j + D].bitcast(F32)
+                rounded[g + j] = [words[:, u::2] for u in range(2)]
 
         last_rounded = sbuf("last_rounded", [P, 3 * D], BF16)
 
@@ -272,7 +268,7 @@ def tile_ranktwokroneckersumlayer_x2_kernel(
             t_pass(opened[h], 0, 0, h, 2)
             t_pass(opened[h], 0, 0, h, 3)
 
-        turned_x, turned_y, waiting = [], [], []
+        turned_x, turned_y = [], []
         for step in range(STEPS):
             n, s = step // 2, step % 2
             g = 2 * step - Z_LAG
@@ -288,8 +284,8 @@ def tile_ranktwokroneckersumlayer_x2_kernel(
                 banks += opened[2 * half : 2 * half + 2] if step == 0 else [t_bank(n, s, 2 * half + h) for h in range(2)]
                 if g + half >= 0:
                     sums[g + half] = z_bank(g + half)
-            while waiting:
-                round_on_gpsimd(waiting.pop(0))
+            if g >= 3:
+                round_on_gpsimd(g - 3, 2)
             ahead = g >= 0
             for m, half, bank in turned_x[::-1] if ahead else turned_x:
                 read_words(SCALAR, bank, x_grouped[m], 2 * half, 2)
@@ -308,20 +304,14 @@ def tile_ranktwokroneckersumlayer_x2_kernel(
                 read_t(SCALAR, banks[0], n, s, 0)
             if g >= 1 and not last:
                 silu(g - 1)
-                if step < Y_TURNED:
-                    round_on_gpsimd(g - 1)
-                else:
-                    waiting.append(g - 1)
             if g >= 0:
                 add_c(sums[g], g)
             read_t(SCALAR, banks[2], n, s, 2)
             read_t(VECTOR, banks[3], n, s, 3)
             if last:
                 silu(g - 1)
-                waiting.append(g - 1)
             if g >= 0:
                 silu(g)
-                waiting.append(g)
             if g + 1 >= 0:
                 add_c(sums[g + 1], g + 1)
             for m in X_TURNED:
@@ -334,18 +324,17 @@ def tile_ranktwokroneckersumlayer_x2_kernel(
         quantise_t(STEPS - 1)
         quantise_y(0, 4)
         spend(y_grouped[0])
-        while waiting:
-            round_on_gpsimd(waiting.pop(0))
+        round_on_gpsimd(8, 2)
         sums = {11: z_bank(11)}
         silu(10)
-        round_on_gpsimd(10)
+        round_on_gpsimd(10, 1)
         add_c(sums[11], 11)
         sums = {g: z_bank(g) for g in (12, 13)}
         add_c(sums[12], 12)
         read_y(SCALAR, bank_6, 6)
         read_y(SCALAR, bank_4, 4)
         silu(11)
-        round_on_gpsimd(11)
+        round_on_gpsimd(11, 1)
         add_c(sums[13], 13)
         sums = {g: z_bank(g) for g in (14, 15)}
         silu(12)

@@ -24,7 +24,7 @@ BANDS = 4 * B
 Z_LAG = 5
 X_TURNED = {1: 0, 2: 1, 3: 3}
 Y_TURNED = 6
-WARM_FIRST, WARM_GAP = 4, 2
+WARM_FIRST, WARM_GAP = (512, 512, 512), (512, 512)
 
 
 def tile_ranktwokroneckersumlayer_x2_kernel(
@@ -46,15 +46,17 @@ def tile_ranktwokroneckersumlayer_x2_kernel(
             return psum.tile(shape, F32, name=kind, tag=f"bank{len(taken) % BANKS}")
 
         w_scales = [sbuf(f"w_scales{w}", [P, D], U8) for w in range(4)]
-        zeros = sbuf("zeros", [P, 1024], BF16)
-        zero_codes = sbuf("zero_codes", [P, 256], U32)
-        zero_scales = sbuf("zero_scales", [P, 256], U8)
+        zeros = sbuf("zeros", [P, P], BF16)
+        zero_codes = sbuf("zero_codes", [P, D], U32)
+        zero_scales = sbuf("zero_scales", [P, D], U8)
         table_in = sbuf("table_in", [P, 1], F32)
         ident = sbuf("ident", [P, P], F32)
-        nc.vector.memset(w_scales[0][:].bitcast(I32), 0)
         nc.vector.memset(zeros[:].bitcast(I32), 0)
+        nc.vector.memset(w_scales[0][:].bitcast(I32), 0)
         nc.vector.memset(table_in[:], 0.0)
-        nc.vector.quantize_mx(out=zero_codes[:].bitcast(FP8X4), scales=zero_scales[:], in_=zeros[:])
+        nc.vector.memset(zero_codes[:, 32:], 0)
+        nc.vector.memset(zero_scales[:, 32:].bitcast(I32), 0)
+        nc.vector.quantize_mx(out=zero_codes[:, 0:32].bitcast(FP8X4), scales=zero_scales[:, 0:32], in_=zeros[:])
         nc.vector.memset(ident[:], 0.0)
         make_identity(nc, ident[:], nomemset=True)
         for w in range(1, 4):
@@ -214,10 +216,17 @@ def tile_ranktwokroneckersumlayer_x2_kernel(
             grouped, first = spent
             spent[1] = first + count
             into = grouped[:, D * first : D * (first + count)]
-            nc.gpsimd.tensor_scalar(out=into, in0=band(y, g, count), scalar1=1.0, scalar2=-0.0, op0=MULT, op1=ADD)
+            nc.gpsimd.tensor_scalar(
+                out=into.rearrange("p (u k e) -> p u k e", u=2, e=2),
+                in0=band(y, g, count).rearrange("p (k u e) -> p u k e", u=2, e=2),
+                scalar1=1.0,
+                scalar2=-0.0,
+                op0=MULT,
+                op1=ADD,
+            )
+            words = into.bitcast(F32).rearrange("p (u j m) -> p u j m", u=2, j=count)
             for j in range(count):
-                words = into[:, D * j : D * j + D].bitcast(F32)
-                rounded[g + j] = [words[:, u::2] for u in range(2)]
+                rounded[g + j] = [words[:, u, j, :] for u in range(2)]
 
         last_rounded = sbuf("last_rounded", [P, 3 * D], BF16)
 
@@ -235,15 +244,15 @@ def tile_ranktwokroneckersumlayer_x2_kernel(
                     nc.tensor.transpose(bank[:, s, u, :], rounded[g + s][u], ident[:])
             return bank
 
-        def warm_up(count):
-            bank = next_bank("bank_w", [P, 256])
-            for i in range(count):
+        def warm_up(widths):
+            bank = next_bank("bank_w", [P, D])
+            for width in widths:
                 nc.tensor.matmul_mx(
-                    out=bank[:],
+                    out=bank[:, :width],
                     lhsT=zero_codes[:, 0:64].bitcast(FP4X4),
                     lhsT_scale=zero_scales[:, 0:P],
-                    rhs=zero_codes[:].bitcast(FP8X4),
-                    rhs_scale=zero_scales[:],
+                    rhs=zero_codes[:, :width].bitcast(FP8X4),
+                    rhs_scale=zero_scales[:, :width],
                     start=True,
                     stop=True,
                 )
@@ -252,21 +261,13 @@ def tile_ranktwokroneckersumlayer_x2_kernel(
 
         warm_up(WARM_FIRST)
         for t in range(4):
-            read_words(t % 2 == 1, turn_x(0, t, 1), x_grouped[0], t, 1)
-            if t == 1:
-                quantise_x(0, 0, 1)
+            read_words(SCALAR, turn_x(0, t, 1), x_grouped[0], t, 1)
+            quantise_x(0, t, 1)
         warm_up(WARM_GAP)
         opened = [next_bank("bank_t", [P, 4, P]) for h in range(4)]
-        for h in range(4):
-            t_pass(opened[h], 0, 0, h, 0)
-        quantise_x(0, 1, 1)
-        for h in range(4):
-            t_pass(opened[h], 0, 0, h, 1)
-        quantise_x(0, 2, 1)
-        quantise_x(0, 3, 1)
-        for h in range(4):
-            t_pass(opened[h], 0, 0, h, 2)
-            t_pass(opened[h], 0, 0, h, 3)
+        for t in range(4):
+            for h in range(4):
+                t_pass(opened[h], 0, 0, h, t)
 
         turned_x, turned_y = [], []
         for step in range(STEPS):

@@ -62,7 +62,7 @@ def tile_ranktwokroneckersumlayer_x2_kernel(
         for w in range(1, 4):
             nc.vector.memset(w_scales[w][:].bitcast(I32), 0)
 
-        x_rows = {}
+        x_rows, x_tiles = {}, {}
         w_words = [sbuf(f"w_words{w}", [P, 2 * D], U8) for w in range(4)]
         c_sb = sbuf("c_sb", [P, 4, D], BF16)
         words_in = [b1_words, b2_words, a1_words, a2_words]
@@ -71,6 +71,7 @@ def tile_ranktwokroneckersumlayer_x2_kernel(
         def load_x(n, first, count):
             rows = sbuf(f"x_in{n}{first}", [P, count, D], BF16)
             nc.sync.dma_start(out=rows[:], in_=x[n].rearrange("(m t) j -> m t j", t=4)[:, first : first + count, :])
+            x_tiles[n] = rows
             for t in range(count):
                 x_rows[n, first + t] = rows[:, t, :]
 
@@ -153,11 +154,24 @@ def tile_ranktwokroneckersumlayer_x2_kernel(
         def read_y(on_vector, bank, g, count=2):
             read_words(on_vector, bank, y_all, g, count)
 
+        x_sorted = {}
+
+        def sort_x(on_vector, n, first):
+            words = sbuf(f"x_sorted{n}{first}", [P, 2, 2, P], F32)
+            rows = x_tiles[n][:, first : first + 2, :].bitcast(F32)
+            copy(on_vector, words[:], rows.rearrange("p t (m u) -> p t u m", u=2))
+            for t in range(2):
+                x_sorted[n, first + t] = words[:, t]
+
         def turn_x(n, first, count):
             bank = next_bank("bank_x", [P, count, 2, P])
             for s in range(count):
                 for u in range(2):
-                    nc.tensor.transpose(bank[:, s, u, :], x_rows[n, first + s].bitcast(F32)[:, u::2], ident[:])
+                    if (n, first + s) in x_sorted:
+                        words = x_sorted[n, first + s][:, u, :]
+                    else:
+                        words = x_rows[n, first + s].bitcast(F32)[:, u::2]
+                    nc.tensor.transpose(bank[:, s, u, :], words, ident[:])
             return bank
 
         def t_pass(bank, n, s, h, t):
@@ -263,14 +277,50 @@ def tile_ranktwokroneckersumlayer_x2_kernel(
         for t in range(4):
             read_words(SCALAR, turn_x(0, t, 1), x_grouped[0], t, 1)
             quantise_x(0, t, 1)
+        sort_x(VECTOR, 1, 0)
+        sort_x(SCALAR, 1, 2)
         warm_up(WARM_GAP)
         opened = [next_bank("bank_t", [P, 4, P]) for h in range(4)]
         for t in range(4):
             for h in range(4):
                 t_pass(opened[h], 0, 0, h, t)
 
-        turned_x, turned_y = [], []
-        for step in range(STEPS):
+        def turn_halves(m):
+            return [turn_x(m, 2 * half, 2) for half in range(2)]
+
+        def read_x(on_vector, banks, m, half):
+            read_words(on_vector, banks[half], x_grouped[m], 2 * half, 2)
+
+        x1 = turn_halves(1)
+        for h in range(3):
+            read_t(h == 1, opened[h], 0, 0, h)
+        read_x(VECTOR, x1, 1, 0)
+        read_t(VECTOR, opened[3], 0, 0, 3)
+        read_x(SCALAR, x1, 1, 1)
+        quantise_x(1, 0, 4)
+        quantise_t(0)
+        for h in range(4):
+            read_t(h in (3,), t_bank(0, 1, h), 0, 1, h)
+        x2 = turn_halves(2)
+        read_x(SCALAR, x2, 2, 0)
+        read_x(VECTOR, x2, 2, 1)
+        quantise_t(1)
+        for h in range(4):
+            read_t(h in (3,), t_bank(1, 0, h), 1, 0, h)
+        banks = [t_bank(1, 1, h) for h in range(2)]
+        quantise_x(2, 0, 4)
+        add_c(z_bank(0), 0)
+        quantise_t(2)
+        for h in range(2):
+            read_t(SCALAR, banks[h], 1, 1, h)
+        read_t(SCALAR, t_bank(1, 1, 2), 1, 1, 2)
+        silu(0)
+        add_c(z_bank(1), 1)
+        read_t(VECTOR, t_bank(1, 1, 3), 1, 1, 3)
+        silu(1)
+        add_c(z_bank(2), 2)
+        turned_x, turned_y = [(3, half, bank) for half, bank in enumerate(turn_halves(3))], []
+        for step in range(4, STEPS):
             n, s = step // 2, step % 2
             g = 2 * step - Z_LAG
             last = step == STEPS - 1
@@ -288,7 +338,7 @@ def tile_ranktwokroneckersumlayer_x2_kernel(
             if g >= 3:
                 round_on_gpsimd(g - 3, 2)
             ahead = g >= 0
-            for m, half, bank in turned_x[::-1] if ahead else turned_x:
+            for m, half, bank in turned_x:
                 read_words(SCALAR, bank, x_grouped[m], 2 * half, 2)
             for first, bank in turned_y[::-1]:
                 read_y(SCALAR, bank, first)

@@ -230,13 +230,9 @@ def tile_ranktwokroneckersumlayer_x2_kernel(
             grouped, first = spent
             spent[1] = first + count
             into = grouped[:, D * first : D * (first + count)]
-            nc.gpsimd.tensor_scalar(
+            nc.gpsimd.tensor_copy(
                 out=into.rearrange("p (u k e) -> p u k e", u=2, e=2),
-                in0=band(y, g, count).rearrange("p (k u e) -> p u k e", u=2, e=2),
-                scalar1=1.0,
-                scalar2=-0.0,
-                op0=MULT,
-                op1=ADD,
+                in_=band(y, g, count).rearrange("p (k u e) -> p u k e", u=2, e=2),
             )
             words = into.bitcast(F32).rearrange("p (u j m) -> p u j m", u=2, j=count)
             for j in range(count):

@@ -12,7 +12,6 @@ FP8X4 = mybir.dt.float8_e4m3fn_x4
 FP4X4 = mybir.dt.float4_e2m1fn_x4
 SILU = mybir.ActivationFunctionType.Silu
 ADD = mybir.AluOpType.add
-MULT = mybir.AluOpType.mult
 
 B, D = 4, 512
 P = 128
@@ -22,8 +21,6 @@ BANKS = 8
 STEPS = 2 * B
 BANDS = 4 * B
 Z_LAG = 5
-X_TURNED = {1: 0, 2: 1, 3: 3}
-Y_TURNED = 6
 WARM_FIRST, WARM_GAP = (512, 512, 512), (512, 512)
 
 
@@ -46,17 +43,16 @@ def tile_ranktwokroneckersumlayer_x2_kernel(
             return psum.tile(shape, F32, name=kind, tag=f"bank{len(taken) % BANKS}")
 
         w_scales = [sbuf(f"w_scales{w}", [P, D], U8) for w in range(4)]
-        zeros = sbuf("zeros", [P, P], BF16)
-        zero_codes = sbuf("zero_codes", [P, D], U32)
-        zero_scales = sbuf("zero_scales", [P, D], U8)
+        zeros = sbuf("zeros", [P, 448], U32)
+        zero_codes, zero_scales = zeros[:, 64:320], zeros[:, 320:448].bitcast(U8)
         table_in = sbuf("table_in", [P, 1], F32)
         ident = sbuf("ident", [P, P], F32)
-        nc.vector.memset(zeros[:].bitcast(I32), 0)
+        nc.vector.memset(zeros[:], 0)
         nc.vector.memset(w_scales[0][:].bitcast(I32), 0)
         nc.vector.memset(table_in[:], 0.0)
-        nc.vector.memset(zero_codes[:, 32:], 0)
-        nc.vector.memset(zero_scales[:, 32:].bitcast(I32), 0)
-        nc.vector.quantize_mx(out=zero_codes[:, 0:32].bitcast(FP8X4), scales=zero_scales[:, 0:32], in_=zeros[:])
+        nc.vector.quantize_mx(
+            out=zero_codes[:, 0:32].bitcast(FP8X4), scales=zero_scales[:, 0:32], in_=zeros[:, 0:64].bitcast(BF16)
+        )
         nc.vector.memset(ident[:], 0.0)
         make_identity(nc, ident[:], nomemset=True)
         for w in range(1, 4):
@@ -127,9 +123,8 @@ def tile_ranktwokroneckersumlayer_x2_kernel(
 
         def quantise(codes, scales, grouped, first, count):
             cols = slice(P * first, P * (first + count))
-            nc.vector.quantize_mx(
-                out=codes[:, cols].bitcast(FP8X4), scales=scales[:, cols], in_=grouped[:, D * first : D * (first + count)]
-            )
+            values = grouped[:, D * first : D * (first + count)]
+            nc.vector.quantize_mx(out=codes[:, cols].bitcast(FP8X4), scales=scales[:, cols], in_=values)
 
         def quantise_x(n, first, count):
             quantise(x_codes[n], x_scales[n], x_grouped[n], first, count)
@@ -138,18 +133,16 @@ def tile_ranktwokroneckersumlayer_x2_kernel(
             n, s = term // 2, term % 2
             quantise(t_codes[n][s], t_scales[n][s], t_grouped[n][s], 0, 4)
 
-        def quantise_y(g, count):
+        def quantise_y(g):
             n = g // 4
-            quantise(y_codes[:, D * n : D * n + D], y_scales[4 * n :, :], y_grouped[n], g % 4, count)
-            cols = slice(P * g, P * (g + count))
+            quantise(y_codes[:, D * n : D * n + D], y_scales[4 * n :, :], y_grouped[n], g % 4, 2)
+            cols = slice(P * g, P * (g + 2))
             nc.sync.dma_start(out=out_1[0, :, cols, :].rearrange("p m t -> p (m t)").bitcast(I32), in_=y_codes[:, cols])
 
         def read_words(on_vector, bank, grouped, first, count):
-            copy(
-                on_vector,
-                grouped[:, D * first : D * (first + count)].bitcast(F32).rearrange("p (s m u) -> p s m u", s=count, u=2),
-                bank[:].rearrange("p s u m -> p s m u"),
-            )
+            out = grouped[:, D * first : D * (first + count)].bitcast(F32)
+            out = out.rearrange("p (s m u) -> p s m u", s=count, u=2)
+            copy(on_vector, out, bank[:].rearrange("p s u m -> p s m u"))
 
         def read_y(on_vector, bank, g, count=2):
             read_words(on_vector, bank, y_all, g, count)
@@ -214,12 +207,16 @@ def tile_ranktwokroneckersumlayer_x2_kernel(
         def add_c(bank, g):
             nc.vector.tensor_tensor(out=band(z, g), in0=bank[:], in1=c_sb[:, g % 4, :], op=ADD)
 
-        def store_y(g):
-            nc.sync.dma_start(out=out_0[g // 4, P * (g % 4) : P * (g % 4 + 1), :], in_=band(y, g))
+        def store_y(g, count=1):
+            rows = out_0[g // 4, P * (g % 4) : P * (g % 4 + count), :].rearrange("(j p) q -> p j q", p=P)
+            nc.sync.dma_start(out=rows, in_=band(y, g, count).rearrange("p (j q) -> p j q", j=count))
 
         def silu(g):
             nc.scalar.activation(band(y, g), band(z, g), SILU)
-            store_y(g)
+            if g >= 4:
+                store_y(g)
+            elif g % 2 == 1:
+                store_y(g - 1, 2)
 
         spent = []
 
@@ -259,34 +256,39 @@ def tile_ranktwokroneckersumlayer_x2_kernel(
             for width in widths:
                 nc.tensor.matmul_mx(
                     out=bank[:, :width],
-                    lhsT=zero_codes[:, 0:64].bitcast(FP4X4),
+                    lhsT=zero_codes[:, 0:P].bitcast(FP8X4),
                     lhsT_scale=zero_scales[:, 0:P],
-                    rhs=zero_codes[:, :width].bitcast(FP8X4),
+                    rhs=zero_codes[:, : width // 2].bitcast(FP4X4),
                     rhs_scale=zero_scales[:, :width],
                     start=True,
                     stop=True,
                 )
 
+        def turn_halves(n):
+            return [turn_x(n, 2 * half, 2) for half in range(2)]
+
+        def read_x(on_vector, banks, n, half):
+            read_words(on_vector, banks[half], x_grouped[n], 2 * half, 2)
+
         VECTOR, SCALAR = True, False
 
         warm_up(WARM_FIRST)
         for t in range(4):
-            read_words(SCALAR, turn_x(0, t, 1), x_grouped[0], t, 1)
-            quantise_x(0, t, 1)
+            read_words(t == 1, turn_x(0, t, 1), x_grouped[0], t, 1)
+            if t >= 1:
+                quantise_x(0, t - 1, 1)
+        quantise_x(0, 3, 1)
         sort_x(VECTOR, 1, 0)
         sort_x(SCALAR, 1, 2)
         warm_up(WARM_GAP)
         opened = [next_bank("bank_t", [P, 4, P]) for h in range(4)]
-        for t in range(4):
+        for t in range(2):
             for h in range(4):
                 t_pass(opened[h], 0, 0, h, t)
-
-        def turn_halves(m):
-            return [turn_x(m, 2 * half, 2) for half in range(2)]
-
-        def read_x(on_vector, banks, m, half):
-            read_words(on_vector, banks[half], x_grouped[m], 2 * half, 2)
-
+        for pair in range(2):
+            for t in (2, 3):
+                for h in (2 * pair, 2 * pair + 1):
+                    t_pass(opened[h], 0, 0, h, t)
         x1 = turn_halves(1)
         for h in range(3):
             read_t(h == 1, opened[h], 0, 0, h)
@@ -295,81 +297,65 @@ def tile_ranktwokroneckersumlayer_x2_kernel(
         read_x(SCALAR, x1, 1, 1)
         quantise_x(1, 0, 4)
         quantise_t(0)
+
         for h in range(4):
-            read_t(h in (3,), t_bank(0, 1, h), 0, 1, h)
+            read_t(h == 3, t_bank(0, 1, h), 0, 1, h)
         x2 = turn_halves(2)
         read_x(SCALAR, x2, 2, 0)
         read_x(VECTOR, x2, 2, 1)
         quantise_t(1)
         for h in range(4):
-            read_t(h in (3,), t_bank(1, 0, h), 1, 0, h)
+            read_t(h == 3, t_bank(1, 0, h), 1, 0, h)
+
         banks = [t_bank(1, 1, h) for h in range(2)]
         quantise_x(2, 0, 4)
         add_c(z_bank(0), 0)
         quantise_t(2)
         for h in range(2):
             read_t(SCALAR, banks[h], 1, 1, h)
-        read_t(SCALAR, t_bank(1, 1, 2), 1, 1, 2)
-        silu(0)
-        add_c(z_bank(1), 1)
-        read_t(VECTOR, t_bank(1, 1, 3), 1, 1, 3)
-        silu(1)
-        add_c(z_bank(2), 2)
-        turned_x, turned_y = [(3, half, bank) for half, bank in enumerate(turn_halves(3))], []
+        for h in (2, 3):
+            read_t(h == 3, t_bank(1, 1, h), 1, 1, h)
+            silu(h - 2)
+            add_c(z_bank(h - 1), h - 1)
+        x3 = turn_halves(3)
+
         for step in range(4, STEPS):
-            n, s = step // 2, step % 2
-            g = 2 * step - Z_LAG
-            last = step == STEPS - 1
-            if step >= 2:
-                quantise_t(step - 1)
-                spend(t_grouped[(step - 1) // 2][(step - 1) % 2])
-            if step >= 3 and step - 2 == X_TURNED.get(n + 1):
-                quantise_x(n + 1, 0, 4)
-                spend(x_grouped[n + 1])
-            banks, sums = [], {}
+            n, s, g = step // 2, step % 2, 2 * step - Z_LAG
+            first, last = step == 4, step == STEPS - 1
+            quantise_t(step - 1)
+            spend(t_grouped[(step - 1) // 2][(step - 1) % 2])
+            if step == 5:
+                quantise_x(3, 0, 4)
+                spend(x_grouped[3])
+            banks, sums = [], []
             for half in range(2):
-                banks += opened[2 * half : 2 * half + 2] if step == 0 else [t_bank(n, s, 2 * half + h) for h in range(2)]
-                if g + half >= 0:
-                    sums[g + half] = z_bank(g + half)
-            if g >= 3:
-                round_on_gpsimd(g - 3, 2)
-            ahead = g >= 0
-            for m, half, bank in turned_x:
-                read_words(SCALAR, bank, x_grouped[m], 2 * half, 2)
-            for first, bank in turned_y[::-1]:
-                read_y(SCALAR, bank, first)
-            if step == 1:
-                quantise_t(0)
-                quantise_x(1, 0, 2)
-                quantise_x(1, 2, 2)
-            second_on_vector = step < 2 or (ahead and bool(turned_x or turned_y))
-            turned_x, turned_y = [], []
-            if step < 2:
-                read_t(SCALAR, banks[0], n, s, 0)
-            read_t(second_on_vector, banks[1], n, s, 1)
-            if step >= 2:
-                read_t(SCALAR, banks[0], n, s, 0)
-            if g >= 1 and not last:
+                banks += [t_bank(n, s, 2 * half + h) for h in range(2)]
+                sums.append(z_bank(g + half))
+            round_on_gpsimd(g - 3, 2)
+            if first:
+                read_x(SCALAR, x3, 3, 0)
+                read_x(SCALAR, x3, 3, 1)
+            if last:
+                read_y(SCALAR, y0[1], 2)
+                read_y(SCALAR, y0[0], 0)
+            read_t(first or last, banks[1], n, s, 1)
+            read_t(SCALAR, banks[0], n, s, 0)
+            if not last:
                 silu(g - 1)
-            if g >= 0:
-                add_c(sums[g], g)
+            add_c(sums[0], g)
             read_t(SCALAR, banks[2], n, s, 2)
             read_t(VECTOR, banks[3], n, s, 3)
             if last:
                 silu(g - 1)
-            if g >= 0:
-                silu(g)
-            if g + 1 >= 0:
-                add_c(sums[g + 1], g + 1)
-            for m in X_TURNED:
-                if X_TURNED[m] == step:
-                    turned_x = [(m, half, turn_x(m, 2 * half, 2)) for half in range(2)]
-            if step == Y_TURNED:
-                turned_y = [(first, turn_y(first)) for first in (0, 2)]
+            silu(g)
+            add_c(sums[1], g + 1)
+            if step == 6:
+                y0 = [turn_y(0), turn_y(2)]
 
         bank_4, bank_6 = turn_y(4), turn_y(6)
         quantise_t(STEPS - 1)
-        quantise_y(0, 4)
+        for g in (2, 0):
+            quantise_y(g)
         spend(y_grouped[0])
         round_on_gpsimd(8, 2)
         sums = {11: z_bank(11)}
@@ -400,22 +386,25 @@ def tile_ranktwokroneckersumlayer_x2_kernel(
             nc.tensor.transpose(last_bank[:, t, :], last_z[:, P * t : P * t + P], ident[:])
         bank_10 = turn_y(10)
         silu(14)
-        nc.scalar.activation(band(y, 15).rearrange("p (m t) -> p m t", t=4), last_z.rearrange("p (t m) -> p m t", t=4), SILU)
+        nc.scalar.activation(
+            band(y, 15).rearrange("p (m t) -> p m t", t=4), last_z.rearrange("p (t m) -> p m t", t=4), SILU
+        )
         store_y(15)
         read_y(VECTOR, bank_8, 8)
         round_on_vector(12, 2)
-        quantise_y(4, 4)
+        for g in (4, 6):
+            quantise_y(g)
         round_on_vector(14, 1)
         nc.scalar.activation(
             band(y_grouped, 15).rearrange("p (m t) -> p m t", t=4), last_bank[:].rearrange("p t m -> p m t"), SILU
         )
         bank_12, bank_14 = turn_y(12), turn_y(14, 1)
-        quantise_y(8, 2)
+        quantise_y(8)
         read_y(SCALAR, bank_10, 10)
         read_y(SCALAR, bank_12, 12)
         read_y(SCALAR, bank_14, 14, 1)
         for g in (10, 12, 14):
-            quantise_y(g, 2)
+            quantise_y(g)
         rows = out_2[0].rearrange("r (n m) -> n r m", n=B)
         for q in range(4):
             nc.scalar.dma_start(

from contextlib import ExitStack

import concourse.mybir as mybir
from concourse.masks import make_identity

F32 = mybir.dt.float32
BF16 = mybir.dt.bfloat16
I32 = mybir.dt.int32
U32 = mybir.dt.uint32
U8 = mybir.dt.uint8
FP8X4 = mybir.dt.float8_e4m3fn_x4
FP4X4 = mybir.dt.float4_e2m1fn_x4
SILU = mybir.ActivationFunctionType.Silu
ADD = mybir.AluOpType.add

B, D = 4, 512
P = 128
FLOPS = 2 * 2 * 2 * B * D * D * D

BANKS = 8
STEPS = 2 * B
BANDS = 4 * B
Z_LAG = 5
WARM_FIRST, WARM_GAP = (512, 512, 512), (512, 512)


def tile_ranktwokroneckersumlayer_x2_kernel(
    tc, x, b1_words, b1_scales, b2_words, b2_scales, a1_words, a1_scales, a2_words, a2_scales, c, out_0, out_1, out_2
):
    nc = tc.nc
    with ExitStack() as ctx:
        keep = ctx.enter_context(tc.tile_pool(name="keep", bufs=1))
        psum = ctx.enter_context(tc.psum_pool(name="psum", bufs=1))
        ctx.enter_context(tc.manual_schedule())

        def sbuf(name, shape, dtype):
            return keep.tile(shape, dtype, name=name, align_bytes=256)

        taken = []

        def next_bank(kind, shape):
            taken.append(kind)
            return psum.tile(shape, F32, name=kind, tag=f"bank{len(taken) % BANKS}")

        w_scales = [sbuf(f"w_scales{w}", [P, D], U8) for w in range(4)]
        zeros = sbuf("zeros", [P, 448], U32)
        zero_codes, zero_scales = zeros[:, 64:320], zeros[:, 320:448].bitcast(U8)
        table_in = sbuf("table_in", [P, 1], F32)
        ident = sbuf("ident", [P, P], F32)
        nc.vector.memset(zeros[:], 0)
        nc.vector.memset(w_scales[0][:].bitcast(I32), 0)
        nc.vector.memset(table_in[:], 0.0)
        nc.vector.quantize_mx(
            out=zero_codes[:, 0:32].bitcast(FP8X4), scales=zero_scales[:, 0:32], in_=zeros[:, 0:64].bitcast(BF16)
        )
        nc.vector.memset(ident[:], 0.0)
        make_identity(nc, ident[:], nomemset=True)
        for w in range(1, 4):
            nc.vector.memset(w_scales[w][:].bitcast(I32), 0)

        x_rows, x_tiles = {}, {}
        w_words = [sbuf(f"w_words{w}", [P, 2 * D], U8) for w in range(4)]
        c_sb = sbuf("c_sb", [P, 4, D], BF16)
        words_in = [b1_words, b2_words, a1_words, a2_words]
        scales_in = [b1_scales, b2_scales, a1_scales, a2_scales]

        def load_x(n, first, count):
            rows = sbuf(f"x_in{n}{first}", [P, count, D], BF16)
            nc.sync.dma_start(out=rows[:], in_=x[n].rearrange("(m t) j -> m t j", t=4)[:, first : first + count, :])
            x_tiles[n] = rows
            for t in range(count):
                x_rows[n, first + t] = rows[:, t, :]

        def load_words(w):
            nc.sync.dma_start(out=w_words[w][:].bitcast(I32), in_=words_in[w][0].bitcast(I32))

        def load_scales(w, queue):
            for q in range(4):
                queue.dma_start(
                    out=w_scales[w][32 * q : 32 * q + 4, :].bitcast(I32),
                    in_=scales_in[w][0, 4 * q : 4 * q + 4, :].bitcast(I32),
                )

        load_x(0, 0, 2)
        load_x(0, 2, 2)
        load_words(0)
        load_scales(0, nc.scalar)
        table_out = sbuf("table_out", [P, 1], F32)
        nc.scalar.activation(table_out[:], table_in[:], SILU)
        load_x(1, 0, 4)
        load_scales(1, nc.sync)
        load_words(1)
        load_x(2, 0, 4)
        load_scales(2, nc.gpsimd)
        load_words(2)
        load_words(3)
        load_scales(3, nc.sync)
        nc.sync.dma_start(out=c_sb[:], in_=c.rearrange("(j p) q -> p j q", p=P))
        load_x(3, 0, 4)

        x_codes = [sbuf(f"x_codes{n}", [P, D], U32) for n in range(B)]
        x_scales = [sbuf(f"x_scales{n}", [P, D], U8) for n in range(B)]
        x_grouped = [sbuf(f"x_grouped{n}", [P, 4 * D], BF16) for n in range(B)]
        t_codes = [[sbuf(f"t_codes{n}{s}", [P, D], U32) for s in range(2)] for n in range(B)]
        t_scales = [[sbuf(f"t_scales{n}{s}", [P, D], U8) for s in range(2)] for n in range(B)]
        t_grouped = [[sbuf(f"t_grouped{n}{s}", [P, 4 * D], BF16) for s in range(2)] for n in range(B)]
        z = [sbuf(f"z{n}", [P, 4 * D], F32) for n in range(B)]
        y = [sbuf(f"y{n}", [P, 4 * D], F32) for n in range(B)]
        y_all = sbuf("y_grouped", [P, B * 4 * D], BF16)
        y_grouped = [y_all[:, 4 * D * n : 4 * D * (n + 1)] for n in range(B)]
        y_codes = sbuf("y_codes", [P, B * D], I32)
        y_scales = sbuf("y_scales", [P, D], U8)
        rounded = {}

        def band(tiles, g, count=1):
            return tiles[g // 4][:, D * (g % 4) : D * (g % 4 + count)]

        def copy(on_vector, out, in_):
            if on_vector:
                nc.vector.tensor_copy(out=out, in_=in_)
            else:
                nc.scalar.copy(out=out, in_=in_)

        def quantise(codes, scales, grouped, first, count):
            cols = slice(P * first, P * (first + count))
            values = grouped[:, D * first : D * (first + count)]
            nc.vector.quantize_mx(out=codes[:, cols].bitcast(FP8X4), scales=scales[:, cols], in_=values)

        def quantise_x(n, first, count):
            quantise(x_codes[n], x_scales[n], x_grouped[n], first, count)

        def quantise_t(term):
            n, s = term // 2, term % 2
            quantise(t_codes[n][s], t_scales[n][s], t_grouped[n][s], 0, 4)

        def quantise_y(g):
            n = g // 4
            quantise(y_codes[:, D * n : D * n + D], y_scales[4 * n :, :], y_grouped[n], g % 4, 2)
            cols = slice(P * g, P * (g + 2))
            nc.sync.dma_start(out=out_1[0, :, cols, :].rearrange("p m t -> p (m t)").bitcast(I32), in_=y_codes[:, cols])

        def read_words(on_vector, bank, grouped, first, count):
            out = grouped[:, D * first : D * (first + count)].bitcast(F32)
            out = out.rearrange("p (s m u) -> p s m u", s=count, u=2)
            copy(on_vector, out, bank[:].rearrange("p s u m -> p s m u"))

        def read_y(on_vector, bank, g, count=2):
            read_words(on_vector, bank, y_all, g, count)

        x_sorted = {}

        def sort_x(on_vector, n, first):
            words = sbuf(f"x_sorted{n}{first}", [P, 2, 2, P], F32)
            rows = x_tiles[n][:, first : first + 2, :].bitcast(F32)
            copy(on_vector, words[:], rows.rearrange("p t (m u) -> p t u m", u=2))
            for t in range(2):
                x_sorted[n, first + t] = words[:, t]

        def turn_x(n, first, count):
            bank = next_bank("bank_x", [P, count, 2, P])
            for s in range(count):
                for u in range(2):
                    if (n, first + s) in x_sorted:
                        words = x_sorted[n, first + s][:, u, :]
                    else:
                        words = x_rows[n, first + s].bitcast(F32)[:, u::2]
                    nc.tensor.transpose(bank[:, s, u, :], words, ident[:])
            return bank

        def t_pass(bank, n, s, h, t):
            cols = slice(P * t, P * t + P)
            nc.tensor.matmul_mx(
                out=bank[:, t, :],
                lhsT=x_codes[n][:, cols].bitcast(FP8X4),
                lhsT_scale=x_scales[n][:, cols],
                rhs=w_words[s][:, 256 * h : 256 * h + 256].bitcast(FP4X4),
                rhs_scale=w_scales[s][:, P * h : P * h + P],
                start=True,
                stop=True,
            )

        def t_bank(n, s, h):
            bank = next_bank("bank_t", [P, 4, P])
            for t in range(4):
                t_pass(bank, n, s, h, t)
            return bank

        def read_t(on_vector, bank, n, s, h):
            out = t_grouped[n][s][:, D * h : D * h + D].rearrange("p (q t) -> p q t", t=4)
            copy(on_vector, out, bank[:].rearrange("p t q -> p q t"))

        def z_bank(g):
            n, j = g // 4, g % 4
            bank = next_bank("bank_z", [P, D])
            for s in range(2):
                nc.tensor.matmul_mx(
                    out=bank[:],
                    lhsT=w_words[2 + s][:, 256 * j : 256 * j + 256].bitcast(FP4X4),
                    lhsT_scale=w_scales[2 + s][:, P * j : P * j + P],
                    rhs=t_codes[n][s][:].bitcast(FP8X4),
                    rhs_scale=t_scales[n][s][:],
                    start=(s == 0),
                    stop=(s == 1),
                )
            return bank

        def add_c(bank, g):
            nc.vector.tensor_tensor(out=band(z, g), in0=bank[:], in1=c_sb[:, g % 4, :], op=ADD)

        def store_y(g, count=1):
            rows = out_0[g // 4, P * (g % 4) : P * (g % 4 + count), :].rearrange("(j p) q -> p j q", p=P)
            nc.sync.dma_start(out=rows, in_=band(y, g, count).rearrange("p (j q) -> p j q", j=count))

        def silu(g):
            nc.scalar.activation(band(y, g), band(z, g), SILU)
            if g >= 4:
                store_y(g)
            elif g % 2 == 1:
                store_y(g - 1, 2)

        spent = []

        def spend(grouped):
            spent[:] = [grouped, 0]

        def round_on_gpsimd(g, count):
            grouped, first = spent
            spent[1] = first + count
            into = grouped[:, D * first : D * (first + count)]
            nc.gpsimd.tensor_copy(
                out=into.rearrange("p (u k e) -> p u k e", u=2, e=2),
                in_=band(y, g, count).rearrange("p (k u e) -> p u k e", u=2, e=2),
            )
            words = into.bitcast(F32).rearrange("p (u j m) -> p u j m", u=2, j=count)
            for j in range(count):
                rounded[g + j] = [words[:, u, j, :] for u in range(2)]

        last_rounded = sbuf("last_rounded", [P, 3 * D], BF16)

        def round_on_vector(g, count):
            out = last_rounded[:, D * (g % 4) : D * (g % 4 + count)]
            nc.vector.tensor_copy(out=out, in_=band(y, g, count))
            for j in range(count):
                words = out[:, D * j : D * j + D].bitcast(F32)
                rounded[g + j] = [words[:, u::2] for u in range(2)]

        def turn_y(g, count=2):
            bank = next_bank("bank_y", [P, count, 2, P])
            for s in range(count):
                for u in range(2):
                    nc.tensor.transpose(bank[:, s, u, :], rounded[g + s][u], ident[:])
            return bank

        def warm_up(widths):
            bank = next_bank("bank_w", [P, D])
            for width in widths:
                nc.tensor.matmul_mx(
                    out=bank[:, :width],
                    lhsT=zero_codes[:, 0:P].bitcast(FP8X4),
                    lhsT_scale=zero_scales[:, 0:P],
                    rhs=zero_codes[:, : width // 2].bitcast(FP4X4),
                    rhs_scale=zero_scales[:, :width],
                    start=True,
                    stop=True,
                )

        def turn_halves(n):
            return [turn_x(n, 2 * half, 2) for half in range(2)]

        def read_x(on_vector, banks, n, half):
            read_words(on_vector, banks[half], x_grouped[n], 2 * half, 2)

        VECTOR, SCALAR = True, False

        warm_up(WARM_FIRST)
        for t in range(4):
            read_words(t == 1, turn_x(0, t, 1), x_grouped[0], t, 1)
            if t >= 1:
                quantise_x(0, t - 1, 1)
        quantise_x(0, 3, 1)
        sort_x(VECTOR, 1, 0)
        sort_x(SCALAR, 1, 2)
        warm_up(WARM_GAP)
        opened = [next_bank("bank_t", [P, 4, P]) for h in range(4)]
        for t in range(2):
            for h in range(4):
                t_pass(opened[h], 0, 0, h, t)
        for pair in range(2):
            for t in (2, 3):
                for h in (2 * pair, 2 * pair + 1):
                    t_pass(opened[h], 0, 0, h, t)
        x1 = turn_halves(1)
        for h in range(3):
            read_t(h == 1, opened[h], 0, 0, h)
        read_x(VECTOR, x1, 1, 0)
        read_t(VECTOR, opened[3], 0, 0, 3)
        read_x(SCALAR, x1, 1, 1)
        quantise_x(1, 0, 4)
        quantise_t(0)

        for h in range(4):
            read_t(h == 3, t_bank(0, 1, h), 0, 1, h)
        x2 = turn_halves(2)
        read_x(SCALAR, x2, 2, 0)
        read_x(VECTOR, x2, 2, 1)
        quantise_t(1)
        for h in range(4):
            read_t(h == 3, t_bank(1, 0, h), 1, 0, h)

        banks = [t_bank(1, 1, h) for h in range(2)]
        quantise_x(2, 0, 4)
        add_c(z_bank(0), 0)
        quantise_t(2)
        for h in range(2):
            read_t(SCALAR, banks[h], 1, 1, h)
        for h in (2, 3):
            read_t(h == 3, t_bank(1, 1, h), 1, 1, h)
            silu(h - 2)
            add_c(z_bank(h - 1), h - 1)
        x3 = turn_halves(3)

        for step in range(4, STEPS):
            n, s, g = step // 2, step % 2, 2 * step - Z_LAG
            first, last = step == 4, step == STEPS - 1
            quantise_t(step - 1)
            spend(t_grouped[(step - 1) // 2][(step - 1) % 2])
            if step == 5:
                quantise_x(3, 0, 4)
                spend(x_grouped[3])
            banks, sums = [], []
            for half in range(2):
                banks += [t_bank(n, s, 2 * half + h) for h in range(2)]
                sums.append(z_bank(g + half))
            round_on_gpsimd(g - 3, 2)
            if first:
                read_x(SCALAR, x3, 3, 0)
                read_x(SCALAR, x3, 3, 1)
            if last:
                read_y(SCALAR, y0[1], 2)
                read_y(SCALAR, y0[0], 0)
            read_t(first or last, banks[1], n, s, 1)
            read_t(SCALAR, banks[0], n, s, 0)
            if not last:
                silu(g - 1)
            add_c(sums[0], g)
            read_t(SCALAR, banks[2], n, s, 2)
            read_t(VECTOR, banks[3], n, s, 3)
            if last:
                silu(g - 1)
            silu(g)
            add_c(sums[1], g + 1)
            if step == 6:
                y0 = [turn_y(0), turn_y(2)]

        bank_4, bank_6 = turn_y(4), turn_y(6)
        quantise_t(STEPS - 1)
        for g in (2, 0):
            quantise_y(g)
        spend(y_grouped[0])
        round_on_gpsimd(8, 2)
        sums = {11: z_bank(11)}
        silu(10)
        round_on_gpsimd(10, 1)
        add_c(sums[11], 11)
        sums = {g: z_bank(g) for g in (12, 13)}
        add_c(sums[12], 12)
        read_y(SCALAR, bank_6, 6)
        read_y(SCALAR, bank_4, 4)
        silu(11)
        round_on_gpsimd(11, 1)
        add_c(sums[13], 13)
        sums = {g: z_bank(g) for g in (14, 15)}
        silu(12)
        silu(13)
        add_c(sums[14], 14)
        last_z = band(z, BANDS - 1)
        nc.vector.tensor_tensor(
            out=last_z.rearrange("p (t m) -> p t m", t=4),
            in0=sums[15][:].rearrange("p (m t) -> p t m", t=4),
            in1=c_sb[:, 3, :].rearrange("p (m t) -> p t m", t=4),
            op=ADD,
        )
        bank_8 = turn_y(8)
        last_bank = next_bank("bank_d", [P, 4, P])
        for t in range(4):
            nc.tensor.transpose(last_bank[:, t, :], last_z[:, P * t : P * t + P], ident[:])
        bank_10 = turn_y(10)
        silu(14)
        nc.scalar.activation(
            band(y, 15).rearrange("p (m t) -> p m t", t=4), last_z.rearrange("p (t m) -> p m t", t=4), SILU
        )
        store_y(15)
        read_y(VECTOR, bank_8, 8)
        round_on_vector(12, 2)
        for g in (4, 6):
            quantise_y(g)
        round_on_vector(14, 1)
        nc.scalar.activation(
            band(y_grouped, 15).rearrange("p (m t) -> p m t", t=4), last_bank[:].rearrange("p t m -> p m t"), SILU
        )
        bank_12, bank_14 = turn_y(12), turn_y(14, 1)
        quantise_y(8)
        read_y(SCALAR, bank_10, 10)
        read_y(SCALAR, bank_12, 12)
        read_y(SCALAR, bank_14, 14, 1)
        for g in (10, 12, 14):
            quantise_y(g)
        rows = out_2[0].rearrange("r (n m) -> n r m", n=B)
        for q in range(4):
            nc.scalar.dma_start(
                out=rows[:, 4 * q : 4 * q + 4, :].bitcast(I32), in_=y_scales[32 * q : 32 * q + 16, :].bitcast(I32)
            )
